import numpy as np
import ml_dtypes


def mxq(x, axis, fmt="e4m3"):
    dtype, down = {"e4m3": (ml_dtypes.float8_e4m3fn, 7), "e5m2": (ml_dtypes.float8_e5m2, 14)}[fmt]
    v = np.moveaxis(np.asarray(x, np.float32).astype(ml_dtypes.bfloat16).astype(np.float64), axis, -1)
    blocks = v.reshape(v.shape[:-1] + (-1, 32))
    amax = np.abs(blocks).max(-1, keepdims=True)
    byte = np.maximum(np.where(amax > 0, np.frexp(amax)[1] - 1 + 127, 0) - down, 1)
    scale = np.exp2(byte - 127.0)
    codes = (blocks / scale).astype(np.float32).astype(dtype).astype(np.float64)
    return np.moveaxis((codes * scale).reshape(v.shape), -1, axis)


WIDE = False


def mx_kscale(k):
    if not WIDE:
        return np.ones(k)
    levels = np.array([10, -10, 5, -5, 0])
    if k % 512:
        return np.exp2(np.random.permutation(np.resize(levels, k // 32))).repeat(32)
    a = np.empty((k // 512, 16))
    for p in range(k // 512):
        a[p, :8] = np.random.permutation(np.resize(levels, 8))
        for g in range(8):
            far = levels[np.abs(levels - a[p, g]) >= 10]
            a[p, g + 8] = far[np.random.randint(len(far))]
    return np.exp2(a.ravel()).repeat(32)


def f64(x):
    return np.asarray(x).astype(np.float64)


def striped(idx):
    return np.tile(idx.reshape(-1, 16).T, (8, 1)).astype(np.uint16)


def unstriped(offs):
    return offs[:16].T.reshape(-1).astype(np.int64)


E2M1 = np.array([0.0, 0.5, 1.0, 1.5, 2.0, 3.0, 4.0, 6.0, -0.0, -0.5, -1.0, -1.5, -2.0, -3.0, -4.0, -6.0])


def pack_weight(w, fmt):
    k, n = w.shape
    w = f64(np.asarray(w, np.float32).astype(ml_dtypes.bfloat16)).reshape(k // 32, 32, n)
    amax = np.abs(w).max(1)
    if fmt == "e4m3":
        byte = np.frexp(amax)[1] - 1 + 127 - 7
    else:
        mant, ex = np.frexp(amax / 6.0)
        byte = np.where(mant > 0.5, ex, ex - 1) + 127
    byte = np.clip(np.where(amax > 0, byte, 1), 1, 254)
    scaled = (w * np.exp2(127.0 - byte)[:, None, :]).reshape(k, n).astype(np.float32)
    by_word = np.ascontiguousarray(scaled.reshape(k // 512, 128, 4, n).transpose(0, 1, 3, 2))
    if fmt == "e4m3":
        words = by_word.astype(ml_dtypes.float8_e4m3fn).view(np.uint8)
    else:
        c = by_word.astype(ml_dtypes.float4_e2m1fn).view(np.uint8) & 0xF
        words = (c[..., 0::2] | (c[..., 1::2] << 4)).reshape(k // 512, 128, 2 * n)
    return np.ascontiguousarray(words), np.ascontiguousarray(byte.astype(np.uint8).reshape(k // 512, 16, n))


def unpack_weight(words, scales, fmt):
    g, _, n = scales.shape
    words = np.ascontiguousarray(words).reshape(g, 128, n, -1)
    if fmt == "e4m3":
        vals = words.view(ml_dtypes.float8_e4m3fn).astype(np.float64)
    else:
        nib = np.empty((g, 128, n, 4), np.uint8)
        nib[..., 0::2] = words & 0xF
        nib[..., 1::2] = words >> 4
        vals = E2M1[nib]
    vals = vals * np.repeat(np.exp2(scales.astype(np.float64) - 127.0), 8, axis=1)[..., None]
    return vals.transpose(0, 1, 3, 2).reshape(g * 512, n)


def gelu(v):
    return 0.5 * v * (1.0 + np.tanh(np.sqrt(2.0 / np.pi) * (v + 0.044715 * v**3)))


def striped8(idx):
    return np.concatenate([v.reshape(-1, 16).T for v in idx]).astype(np.uint16)


def unstriped8(offs):
    return np.stack([offs[16 * g:16 * g + 16].T.reshape(-1) for g in range(8)]).astype(np.int64)


def runs(v, idx8):
    k = np.arange(v.shape[0])
    return v[k[:, None], idx8[k % 512 // 64]]


K, K2, H, N, T, S = 1024, 512, 512, 384, 2048, 1024

def setup_inputs():
    n = np.random.standard_normal
    s = mx_kscale(K)[:, None]
    s2 = mx_kscale(K2)[:, None]
    u = mx_kscale(H)[:, None]
    tab_words, tab_scales = pack_weight(n((K, T)) * s, "e4m3")
    tab2_words, tab2_scales = pack_weight(n((K2, T)) * s2, "e4m3")
    offs = striped8(np.stack([np.random.permutation(T)[:S] for _ in range(8)]))
    offs2 = striped(np.random.permutation(T)[:S])
    w1 = (n((K, H)) / np.sqrt(K) / s).astype(np.float32)
    w2_words, w2_scales = pack_weight(n((K, H)) / np.sqrt(K) / s, "e2m1")
    w3_words, w3_scales = pack_weight(n((K2, H)) / np.sqrt(K2) / s2, "e4m3")
    w4 = (n((K2, H)) / np.sqrt(K2) / s2).astype(np.float32)
    win = (np.exp(0.3 * n(H)) * u[:, 0]).astype(np.float32)
    w5 = (n((H, N)) / np.sqrt(H) / u).astype(np.float32)
    return dict(tab_words=tab_words, tab_scales=tab_scales, tab2_words=tab2_words, tab2_scales=tab2_scales,
                offs=offs, offs2=offs2, w1=w1, w2_words=w2_words, w2_scales=w2_scales,
                w3_words=w3_words, w3_scales=w3_scales, w4=w4, win=win, w5=w5)

def reference(tab_words, tab_scales, tab2_words, tab2_scales, offs, offs2, w1, w2_words, w2_scales,
              w3_words, w3_scales, w4, win, w5):
    v = runs(unpack_weight(tab_words, tab_scales, "e4m3"), unstriped8(offs))
    v2 = unpack_weight(tab2_words, tab2_scales, "e4m3")[:, unstriped(offs2)]
    xr = mxq(f64(w1), 0, "e4m3").T @ v
    xi = unpack_weight(w2_words, w2_scales, "e2m1").T @ v
    yr = unpack_weight(w3_words, w3_scales, "e4m3").T @ v2
    yi = mxq(f64(w4), 0, "e4m3").T @ v2
    h = (xr * yr + xi * yi) * f64(win)[:, None]
    return mxq(f64(w5), 0, "e4m3").T @ mxq(h, 0, "e4m3")

@@ -1,0 +1,239 @@
+from contextlib import ExitStack
+
+import concourse.mybir as mybir
+from concourse.masks import make_identity
+
+K, K2, H, N, T, S = 1024, 512, 512, 384, 2048, 1024
+FLOPS = 2 * S * (2 * K * H + 2 * K2 * H + H * N)
+
+F32 = mybir.dt.float32
+BF16 = mybir.dt.bfloat16
+I32 = mybir.dt.int32
+U32 = mybir.dt.uint32
+U16 = mybir.dt.uint16
+U8 = mybir.dt.uint8
+FP8X4 = mybir.dt.float8_e4m3fn_x4
+FP4X4 = mybir.dt.float4_e2m1fn_x4
+MULT = mybir.AluOpType.mult
+ADD = mybir.AluOpType.add
+COPY = mybir.ActivationFunctionType.Copy
+
+P = 128
+HALF = 512
+TAIL = 128
+
+
+def tile_list_raman_phase_traces_kernel(tc, tab_words, tab_scales, tab2_words, tab2_scales, offs, offs2,
+                                                 w1, w2_words, w2_scales, w3_words, w3_scales, w4, win, w5, out):
+    nc = tc.nc
+    with ExitStack() as ctx:
+        lists = ctx.enter_context(tc.tile_pool(name="lists", bufs=1))
+        sb = ctx.enter_context(tc.tile_pool(name="sb", bufs=1))
+        psum = ctx.enter_context(tc.psum_pool(name="psum", bufs=1))
+
+        def tile(name, shape, dtype, after=None):
+            return sb.tile(shape, dtype, name=name, tag=after or name, align_bytes=64)
+
+        offs_sb = lists.tile([P, S // 16], U16, name="offs_sb")
+        offs2_sb = lists.tile([P, S // 16], U16, name="offs2_sb")
+
+        tab_bytes = tile("tab_bytes", [P, T], U8)
+        tab2_bytes = tile("tab2_bytes", [P, T], U8)
+        v_scale = [tile("v_scale%d" % a, [P, S], U8) for a in range(2)]
+        win_rows = tile("win_rows", [P, P], F32)
+        ident = tile("ident", [P, P], F32)
+        w2_scale_raw = tile("w2_scale_raw", [P, 2 * H], U8)
+        w3_scale_raw = tile("w3_scale_raw", [P, H], U8)
+        nc.gpsimd.memset(tab_bytes[:].bitcast(I32), 0)
+        nc.vector.memset(tab2_bytes[:].bitcast(I32), 0)
+        nc.gpsimd.memset(win_rows[:], 0.0)
+        make_identity(nc, ident[:])
+        for plane in (v_scale[0], v_scale[1], w2_scale_raw, w3_scale_raw):
+            nc.vector.memset(plane[:].bitcast(I32), 0)
+
+        def load_words(name, words, width):
+            t = tile(name, [P, width], U32)
+            nc.sync.dma_start(out=t[:].bitcast(I32), in_=words.rearrange("p t i -> p (t i)").bitcast(I32))
+            return t
+
+        def load_rows(name, rows):
+            t = tile(name, [P, 4, H], F32)
+            nc.sync.dma_start(out=t[:], in_=rows.rearrange("(p j) c -> p j c", j=4))
+            return t
+
+        def load_w3_scales(d):
+            nc.sync.dma_start(out=w3_scale_raw[:].bitcast(I32)[32 * d:32 * d + 4, :],
+                              in_=w3_scales[0, 4 * d:4 * d + 4, :].bitcast(I32))
+
+        nc.sync.dma_start(offs_sb[:], offs)
+        nc.sync.dma_start(offs2_sb[:], offs2)
+        for a in range(2):
+            nc.scalar.dma_start(out=tab_bytes[:].bitcast(I32)[4 * a:P:8, :], in_=tab_scales[a].bitcast(I32))
+        for d in range(4):
+            nc.scalar.dma_start(out=tab2_bytes[:].bitcast(I32)[32 * d:32 * d + 4, :],
+                                in_=tab2_scales[0, 4 * d:4 * d + 4, :].bitcast(I32))
+        nc.scalar.dma_start(out=win_rows[0:4, :].rearrange("t (b q) -> t b q", q=4),
+                            in_=win.rearrange("(b t q) -> t b q", t=4, q=4))
+        tab2_w = load_words("tab2_w", tab2_words[0], T)
+        w4_raw = load_rows("w4_raw", w4)
+        tab_w = [load_words("tab_w0", tab_words[0], T)]
+        w2_raw = tile("w2_raw", [P, 2, 2 * H], U8)
+        nc.sync.dma_start(out=w2_raw[:].bitcast(I32), in_=w2_words.rearrange("a p c -> p a c").bitcast(I32))
+        for d in range(4):
+            nc.sync.dma_start(out=w2_scale_raw[:].bitcast(I32).rearrange("p (a c) -> p a c", a=2)[32 * d:32 * d + 4],
+                              in_=w2_scales[:, 4 * d:4 * d + 4, :].rearrange("a r c -> r a c").bitcast(I32))
+        tab_w.append(load_words("tab_w1", tab_words[1], T))
+        w1_raw = [load_rows("w1_raw0", w1[0:512, :])]
+        w3_raw = load_words("w3_raw", w3_words[0], H)
+        load_w3_scales(0)
+        load_w3_scales(1)
+        w1_raw.append(load_rows("w1_raw1", w1[512:K, :]))
+        load_w3_scales(2)
+        load_w3_scales(3)
+        w5_raw = tile("w5_raw", [P, 4, N], F32)
+        w5_by_q = w5.rearrange("(b t q) n -> q b t n", t=4, q=4)
+        for q in range(4):
+            nc.sync.dma_start(out=w5_raw[q:P:4, :, :], in_=w5_by_q[q])
+
+        win_ps = psum.tile([P, HALF], F32, name="win_ps", tag="o", bufs=2)
+        nc.tensor.transpose(win_ps[:, 0:P], win_rows[:], ident[:])
+        win_col = tile("win_col", [P, 4], F32)
+        nc.scalar.activation(out=win_col[:], in_=win_ps[:, 0:4], func=COPY)
+
+        picked = tile("picked", [P, S], U8)
+        nc.vector.tensor_copy(picked[:], tab_bytes[:].indirect(offs_sb[:]))
+        v2_scale = tile("v2_scale", [P, S], U8)
+        nc.vector.tensor_copy(v2_scale[:], tab2_bytes[:].indirect(offs2_sb[:]))
+
+        def gather_words(name, window, offsets, after=None):
+            t = tile(name, [P, 16 * offsets.shape[1]], U32, after)
+            nc.vector.tensor_copy(t[:], window[:].indirect(offsets))
+            return t
+
+        def round_weight(name, raw):
+            g = tile(name, [P, 4 * H], BF16)
+            nc.scalar.copy(out=g[:].rearrange("p (t b q j) -> p t b j q", t=4, q=4, j=4),
+                           in_=raw[:].rearrange("p j (b t q) -> p t b j q", t=4, q=4))
+            return g
+
+        def quantize(name, src, width):
+            codes = tile(name + "_codes", [P, width], U32)
+            scales = tile(name + "_scales", [P, width], U8)
+            nc.vector.quantize_mx(out=codes[:].bitcast(FP8X4), scales=scales[:], in_=src)
+            return codes, scales
+
+        v2 = gather_words("v2", tab2_w, offs2_sb[:])
+        w4_bf = round_weight("w4_bf", w4_raw)
+        w4_codes, w4_scales = quantize("w4", w4_bf[:], H)
+        for a in range(2):
+            for r in range(4):
+                nc.scalar.dma_start(out=v_scale[a][:].bitcast(I32)[r:P:32, :],
+                                    in_=picked[:].bitcast(I32)[8 * r + 4 * a:P:32, :])
+
+        def y_part(name, codes, scales, h):
+            y = tile(name, [P, 4, HALF], F32)
+            for t in range(4):
+                bank = psum.tile([P, HALF], F32, name="y_ps", tag="y", bufs=3)
+                nc.tensor.matmul_mx(out=bank[:], lhsT=codes[:, P * t:P * (t + 1)].bitcast(FP8X4),
+                                    lhsT_scale=scales[:, P * t:P * (t + 1)], rhs=v2[:, HALF * h:HALF * (h + 1)].bitcast(FP8X4),
+                                    rhs_scale=v2_scale[:, HALF * h:HALF * (h + 1)], start=True, stop=True)
+                nc.scalar.activation(out=y[:, t, :], in_=bank[:], func=COPY, scale=win_col[:, t:t + 1])
+            return y
+
+        yi = [y_part("yi%d" % h, w4_codes, w4_scales, h) for h in range(2)]
+
+        v_first = gather_words("v_first", tab_w[0], offs_sb[:], "w4_bf")
+        v = [[v_first[:, HALF * h:HALF * (h + 1)]] for h in range(2)]
+        w2_codes = tile("w2_codes", [P, 2, 2 * H], U8)
+        nc.vector.tensor_copy(out=w2_codes[:].bitcast(I32).rearrange("p a (t b e) -> p a t b e", t=4, e=2),
+                              in_=w2_raw[:].bitcast(I32).rearrange("p a (b t e) -> p a t b e", t=4, e=2))
+        w2_scale = tile("w2_scale", [P, 2 * H], U8)
+        nc.vector.tensor_copy(out=w2_scale[:].bitcast(I32).rearrange("p (a t b) -> p a t b", a=2, t=4),
+                              in_=w2_scale_raw[:].bitcast(I32).rearrange("p (a b t) -> p a t b", a=2, t=4))
+        for h in range(2):
+            v[h].append(gather_words("v%d_1" % h, tab_w[1], offs_sb[:, 32 * h:32 * (h + 1)])[:])
+
+        def x_times_y(name, lhs, y, h):
+            prod = tile(name, [P, 4, HALF], F32)
+            for t in range(4):
+                bank = psum.tile([P, HALF], F32, name="x_ps", tag="x", bufs=3)
+                for a in range(2):
+                    codes, scales = lhs(a, t)
+                    nc.tensor.matmul_mx(out=bank[:], lhsT=codes, lhsT_scale=scales, rhs=v[h][a].bitcast(FP8X4),
+                                        rhs_scale=v_scale[a][:, HALF * h:HALF * (h + 1)],
+                                        start=(a == 0), stop=(a == 1))
+                nc.vector.tensor_tensor(out=prod[:, t, :], in0=bank[:], in1=y[:, t, :], op=MULT)
+            return prod
+
+        def w2_lhs(a, t):
+            return (w2_codes[:, a, 2 * P * t:2 * P * (t + 1)].bitcast(FP4X4),
+                    w2_scale[:, H * a + P * t:H * a + P * (t + 1)])
+
+        w1_bf = [round_weight("w1_bf%d" % a, w1_raw[a]) for a in range(2)]
+        prod_i = [x_times_y("prod_i0", w2_lhs, yi[0], 0)]
+        w1_q = [quantize("w1_0", w1_bf[0][:], H)]
+        w3_codes = tile("w3_codes", [P, H], U32)
+        nc.vector.tensor_copy(out=w3_codes[:].bitcast(I32).rearrange("p (t b q) -> p t b q", t=4, q=4),
+                              in_=w3_raw[:].bitcast(I32).rearrange("p (b t q) -> p t b q", t=4, q=4))
+        w3_scale = tile("w3_scale", [P, H], U8)
+        nc.vector.tensor_copy(out=w3_scale[:].bitcast(I32).rearrange("p (t b) -> p t b", t=4),
+                              in_=w3_scale_raw[:].bitcast(I32).rearrange("p (b t) -> p t b", t=4))
+        prod_i.append(x_times_y("prod_i1", w2_lhs, yi[1], 1))
+        w1_q.append(quantize("w1_1", w1_bf[1][:], H))
+
+
+        def w1_lhs(a, t):
+            return (w1_q[a][0][:, P * t:P * (t + 1)].bitcast(FP8X4), w1_q[a][1][:, P * t:P * (t + 1)])
+
+        yr = [y_part("yr%d" % h, w3_codes, w3_scale, h) for h in range(2)]
+
+        w5_bf = tile("w5_bf", [P, 4 * N], BF16)
+        nc.scalar.copy(out=w5_bf[:].rearrange("p (c i t) -> p c t i", i=4, t=4),
+                       in_=w5_raw[:].rearrange("p t (c i) -> p c t i", i=4))
+
+        def add_round(name, h, j0, width):
+            hb = tile(name, [P, 4 * width], BF16)
+            nc.vector.tensor_tensor(out=hb[:].rearrange("p (c i t) -> p c t i", i=4, t=4),
+                                    in0=prod_r[h][:, :, j0:j0 + width].rearrange("p t (c i) -> p c t i", i=4),
+                                    in1=prod_i[h][:, :, j0:j0 + width].rearrange("p t (c i) -> p c t i", i=4),
+                                    op=ADD)
+            return hb
+
+        out_rows = out.rearrange("(i p) j -> p i j", p=P)
+        prod_r = [x_times_y("prod_r0", w1_lhs, yr[0], 0)]
+        h_bf0 = add_round("h_bf0", 0, 0, HALF)
+        w5_codes = tile("w5_codes", [P, N], U32)
+        w5_scales = tile("w5_scales", [P, N], U8)
+        nc.vector.quantize_mx(out=w5_codes[:, 0:256].bitcast(FP8X4), scales=w5_scales[:, 0:256], in_=w5_bf[:, 0:1024])
+        nc.vector.quantize_mx(out=w5_codes[:, 256:N].bitcast(FP8X4), scales=w5_scales[:, 256:N], in_=w5_bf[:, 1024:4 * N])
+        h_codes, h_scales = quantize("h0", h_bf0[:], HALF)
+        for i in range(3):
+            bank = psum.tile([P, HALF], F32, name="o_ps", tag="o", bufs=2)
+            nc.tensor.matmul_mx(out=bank[:], lhsT=w5_codes[:, P * i:P * (i + 1)].bitcast(FP8X4),
+                                lhsT_scale=w5_scales[:, P * i:P * (i + 1)], rhs=h_codes[:].bitcast(FP8X4),
+                                rhs_scale=h_scales[:], start=True, stop=True)
+            res = tile("res0_%d" % i, [P, HALF], F32)
+            nc.scalar.copy(out=res[:], in_=bank[:])
+            nc.sync.dma_start(out=out_rows[:, i, 0:HALF], in_=res[:])
+
+        prod_r.append(x_times_y("prod_r1", w1_lhs, yr[1], 1))
+
+        def finish(c, hb):
+            codes, scales = quantize("h1_%d" % c, hb[:], TAIL)
+            bank = psum.tile([P, HALF], F32, name="o_ps", tag="o", bufs=2)
+            for i in range(3):
+                nc.tensor.matmul_mx(out=bank[:, TAIL * i:TAIL * (i + 1)],
+                                    lhsT=w5_codes[:, P * i:P * (i + 1)].bitcast(FP8X4),
+                                    lhsT_scale=w5_scales[:, P * i:P * (i + 1)], rhs=codes[:].bitcast(FP8X4),
+                                    rhs_scale=scales[:], start=True, stop=True)
+            res = tile("res1_%d" % c, [P, 3, TAIL], F32)
+            nc.scalar.copy(out=res[:], in_=bank[:, 0:3 * TAIL].rearrange("p (i j) -> p i j", i=3))
+            nc.sync.dma_start(out=out_rows[:, :, HALF + TAIL * c:HALF + TAIL * (c + 1)], in_=res[:])
+
+        chunks = HALF // TAIL
+        hbs = []
+        for c in range(chunks + 1):
+            if c < chunks:
+                hbs.append(add_round("h_bf1_%d" % c, 1, TAIL * c, TAIL))
+            if c > 0:
+                finish(c - 1, hbs[c - 1])

@@ -21,6 +21,9 @@ COPY = mybir.ActivationFunctionType.Copy
 P = 128
 HALF = 512
 TAIL = 128
+YB = 4
+FILL = 2
+EARLY = 3
 
 
 def tile_list_raman_phase_traces_kernel(tc, tab_words, tab_scales, tab2_words, tab2_scales, offs, offs2,
@@ -39,17 +42,15 @@ def tile_list_raman_phase_traces_kernel(tc, tab_words, tab_scales, tab2_words, t
 
         tab_bytes = tile("tab_bytes", [P, T], U8)
         tab2_bytes = tile("tab2_bytes", [P, T], U8)
-        v_scale = [tile("v_scale%d" % a, [P, S], U8) for a in range(2)]
+        w_bytes = tile("w_bytes", [P, 2 * H], U8)
+        plane = [tile("plane0", [P, S + 2 * H], U8), tile("plane1", [P, S + H], U8)]
         win_rows = tile("win_rows", [P, P], F32)
         ident = tile("ident", [P, P], F32)
-        w2_scale_raw = tile("w2_scale_raw", [P, 2 * H], U8)
-        w3_scale_raw = tile("w3_scale_raw", [P, H], U8)
         nc.gpsimd.memset(tab_bytes[:].bitcast(I32), 0)
-        nc.vector.memset(tab2_bytes[:].bitcast(I32), 0)
-        nc.gpsimd.memset(win_rows[:], 0.0)
         make_identity(nc, ident[:])
-        for plane in (v_scale[0], v_scale[1], w2_scale_raw, w3_scale_raw):
-            nc.vector.memset(plane[:].bitcast(I32), 0)
+        nc.gpsimd.memset(win_rows[:], 0.0)
+        for zeroed in (tab2_bytes, w_bytes, plane[0], plane[1]):
+            nc.vector.memset(zeroed[:].bitcast(I32), 0)
 
         def load_words(name, words, width):
             t = tile(name, [P, width], U32)
@@ -61,49 +62,65 @@ def tile_list_raman_phase_traces_kernel(tc, tab_words, tab_scales, tab2_words, t
             nc.sync.dma_start(out=t[:], in_=rows.rearrange("(p j) c -> p j c", j=4))
             return t
 
-        def load_w3_scales(d):
-            nc.sync.dma_start(out=w3_scale_raw[:].bitcast(I32)[32 * d:32 * d + 4, :],
-                              in_=w3_scales[0, 4 * d:4 * d + 4, :].bitcast(I32))
+        def load_scale_rows(dst, first, rows):
+            nc.sync.dma_start(out=dst.bitcast(I32)[first:P:8, :], in_=rows.bitcast(I32))
+
+        def load_tab2_scales(d):
+            nc.sync.dma_start(out=tab2_bytes[:].bitcast(I32)[32 * d:32 * d + 4, :],
+                              in_=tab2_scales[0, 4 * d:4 * d + 4, :].bitcast(I32))
 
         nc.sync.dma_start(offs_sb[:], offs)
         nc.sync.dma_start(offs2_sb[:], offs2)
         for a in range(2):
-            nc.scalar.dma_start(out=tab_bytes[:].bitcast(I32)[4 * a:P:8, :], in_=tab_scales[a].bitcast(I32))
-        for d in range(4):
-            nc.scalar.dma_start(out=tab2_bytes[:].bitcast(I32)[32 * d:32 * d + 4, :],
-                                in_=tab2_scales[0, 4 * d:4 * d + 4, :].bitcast(I32))
-        nc.scalar.dma_start(out=win_rows[0:4, :].rearrange("t (b q) -> t b q", q=4),
-                            in_=win.rearrange("(b t q) -> t b q", t=4, q=4))
-        tab2_w = load_words("tab2_w", tab2_words[0], T)
+            load_scale_rows(tab_bytes[:], 4 * a, tab_scales[a])
+        nc.sync.dma_start(out=win_rows[0:4, :].rearrange("t (b q) -> t b q", q=4),
+                          in_=win.rearrange("(b t q) -> t b q", t=4, q=4))
         w4_raw = load_rows("w4_raw", w4)
-        tab_w = [load_words("tab_w0", tab_words[0], T)]
-        w2_raw = tile("w2_raw", [P, 2, 2 * H], U8)
-        nc.sync.dma_start(out=w2_raw[:].bitcast(I32), in_=w2_words.rearrange("a p c -> p a c").bitcast(I32))
         for d in range(4):
-            nc.sync.dma_start(out=w2_scale_raw[:].bitcast(I32).rearrange("p (a c) -> p a c", a=2)[32 * d:32 * d + 4],
-                              in_=w2_scales[:, 4 * d:4 * d + 4, :].rearrange("a r c -> r a c").bitcast(I32))
-        tab_w.append(load_words("tab_w1", tab_words[1], T))
+            load_tab2_scales(d)
+        for a in range(2):
+            load_scale_rows(w_bytes[:, 0:H], 4 * a, w2_scales[a])
+        tab2_w = load_words("tab2_w", tab2_words[0], T)
+        load_scale_rows(w_bytes[:, H:2 * H], 0, w3_scales[0])
         w1_raw = [load_rows("w1_raw0", w1[0:512, :])]
-        w3_raw = load_words("w3_raw", w3_words[0], H)
-        load_w3_scales(0)
-        load_w3_scales(1)
-        w1_raw.append(load_rows("w1_raw1", w1[512:K, :]))
-        load_w3_scales(2)
-        load_w3_scales(3)
-        w5_raw = tile("w5_raw", [P, 4, N], F32)
-        w5_by_q = w5.rearrange("(b t q) n -> q b t n", t=4, q=4)
-        for q in range(4):
-            nc.sync.dma_start(out=w5_raw[q:P:4, :, :], in_=w5_by_q[q])
-
-        win_ps = psum.tile([P, HALF], F32, name="win_ps", tag="o", bufs=2)
+        tab_w = [load_words("tab_w0", tab_words[0], T)]
+        win_ps = psum.tile([P, HALF], F32, name="win_ps", tag="y", bufs=YB)
         nc.tensor.transpose(win_ps[:, 0:P], win_rows[:], ident[:])
         win_col = tile("win_col", [P, 4], F32)
         nc.scalar.activation(out=win_col[:], in_=win_ps[:, 0:4], func=COPY)
 
+        staged = tile("staged", [P, S + 2 * H], U8)
         picked = tile("picked", [P, S], U8)
         nc.vector.tensor_copy(picked[:], tab_bytes[:].indirect(offs_sb[:]))
         v2_scale = tile("v2_scale", [P, S], U8)
         nc.vector.tensor_copy(v2_scale[:], tab2_bytes[:].indirect(offs2_sb[:]))
+        nc.vector.tensor_copy(out=staged[:, 0:S].bitcast(I32), in_=picked[:].bitcast(I32))
+        nc.vector.tensor_copy(out=staged[:, S:S + 2 * H].bitcast(I32).rearrange("p (s t b) -> p s t b", s=2, t=4),
+                              in_=w_bytes[:].bitcast(I32).rearrange("p (s b t) -> p s t b", s=2, t=4))
+        v_scale = [plane[a][:, 0:S] for a in range(2)]
+        w2_scale = [plane[a][:, S:S + H] for a in range(2)]
+        w3_scale = plane[0][:, S + H:S + 2 * H]
+
+        def move_scale_rows(a, rows):
+            for r in rows:
+                nc.sync.dma_start(out=plane[a][:].bitcast(I32)[r:P:32, :],
+                                  in_=staged[:, 0:plane[a].shape[1]].bitcast(I32)[8 * r + 4 * a:P:32, :])
+
+        move_scale_rows(1, range(4))
+        tab_w.append(load_words("tab_w1", tab_words[1], T))
+        move_scale_rows(0, range(4))
+        w2_raw = tile("w2_raw", [P, 2, 2 * H], U8)
+        nc.sync.dma_start(out=w2_raw[:].bitcast(I32), in_=w2_words.rearrange("a p c -> p a c").bitcast(I32))
+        w3_raw = load_words("w3_raw", w3_words[0], H)
+        w1_last = []
+        for u in range(2):
+            w1_last.append(tile("w1_last%d" % u, [P, 4, H // 2], F32))
+            nc.sync.dma_start(out=w1_last[u][:],
+                              in_=w1[512:K, 256 * u:256 * (u + 1)].rearrange("(p j) c -> p j c", j=4))
+        w5_raw = tile("w5_raw", [P, 4, N], F32)
+        w5_by_q = w5.rearrange("(b t q) n -> q b t n", t=4, q=4)
+        for q in range(4):
+            nc.sync.dma_start(out=w5_raw[q:P:4, :, :], in_=w5_by_q[q])
 
         def gather_words(name, window, offsets, after=None):
             t = tile(name, [P, 16 * offsets.shape[1]], U32, after)
@@ -112,128 +129,120 @@ def tile_list_raman_phase_traces_kernel(tc, tab_words, tab_scales, tab2_words, t
 
         def round_weight(name, raw):
             g = tile(name, [P, 4 * H], BF16)
-            nc.scalar.copy(out=g[:].rearrange("p (t b q j) -> p t b j q", t=4, q=4, j=4),
-                           in_=raw[:].rearrange("p j (b t q) -> p t b j q", t=4, q=4))
+            for t in range(4):
+                nc.scalar.activation(out=g[:, H * t:H * (t + 1)].rearrange("p (b q j) -> p b j q", q=4, j=4),
+                                     in_=raw[:].rearrange("p j (b t q) -> p t b j q", t=4, q=4)[:, t], func=COPY)
             return g
 
-        def quantize(name, src, width):
-            codes = tile(name + "_codes", [P, width], U32)
+        def quantize(name, src, width, after=None):
+            codes = tile(name + "_codes", [P, width], U32, after)
             scales = tile(name + "_scales", [P, width], U8)
             nc.vector.quantize_mx(out=codes[:].bitcast(FP8X4), scales=scales[:], in_=src)
             return codes, scales
 
-        v2 = gather_words("v2", tab2_w, offs2_sb[:])
         w4_bf = round_weight("w4_bf", w4_raw)
-        w4_codes, w4_scales = quantize("w4", w4_bf[:], H)
-        for a in range(2):
-            for r in range(4):
-                nc.scalar.dma_start(out=v_scale[a][:].bitcast(I32)[r:P:32, :],
-                                    in_=picked[:].bitcast(I32)[8 * r + 4 * a:P:32, :])
+        w4_codes, w4_scales = quantize("w4", w4_bf[:], H, "w_bytes")
+        v2 = [gather_words("v2_0", tab2_w, offs2_sb[:, 0:32]), gather_words("v2_1", tab2_w, offs2_sb[:, 32:64], "w4_bf")]
 
-        def y_part(name, codes, scales, h):
-            y = tile(name, [P, 4, HALF], F32)
+        def y_part(name, codes, scales, h, after=None):
+            y = tile(name, [P, 4, HALF], F32, after)
             for t in range(4):
-                bank = psum.tile([P, HALF], F32, name="y_ps", tag="y", bufs=3)
+                bank = psum.tile([P, HALF], F32, name="y_ps", tag="y", bufs=YB)
                 nc.tensor.matmul_mx(out=bank[:], lhsT=codes[:, P * t:P * (t + 1)].bitcast(FP8X4),
-                                    lhsT_scale=scales[:, P * t:P * (t + 1)], rhs=v2[:, HALF * h:HALF * (h + 1)].bitcast(FP8X4),
+                                    lhsT_scale=scales[:, P * t:P * (t + 1)], rhs=v2[h][:].bitcast(FP8X4),
                                     rhs_scale=v2_scale[:, HALF * h:HALF * (h + 1)], start=True, stop=True)
                 nc.scalar.activation(out=y[:, t, :], in_=bank[:], func=COPY, scale=win_col[:, t:t + 1])
             return y
 
-        yi = [y_part("yi%d" % h, w4_codes, w4_scales, h) for h in range(2)]
 
-        v_first = gather_words("v_first", tab_w[0], offs_sb[:], "w4_bf")
+        w1_bf = [round_weight("w1_bf0", w1_raw[0])]
+        yi = [y_part("yi0", w4_codes, w4_scales, 0, "w1_raw0"), y_part("yi1", w4_codes, w4_scales, 1)]
+        v_first = gather_words("v_first", tab_w[0], offs_sb[:])
         v = [[v_first[:, HALF * h:HALF * (h + 1)]] for h in range(2)]
+        w1_q = [quantize("w1_0", w1_bf[0][:], H, "tab_w0")]
+        v[0].append(gather_words("v0_1", tab_w[1], offs_sb[:, 0:32])[:])
         w2_codes = tile("w2_codes", [P, 2, 2 * H], U8)
         nc.vector.tensor_copy(out=w2_codes[:].bitcast(I32).rearrange("p a (t b e) -> p a t b e", t=4, e=2),
                               in_=w2_raw[:].bitcast(I32).rearrange("p a (b t e) -> p a t b e", t=4, e=2))
-        w2_scale = tile("w2_scale", [P, 2 * H], U8)
-        nc.vector.tensor_copy(out=w2_scale[:].bitcast(I32).rearrange("p (a t b) -> p a t b", a=2, t=4),
-                              in_=w2_scale_raw[:].bitcast(I32).rearrange("p (a b t) -> p a t b", a=2, t=4))
-        for h in range(2):
-            v[h].append(gather_words("v%d_1" % h, tab_w[1], offs_sb[:, 32 * h:32 * (h + 1)])[:])
-
-        def x_times_y(name, lhs, y, h):
-            prod = tile(name, [P, 4, HALF], F32)
-            for t in range(4):
-                bank = psum.tile([P, HALF], F32, name="x_ps", tag="x", bufs=3)
-                for a in range(2):
-                    codes, scales = lhs(a, t)
-                    nc.tensor.matmul_mx(out=bank[:], lhsT=codes, lhsT_scale=scales, rhs=v[h][a].bitcast(FP8X4),
-                                        rhs_scale=v_scale[a][:, HALF * h:HALF * (h + 1)],
-                                        start=(a == 0), stop=(a == 1))
-                nc.vector.tensor_tensor(out=prod[:, t, :], in0=bank[:], in1=y[:, t, :], op=MULT)
-            return prod
-
-        def w2_lhs(a, t):
-            return (w2_codes[:, a, 2 * P * t:2 * P * (t + 1)].bitcast(FP4X4),
-                    w2_scale[:, H * a + P * t:H * a + P * (t + 1)])
-
-        w1_bf = [round_weight("w1_bf%d" % a, w1_raw[a]) for a in range(2)]
-        prod_i = [x_times_y("prod_i0", w2_lhs, yi[0], 0)]
-        w1_q = [quantize("w1_0", w1_bf[0][:], H)]
+        v[1].append(gather_words("v1_1", tab_w[1], offs_sb[:, 32:64], "w2_raw")[:])
         w3_codes = tile("w3_codes", [P, H], U32)
         nc.vector.tensor_copy(out=w3_codes[:].bitcast(I32).rearrange("p (t b q) -> p t b q", t=4, q=4),
                               in_=w3_raw[:].bitcast(I32).rearrange("p (b t q) -> p t b q", t=4, q=4))
-        w3_scale = tile("w3_scale", [P, H], U8)
-        nc.vector.tensor_copy(out=w3_scale[:].bitcast(I32).rearrange("p (t b) -> p t b", t=4),
-                              in_=w3_scale_raw[:].bitcast(I32).rearrange("p (b t) -> p t b", t=4))
-        prod_i.append(x_times_y("prod_i1", w2_lhs, yi[1], 1))
+        w1_bf.append(tile("w1_bf1", [P, 4 * H], BF16))
+        for u in range(2):
+            for t in range(4):
+                nc.scalar.activation(
+                    out=w1_bf[1][:, H * t + 256 * u:H * t + 256 * (u + 1)].rearrange("p (b q j) -> p b j q", q=4, j=4),
+                    in_=w1_last[u][:].rearrange("p j (b t q) -> p t b j q", t=4, q=4)[:, t], func=COPY)
         w1_q.append(quantize("w1_1", w1_bf[1][:], H))
 
+        def x_times_y(prod, lhs, y, h, slots):
+            for t in slots:
+                bank = psum.tile([P, HALF], F32, name="x_ps", tag="x", bufs=8 - YB)
+                for a in (1, 0):
+                    codes, scales = lhs(a, t)
+                    nc.tensor.matmul_mx(out=bank[:], lhsT=codes, lhsT_scale=scales, rhs=v[h][a].bitcast(FP8X4),
+                                        rhs_scale=v_scale[a][:, HALF * h:HALF * (h + 1)],
+                                        start=(a == 1), stop=(a == 0))
+                nc.vector.tensor_tensor(out=prod[:, t, :], in0=bank[:], in1=y[:, t, :], op=MULT)
+
+        def w2_lhs(a, t):
+            return (w2_codes[:, a, 2 * P * t:2 * P * (t + 1)].bitcast(FP4X4),
+                    w2_scale[a][:, P * t:P * (t + 1)])
 
         def w1_lhs(a, t):
             return (w1_q[a][0][:, P * t:P * (t + 1)].bitcast(FP8X4), w1_q[a][1][:, P * t:P * (t + 1)])
 
-        yr = [y_part("yr%d" % h, w3_codes, w3_scale, h) for h in range(2)]
+        def add_round(engine, hb, h, j0, width):
+            engine.tensor_tensor(out=hb.rearrange("p (c i t) -> p c t i", i=2, t=4),
+                                 in0=prod_r[h][:, :, j0:j0 + width].rearrange("p t (c i) -> p c t i", i=2),
+                                 in1=prod_i[h][:, :, j0:j0 + width].rearrange("p t (c i) -> p c t i", i=2),
+                                 op=ADD)
 
+        prod_i = [tile("prod_i%d" % h, [P, 4, HALF], F32) for h in range(2)]
+        prod_r = [tile("prod_r%d" % h, [P, 4, HALF], F32) for h in range(2)]
+        x_times_y(prod_i[0], w2_lhs, yi[0], 0, range(4))
+        yr = [y_part("yr0", w3_codes, w3_scale, 0, "w1_last1")]
+        x_times_y(prod_i[1], w2_lhs, yi[1], 1, range(FILL))
+        x_times_y(prod_r[0], w1_lhs, yr[0], 0, range(4))
+        h_bf = []
+        for c in range(EARLY):
+            h_bf.append(tile("h_bf%d" % c, [P, 4 * TAIL], BF16))
+            add_round(nc.gpsimd, h_bf[c][:], 0, TAIL * c, TAIL)
+        yr.append(y_part("yr1", w3_codes, w3_scale, 1))
         w5_bf = tile("w5_bf", [P, 4 * N], BF16)
         nc.scalar.copy(out=w5_bf[:].rearrange("p (c i t) -> p c t i", i=4, t=4),
                        in_=w5_raw[:].rearrange("p t (c i) -> p c t i", i=4))
-
-        def add_round(name, h, j0, width):
-            hb = tile(name, [P, 4 * width], BF16)
-            nc.vector.tensor_tensor(out=hb[:].rearrange("p (c i t) -> p c t i", i=4, t=4),
-                                    in0=prod_r[h][:, :, j0:j0 + width].rearrange("p t (c i) -> p c t i", i=4),
-                                    in1=prod_i[h][:, :, j0:j0 + width].rearrange("p t (c i) -> p c t i", i=4),
-                                    op=ADD)
-            return hb
+        x_times_y(prod_i[1], w2_lhs, yi[1], 1, range(FILL, 4))
+        x_times_y(prod_r[1], w1_lhs, yr[1], 1, range(4))
 
         out_rows = out.rearrange("(i p) j -> p i j", p=P)
-        prod_r = [x_times_y("prod_r0", w1_lhs, yr[0], 0)]
-        h_bf0 = add_round("h_bf0", 0, 0, HALF)
-        w5_codes = tile("w5_codes", [P, N], U32)
+        w5_codes = tile("w5_codes", [P, N], U32, "yr1")
         w5_scales = tile("w5_scales", [P, N], U8)
         nc.vector.quantize_mx(out=w5_codes[:, 0:256].bitcast(FP8X4), scales=w5_scales[:, 0:256], in_=w5_bf[:, 0:1024])
         nc.vector.quantize_mx(out=w5_codes[:, 256:N].bitcast(FP8X4), scales=w5_scales[:, 256:N], in_=w5_bf[:, 1024:4 * N])
-        h_codes, h_scales = quantize("h0", h_bf0[:], HALF)
-        for i in range(3):
-            bank = psum.tile([P, HALF], F32, name="o_ps", tag="o", bufs=2)
-            nc.tensor.matmul_mx(out=bank[:], lhsT=w5_codes[:, P * i:P * (i + 1)].bitcast(FP8X4),
-                                lhsT_scale=w5_scales[:, P * i:P * (i + 1)], rhs=h_codes[:].bitcast(FP8X4),
-                                rhs_scale=h_scales[:], start=True, stop=True)
-            res = tile("res0_%d" % i, [P, HALF], F32)
-            nc.scalar.copy(out=res[:], in_=bank[:])
-            nc.sync.dma_start(out=out_rows[:, i, 0:HALF], in_=res[:])
 
-        prod_r.append(x_times_y("prod_r1", w1_lhs, yr[1], 1))
+        chunks = S // TAIL
 
-        def finish(c, hb):
-            codes, scales = quantize("h1_%d" % c, hb[:], TAIL)
-            bank = psum.tile([P, HALF], F32, name="o_ps", tag="o", bufs=2)
+        def finish(c):
+            codes, scales = quantize("h%d" % c, h_bf[c][:], TAIL, "w5_bf" if c == 0 else None)
+            bank = psum.tile([P, HALF], F32, name="o_ps", tag="y", bufs=YB)
             for i in range(3):
                 nc.tensor.matmul_mx(out=bank[:, TAIL * i:TAIL * (i + 1)],
                                     lhsT=w5_codes[:, P * i:P * (i + 1)].bitcast(FP8X4),
                                     lhsT_scale=w5_scales[:, P * i:P * (i + 1)], rhs=codes[:].bitcast(FP8X4),
                                     rhs_scale=scales[:], start=True, stop=True)
-            res = tile("res1_%d" % c, [P, 3, TAIL], F32)
-            nc.scalar.copy(out=res[:], in_=bank[:, 0:3 * TAIL].rearrange("p (i j) -> p i j", i=3))
-            nc.sync.dma_start(out=out_rows[:, :, HALF + TAIL * c:HALF + TAIL * (c + 1)], in_=res[:])
+            res = tile("res%d" % c, [P, 3, TAIL], F32)
+            if c == chunks - 1:
+                nc.vector.tensor_copy(out=res[:], in_=bank[:, 0:3 * TAIL].rearrange("p (i j) -> p i j", i=3))
+            else:
+                nc.scalar.copy(out=res[:], in_=bank[:, 0:3 * TAIL].rearrange("p (i j) -> p i j", i=3))
+            nc.sync.dma_start(out=out_rows[:, :, TAIL * c:TAIL * (c + 1)], in_=res[:])
 
-        chunks = HALF // TAIL
-        hbs = []
-        for c in range(chunks + 1):
+        for c in range(EARLY - 1):
+            finish(c)
+        for c in range(EARLY, chunks + 1):
             if c < chunks:
-                hbs.append(add_round("h_bf1_%d" % c, 1, TAIL * c, TAIL))
-            if c > 0:
-                finish(c - 1, hbs[c - 1])
+                h_bf.append(tile("h_bf%d" % c, [P, 4 * TAIL], BF16, "h_bf0" if c == EARLY else None))
+                add_round(nc.vector, h_bf[c][:], c // 4, TAIL * (c % 4), TAIL)
+            finish(c - 1)

@@ -23,7 +23,6 @@ HALF = 512
 TAIL = 128
 YB = 4
 FILL = 2
-EARLY = 3
 
 
 def tile_list_raman_phase_traces_kernel(tc, tab_words, tab_scales, tab2_words, tab2_scales, offs, offs2,
@@ -199,20 +198,24 @@ def tile_list_raman_phase_traces_kernel(tc, tab_words, tab_scales, tab2_words, t
                                  in1=prod_i[h][:, :, j0:j0 + width].rearrange("p t (c i) -> p c t i", i=2),
                                  op=ADD)
 
-        prod_i = [tile("prod_i%d" % h, [P, 4, HALF], F32) for h in range(2)]
+        prod_i = [tile("prod_i0", [P, 4, HALF], F32), tile("prod_i1", [P, 4, HALF], F32, "w1_bf1")]
         prod_r = [tile("prod_r%d" % h, [P, 4, HALF], F32) for h in range(2)]
         x_times_y(prod_i[0], w2_lhs, yi[0], 0, range(4))
         yr = [y_part("yr0", w3_codes, w3_scale, 0, "w1_last1")]
         x_times_y(prod_i[1], w2_lhs, yi[1], 1, range(FILL))
-        x_times_y(prod_r[0], w1_lhs, yr[0], 0, range(4))
-        h_bf = []
-        for c in range(EARLY):
-            h_bf.append(tile("h_bf%d" % c, [P, 4 * TAIL], BF16))
-            add_round(nc.gpsimd, h_bf[c][:], 0, TAIL * c, TAIL)
         yr.append(y_part("yr1", w3_codes, w3_scale, 1))
+        x_times_y(prod_r[0], w1_lhs, yr[0], 0, range(4))
+        h_rows = tile("h_rows", [P, 4, HALF], BF16)
+        for t in range(4):
+            nc.gpsimd.tensor_tensor(out=h_rows[:, t, :], in0=prod_r[0][:, t, :], in1=prod_i[0][:, t, :], op=ADD)
         w5_bf = tile("w5_bf", [P, 4 * N], BF16)
         nc.scalar.copy(out=w5_bf[:].rearrange("p (c i t) -> p c t i", i=4, t=4),
                        in_=w5_raw[:].rearrange("p t (c i) -> p c t i", i=4))
+        h_bf = []
+        for c in range(4):
+            h_bf.append(tile("h_bf%d" % c, [P, 4 * TAIL], BF16))
+            nc.scalar.copy(out=h_bf[c][:].rearrange("p (c i t) -> p c t i", i=4, t=4),
+                           in_=h_rows[:, :, TAIL * c:TAIL * (c + 1)].rearrange("p t (c i) -> p c t i", i=4))
         x_times_y(prod_i[1], w2_lhs, yi[1], 1, range(FILL, 4))
         x_times_y(prod_r[1], w1_lhs, yr[1], 1, range(4))
 
@@ -225,7 +228,7 @@ def tile_list_raman_phase_traces_kernel(tc, tab_words, tab_scales, tab2_words, t
         chunks = S // TAIL
 
         def finish(c):
-            codes, scales = quantize("h%d" % c, h_bf[c][:], TAIL, "w5_bf" if c == 0 else None)
+            codes, scales = quantize("h%d" % c, h_bf[c][:], TAIL)
             bank = psum.tile([P, HALF], F32, name="o_ps", tag="y", bufs=YB)
             for i in range(3):
                 nc.tensor.matmul_mx(out=bank[:, TAIL * i:TAIL * (i + 1)],
@@ -239,10 +242,16 @@ def tile_list_raman_phase_traces_kernel(tc, tab_words, tab_scales, tab2_words, t
                 nc.scalar.copy(out=res[:], in_=bank[:, 0:3 * TAIL].rearrange("p (i j) -> p i j", i=3))
             nc.sync.dma_start(out=out_rows[:, :, TAIL * c:TAIL * (c + 1)], in_=res[:])
 
-        for c in range(EARLY - 1):
-            finish(c)
-        for c in range(EARLY, chunks + 1):
-            if c < chunks:
-                h_bf.append(tile("h_bf%d" % c, [P, 4 * TAIL], BF16, "h_bf0" if c == EARLY else None))
-                add_round(nc.vector, h_bf[c][:], c // 4, TAIL * (c % 4), TAIL)
+        def add_late(c):
+            h_bf.append(tile("h_bf%d" % c, [P, 4 * TAIL], BF16))
+            add_round(nc.vector, h_bf[c][:], 1, TAIL * (c - 4), TAIL)
+
+        finish(0)
+        finish(1)
+        add_late(4)
+        finish(2)
+        finish(3)
+        for c in range(5, chunks):
+            add_late(c)
             finish(c - 1)
+        finish(chunks - 1)

@@ -46,10 +46,9 @@ def tile_list_raman_phase_traces_kernel(tc, tab_words, tab_scales, tab2_words, t
         win_rows = tile("win_rows", [P, P], F32)
         ident = tile("ident", [P, P], F32)
         nc.gpsimd.memset(tab_bytes[:].bitcast(I32), 0)
-        make_identity(nc, ident[:])
-        nc.gpsimd.memset(win_rows[:], 0.0)
-        for zeroed in (tab2_bytes, w_bytes, plane[0], plane[1]):
+        for zeroed in (w_bytes, tab2_bytes, win_rows, ident, plane[0], plane[1]):
             nc.vector.memset(zeroed[:].bitcast(I32), 0)
+        make_identity(nc, ident[:], nomemset=True)
 
         def load_words(name, words, width):
             t = tile(name, [P, width], U32)
@@ -72,21 +71,19 @@ def tile_list_raman_phase_traces_kernel(tc, tab_words, tab_scales, tab2_words, t
         nc.sync.dma_start(offs2_sb[:], offs2)
         for a in range(2):
             load_scale_rows(tab_bytes[:], 4 * a, tab_scales[a])
-        nc.sync.dma_start(out=win_rows[0:4, :].rearrange("t (b q) -> t b q", q=4),
-                          in_=win.rearrange("(b t q) -> t b q", t=4, q=4))
+        load_scale_rows(w_bytes[:, H:2 * H], 0, w3_scales[0])
         w4_raw = load_rows("w4_raw", w4)
         for d in range(4):
             load_tab2_scales(d)
         for a in range(2):
             load_scale_rows(w_bytes[:, 0:H], 4 * a, w2_scales[a])
         tab2_w = load_words("tab2_w", tab2_words[0], T)
-        load_scale_rows(w_bytes[:, H:2 * H], 0, w3_scales[0])
+        nc.sync.dma_start(out=win_rows[0:4, :].rearrange("t (b q) -> t b q", q=4),
+                          in_=win.rearrange("(b t q) -> t b q", t=4, q=4))
         w1_raw = [load_rows("w1_raw0", w1[0:512, :])]
         tab_w = [load_words("tab_w0", tab_words[0], T)]
         win_ps = psum.tile([P, HALF], F32, name="win_ps", tag="y", bufs=YB)
         nc.tensor.transpose(win_ps[:, 0:P], win_rows[:], ident[:])
-        win_col = tile("win_col", [P, 4], F32)
-        nc.scalar.activation(out=win_col[:], in_=win_ps[:, 0:4], func=COPY)
 
         staged = tile("staged", [P, S + 2 * H], U8)
         picked = tile("picked", [P, S], U8)
@@ -140,8 +137,8 @@ def tile_list_raman_phase_traces_kernel(tc, tab_words, tab_scales, tab2_words, t
             return codes, scales
 
         w4_bf = round_weight("w4_bf", w4_raw)
-        w4_codes, w4_scales = quantize("w4", w4_bf[:], H, "w_bytes")
-        v2 = [gather_words("v2_0", tab2_w, offs2_sb[:, 0:32]), gather_words("v2_1", tab2_w, offs2_sb[:, 32:64], "w4_bf")]
+        w4_codes, w4_scales = quantize("w4", w4_bf[:], H, "tab2_bytes")
+        v2 = [gather_words("v2_0", tab2_w, offs2_sb[:, 0:32]), gather_words("v2_1", tab2_w, offs2_sb[:, 32:64])]
 
         def y_part(name, codes, scales, h, after=None):
             y = tile(name, [P, 4, HALF], F32, after)
@@ -155,18 +152,20 @@ def tile_list_raman_phase_traces_kernel(tc, tab_words, tab_scales, tab2_words, t
 
 
         w1_bf = [round_weight("w1_bf0", w1_raw[0])]
-        yi = [y_part("yi0", w4_codes, w4_scales, 0, "w1_raw0"), y_part("yi1", w4_codes, w4_scales, 1)]
+        win_col = tile("win_col", [P, 4], F32, "w1_raw0")
+        nc.scalar.activation(out=win_col[:], in_=win_ps[:, 0:4], func=COPY)
+        yi = [y_part("yi%d" % h, w4_codes, w4_scales, h) for h in range(2)]
         v_first = gather_words("v_first", tab_w[0], offs_sb[:])
         v = [[v_first[:, HALF * h:HALF * (h + 1)]] for h in range(2)]
-        w1_q = [quantize("w1_0", w1_bf[0][:], H, "tab_w0")]
         v[0].append(gather_words("v0_1", tab_w[1], offs_sb[:, 0:32])[:])
         w2_codes = tile("w2_codes", [P, 2, 2 * H], U8)
         nc.vector.tensor_copy(out=w2_codes[:].bitcast(I32).rearrange("p a (t b e) -> p a t b e", t=4, e=2),
                               in_=w2_raw[:].bitcast(I32).rearrange("p a (b t e) -> p a t b e", t=4, e=2))
-        v[1].append(gather_words("v1_1", tab_w[1], offs_sb[:, 32:64], "w2_raw")[:])
         w3_codes = tile("w3_codes", [P, H], U32)
         nc.vector.tensor_copy(out=w3_codes[:].bitcast(I32).rearrange("p (t b q) -> p t b q", t=4, q=4),
                               in_=w3_raw[:].bitcast(I32).rearrange("p (b t q) -> p t b q", t=4, q=4))
+        v[1].append(gather_words("v1_1", tab_w[1], offs_sb[:, 32:64], "w2_raw")[:])
+        w1_q = [quantize("w1_0", w1_bf[0][:], H, "w3_raw")]
         w1_bf.append(tile("w1_bf1", [P, 4 * H], BF16))
         for u in range(2):
             for t in range(4):
@@ -183,7 +182,7 @@ def tile_list_raman_phase_traces_kernel(tc, tab_words, tab_scales, tab2_words, t
                     nc.tensor.matmul_mx(out=bank[:], lhsT=codes, lhsT_scale=scales, rhs=v[h][a].bitcast(FP8X4),
                                         rhs_scale=v_scale[a][:, HALF * h:HALF * (h + 1)],
                                         start=(a == 1), stop=(a == 0))
-                nc.vector.tensor_tensor(out=prod[:, t, :], in0=bank[:], in1=y[:, t, :], op=MULT)
+                nc.vector.tensor_tensor(out=prod[:, t, :], in0=y[:, t, :], in1=bank[:], op=MULT)
 
         def w2_lhs(a, t):
             return (w2_codes[:, a, 2 * P * t:2 * P * (t + 1)].bitcast(FP4X4),
@@ -211,47 +210,60 @@ def tile_list_raman_phase_traces_kernel(tc, tab_words, tab_scales, tab2_words, t
         w5_bf = tile("w5_bf", [P, 4 * N], BF16)
         nc.scalar.copy(out=w5_bf[:].rearrange("p (c i t) -> p c t i", i=4, t=4),
                        in_=w5_raw[:].rearrange("p t (c i) -> p c t i", i=4))
+        h_first = tile("h_first", [P, 4 * HALF], BF16, "w5_raw")
         h_bf = []
         for c in range(4):
-            h_bf.append(tile("h_bf%d" % c, [P, 4 * TAIL], BF16))
-            nc.scalar.copy(out=h_bf[c][:].rearrange("p (c i t) -> p c t i", i=4, t=4),
+            h_bf.append(h_first[:, 4 * TAIL * c:4 * TAIL * (c + 1)])
+            nc.scalar.copy(out=h_bf[c].rearrange("p (c i t) -> p c t i", i=4, t=4),
                            in_=h_rows[:, :, TAIL * c:TAIL * (c + 1)].rearrange("p t (c i) -> p c t i", i=4))
         x_times_y(prod_i[1], w2_lhs, yi[1], 1, range(FILL, 4))
         x_times_y(prod_r[1], w1_lhs, yr[1], 1, range(4))
 
         out_rows = out.rearrange("(i p) j -> p i j", p=P)
-        w5_codes = tile("w5_codes", [P, N], U32, "yr1")
+        w5_codes = tile("w5_codes", [P, N], U32, "yi1")
         w5_scales = tile("w5_scales", [P, N], U8)
         nc.vector.quantize_mx(out=w5_codes[:, 0:256].bitcast(FP8X4), scales=w5_scales[:, 0:256], in_=w5_bf[:, 0:1024])
         nc.vector.quantize_mx(out=w5_codes[:, 256:N].bitcast(FP8X4), scales=w5_scales[:, 256:N], in_=w5_bf[:, 1024:4 * N])
 
         chunks = S // TAIL
+        pairs = []
 
         def finish(c):
-            codes, scales = quantize("h%d" % c, h_bf[c][:], TAIL)
+            codes, scales = quantize("h%d" % c, h_bf[c], TAIL)
             bank = psum.tile([P, HALF], F32, name="o_ps", tag="y", bufs=YB)
             for i in range(3):
                 nc.tensor.matmul_mx(out=bank[:, TAIL * i:TAIL * (i + 1)],
                                     lhsT=w5_codes[:, P * i:P * (i + 1)].bitcast(FP8X4),
                                     lhsT_scale=w5_scales[:, P * i:P * (i + 1)], rhs=codes[:].bitcast(FP8X4),
                                     rhs_scale=scales[:], start=True, stop=True)
-            res = tile("res%d" % c, [P, 3, TAIL], F32)
-            if c == chunks - 1:
-                nc.vector.tensor_copy(out=res[:], in_=bank[:, 0:3 * TAIL].rearrange("p (i j) -> p i j", i=3))
+            sums = bank[:, 0:3 * TAIL].rearrange("p (i j) -> p i j", i=3)
+            if c < 6:
+                if c % 2 == 0:
+                    pairs.append(tile("res%d" % c, [P, 3, 2 * TAIL], F32))
+                nc.scalar.copy(out=pairs[c // 2][:, :, TAIL * (c % 2):TAIL * (c % 2 + 1)], in_=sums)
+                if c % 2 == 1:
+                    nc.sync.dma_start(out=out_rows[:, :, TAIL * (c - 1):TAIL * (c + 1)], in_=pairs[c // 2][:])
             else:
-                nc.scalar.copy(out=res[:], in_=bank[:, 0:3 * TAIL].rearrange("p (i j) -> p i j", i=3))
-            nc.sync.dma_start(out=out_rows[:, :, TAIL * c:TAIL * (c + 1)], in_=res[:])
+                res = tile("res%d" % c, [P, 3, TAIL], F32)
+                if c == chunks - 1:
+                    nc.vector.tensor_copy(out=res[:], in_=sums)
+                else:
+                    nc.scalar.copy(out=res[:], in_=sums)
+                nc.sync.dma_start(out=out_rows[:, :, TAIL * c:TAIL * (c + 1)], in_=res[:])
 
         def add_late(c):
-            h_bf.append(tile("h_bf%d" % c, [P, 4 * TAIL], BF16))
-            add_round(nc.vector, h_bf[c][:], 1, TAIL * (c - 4), TAIL)
+            h_bf.append(tile("h_bf%d" % c, [P, 4 * TAIL], BF16)[:])
+            add_round(nc.vector, h_bf[c], 1, TAIL * (c - 4), TAIL)
 
         finish(0)
         finish(1)
         add_late(4)
         finish(2)
+        add_late(5)
         finish(3)
-        for c in range(5, chunks):
-            add_late(c)
-            finish(c - 1)
-        finish(chunks - 1)
+        finish(4)
+        add_late(6)
+        finish(5)
+        add_late(7)
+        finish(6)
+        finish(7)

@@ -21,12 +21,10 @@ COPY = mybir.ActivationFunctionType.Copy
 P = 128
 HALF = 512
 TAIL = 128
-YB = 4
-FILL = 2
 
 
 def tile_list_raman_phase_traces_kernel(tc, tab_words, tab_scales, tab2_words, tab2_scales, offs, offs2,
-                                                 w1, w2_words, w2_scales, w3_words, w3_scales, w4, win, w5, out):
+                                                     w1, w2_words, w2_scales, w3_words, w3_scales, w4, win, w5, out):
     nc = tc.nc
     with ExitStack() as ctx:
         lists = ctx.enter_context(tc.tile_pool(name="lists", bufs=1))
@@ -42,11 +40,11 @@ def tile_list_raman_phase_traces_kernel(tc, tab_words, tab_scales, tab2_words, t
         tab_bytes = tile("tab_bytes", [P, T], U8)
         tab2_bytes = tile("tab2_bytes", [P, T], U8)
         w_bytes = tile("w_bytes", [P, 2 * H], U8)
-        plane = [tile("plane0", [P, S + 2 * H], U8), tile("plane1", [P, S + H], U8)]
+        plane = [tile("plane0", [P, S + 2 * H], U8), tile("plane1", [P, S + 2 * H], U8)]
         win_rows = tile("win_rows", [P, P], F32)
         ident = tile("ident", [P, P], F32)
-        nc.gpsimd.memset(tab_bytes[:].bitcast(I32), 0)
-        for zeroed in (w_bytes, tab2_bytes, win_rows, ident, plane[0], plane[1]):
+        nc.gpsimd.memset(tab2_bytes[:].bitcast(I32), 0)
+        for zeroed in (tab_bytes, w_bytes, win_rows, ident, plane[1]):
             nc.vector.memset(zeroed[:].bitcast(I32), 0)
         make_identity(nc, ident[:], nomemset=True)
 
@@ -56,79 +54,47 @@ def tile_list_raman_phase_traces_kernel(tc, tab_words, tab_scales, tab2_words, t
             return t
 
         def load_rows(name, rows):
-            t = tile(name, [P, 4, H], F32)
+            t = tile(name, [P, 4, rows.shape[1]], F32)
             nc.sync.dma_start(out=t[:], in_=rows.rearrange("(p j) c -> p j c", j=4))
             return t
 
-        def load_scale_rows(dst, first, rows):
-            nc.sync.dma_start(out=dst.bitcast(I32)[first:P:8, :], in_=rows.bitcast(I32))
+        def load_w1(i):
+            a, u = divmod(i, 2)
+            return load_rows("w1_raw%d" % i, w1[512 * a:512 * (a + 1), 256 * u:256 * (u + 1)])
 
         def load_tab2_scales(d):
             nc.sync.dma_start(out=tab2_bytes[:].bitcast(I32)[32 * d:32 * d + 4, :],
                               in_=tab2_scales[0, 4 * d:4 * d + 4, :].bitcast(I32))
 
+        def load_scale_rows(dst, rows):
+            nc.sync.dma_start(out=dst.bitcast(I32)[0:P:4, :], in_=rows.bitcast(I32).rearrange("a z c -> z a c"))
+
         nc.sync.dma_start(offs_sb[:], offs)
+        w3_raw = load_words("w3_raw", w3_words[0], H)
+        load_scale_rows(tab_bytes[:], tab_scales)
         nc.sync.dma_start(offs2_sb[:], offs2)
-        for a in range(2):
-            load_scale_rows(tab_bytes[:], 4 * a, tab_scales[a])
-        load_scale_rows(w_bytes[:, H:2 * H], 0, w3_scales[0])
+        load_tab2_scales(0)
         w4_raw = load_rows("w4_raw", w4)
-        for d in range(4):
+        for d in range(1, 4):
             load_tab2_scales(d)
-        for a in range(2):
-            load_scale_rows(w_bytes[:, 0:H], 4 * a, w2_scales[a])
-        tab2_w = load_words("tab2_w", tab2_words[0], T)
+        load_scale_rows(w_bytes[:, 0:H], w2_scales)
+        nc.sync.dma_start(out=w_bytes[:, H:2 * H].bitcast(I32)[4:P:8, :], in_=w3_scales[0].bitcast(I32))
         nc.sync.dma_start(out=win_rows[0:4, :].rearrange("t (b q) -> t b q", q=4),
                           in_=win.rearrange("(b t q) -> t b q", t=4, q=4))
-        w1_raw = [load_rows("w1_raw0", w1[0:512, :])]
+        tab2_w = load_words("tab2_w", tab2_words[0], T)
         tab_w = [load_words("tab_w0", tab_words[0], T)]
-        win_ps = psum.tile([P, HALF], F32, name="win_ps", tag="y", bufs=YB)
-        nc.tensor.transpose(win_ps[:, 0:P], win_rows[:], ident[:])
-
-        staged = tile("staged", [P, S + 2 * H], U8)
-        picked = tile("picked", [P, S], U8)
-        nc.vector.tensor_copy(picked[:], tab_bytes[:].indirect(offs_sb[:]))
-        v2_scale = tile("v2_scale", [P, S], U8)
-        nc.vector.tensor_copy(v2_scale[:], tab2_bytes[:].indirect(offs2_sb[:]))
-        nc.vector.tensor_copy(out=staged[:, 0:S].bitcast(I32), in_=picked[:].bitcast(I32))
-        nc.vector.tensor_copy(out=staged[:, S:S + 2 * H].bitcast(I32).rearrange("p (s t b) -> p s t b", s=2, t=4),
-                              in_=w_bytes[:].bitcast(I32).rearrange("p (s b t) -> p s t b", s=2, t=4))
-        v_scale = [plane[a][:, 0:S] for a in range(2)]
-        w2_scale = [plane[a][:, S:S + H] for a in range(2)]
-        w3_scale = plane[0][:, S + H:S + 2 * H]
-
-        def move_scale_rows(a, rows):
-            for r in rows:
-                nc.sync.dma_start(out=plane[a][:].bitcast(I32)[r:P:32, :],
-                                  in_=staged[:, 0:plane[a].shape[1]].bitcast(I32)[8 * r + 4 * a:P:32, :])
-
-        move_scale_rows(1, range(4))
-        tab_w.append(load_words("tab_w1", tab_words[1], T))
-        move_scale_rows(0, range(4))
         w2_raw = tile("w2_raw", [P, 2, 2 * H], U8)
         nc.sync.dma_start(out=w2_raw[:].bitcast(I32), in_=w2_words.rearrange("a p c -> p a c").bitcast(I32))
-        w3_raw = load_words("w3_raw", w3_words[0], H)
-        w1_last = []
-        for u in range(2):
-            w1_last.append(tile("w1_last%d" % u, [P, 4, H // 2], F32))
-            nc.sync.dma_start(out=w1_last[u][:],
-                              in_=w1[512:K, 256 * u:256 * (u + 1)].rearrange("(p j) c -> p j c", j=4))
-        w5_raw = tile("w5_raw", [P, 4, N], F32)
-        w5_by_q = w5.rearrange("(b t q) n -> q b t n", t=4, q=4)
-        for q in range(4):
-            nc.sync.dma_start(out=w5_raw[q:P:4, :, :], in_=w5_by_q[q])
 
-        def gather_words(name, window, offsets, after=None):
-            t = tile(name, [P, 16 * offsets.shape[1]], U32, after)
-            nc.vector.tensor_copy(t[:], window[:].indirect(offsets))
-            return t
+        low = [psum.tile([P, HALF], F32, name="low%d" % t) for t in range(4)]
+        high = [psum.tile([P, HALF], F32, name="high%d" % t) for t in range(4)]
+        win_ps = high[3]
+        nc.tensor.transpose(win_ps[:, 0:P], win_rows[:], ident[:])
 
-        def round_weight(name, raw):
-            g = tile(name, [P, 4 * H], BF16)
-            for t in range(4):
-                nc.scalar.activation(out=g[:, H * t:H * (t + 1)].rearrange("p (b q j) -> p b j q", q=4, j=4),
-                                     in_=raw[:].rearrange("p j (b t q) -> p t b j q", t=4, q=4)[:, t], func=COPY)
-            return g
+        def round_weight(copy, dst, raw, b0):
+            blocks = raw.shape[2] // 16
+            copy(out=dst[:].rearrange("p (t b q j) -> p t b j q", t=4, q=4, j=4)[:, :, b0:b0 + blocks],
+                 in_=raw[:].rearrange("p j (b t q) -> p t b j q", t=4, q=4))
 
         def quantize(name, src, width, after=None):
             codes = tile(name + "_codes", [P, width], U32, after)
@@ -136,53 +102,78 @@ def tile_list_raman_phase_traces_kernel(tc, tab_words, tab_scales, tab2_words, t
             nc.vector.quantize_mx(out=codes[:].bitcast(FP8X4), scales=scales[:], in_=src)
             return codes, scales
 
-        w4_bf = round_weight("w4_bf", w4_raw)
-        w4_codes, w4_scales = quantize("w4", w4_bf[:], H, "tab2_bytes")
-        v2 = [gather_words("v2_0", tab2_w, offs2_sb[:, 0:32]), gather_words("v2_1", tab2_w, offs2_sb[:, 32:64])]
+        def gather_words(name, window, offsets, after=None):
+            t = tile(name, [P, 16 * offsets.shape[1]], U32, after)
+            nc.vector.tensor_copy(t[:], window[:].indirect(offsets))
+            return t
 
-        def y_part(name, codes, scales, h, after=None):
-            y = tile(name, [P, 4, HALF], F32, after)
+        w4_bf = tile("w4_bf", [P, 4 * H], BF16)
+        round_weight(nc.scalar.copy, w4_bf, w4_raw, 0)
+
+        picked = tile("picked", [P, S], U8)
+        nc.vector.tensor_copy(picked[:], tab_bytes[:].indirect(offs_sb[:]))
+        nc.vector.tensor_copy(out=plane[0][:, 0:S].bitcast(I32), in_=picked[:].bitcast(I32))
+        nc.gpsimd.tensor_copy(out=plane[0][:, S:S + 2 * H].bitcast(I32).rearrange("p (s t b) -> p s t b", s=2, t=4),
+                              in_=w_bytes[:].bitcast(I32).rearrange("p (s b t) -> p s t b", s=2, t=4))
+        v2_scale = tile("v2_scale", [P, S], U8)
+        nc.vector.tensor_copy(v2_scale[:], tab2_bytes[:].indirect(offs2_sb[:]))
+        for r in range(4):
+            nc.sync.dma_start(out=plane[1][:].bitcast(I32)[r:P:32, :],
+                              in_=plane[0][:].bitcast(I32)[8 * r + 4:P:32, :])
+        tab_w.append(load_words("tab_w1", tab_words[1], T))
+        for r in range(1, 4):
+            nc.sync.dma_start(out=plane[0][:, 0:S + H].bitcast(I32)[r:P:32, :],
+                              in_=plane[0][:, 0:S + H].bitcast(I32)[8 * r:P:32, :])
+        w1_raw = [load_w1(i) for i in range(4)]
+        w5_raw = tile("w5_raw", [P, 4, N], F32)
+        w5_by_slot = w5.rearrange("(b t q) n -> t b q n", t=4, q=4)
+        for t in range(4):
+            nc.sync.dma_start(out=w5_raw[:, t, :], in_=w5_by_slot[t])
+        v_scale = [plane[a][:, 0:S] for a in range(2)]
+        w2_scale = [plane[a][:, S:S + H] for a in range(2)]
+        w3_scale = plane[1][:, S + H:S + 2 * H]
+
+        win_col = tile("win_col", [P, 4], F32)
+        nc.scalar.copy(out=win_col[:], in_=win_ps[:, 0:4])
+        w4_codes, w4_scales = quantize("w4", w4_bf[:], H)
+        v2 = [gather_words("v2_%d" % h, tab2_w, offs2_sb[:, 32 * h:32 * (h + 1)]) for h in range(2)]
+
+        def y_part(name, codes, scales, h, banks, after):
+            rows = 4 // len(after)
+            parts = [tile("%s_%d" % (name, u), [P, rows, HALF], F32, tag) for u, tag in enumerate(after)]
+            y = [parts[t // rows][:, t % rows, :] for t in range(4)]
             for t in range(4):
-                bank = psum.tile([P, HALF], F32, name="y_ps", tag="y", bufs=YB)
+                bank = banks[t]
                 nc.tensor.matmul_mx(out=bank[:], lhsT=codes[:, P * t:P * (t + 1)].bitcast(FP8X4),
                                     lhsT_scale=scales[:, P * t:P * (t + 1)], rhs=v2[h][:].bitcast(FP8X4),
                                     rhs_scale=v2_scale[:, HALF * h:HALF * (h + 1)], start=True, stop=True)
-                nc.scalar.activation(out=y[:, t, :], in_=bank[:], func=COPY, scale=win_col[:, t:t + 1])
+                nc.scalar.activation(out=y[t], in_=bank[:], func=COPY, scale=win_col[:, t:t + 1])
             return y
 
-
-        w1_bf = [round_weight("w1_bf0", w1_raw[0])]
-        win_col = tile("win_col", [P, 4], F32, "w1_raw0")
-        nc.scalar.activation(out=win_col[:], in_=win_ps[:, 0:4], func=COPY)
-        yi = [y_part("yi%d" % h, w4_codes, w4_scales, h) for h in range(2)]
-        v_first = gather_words("v_first", tab_w[0], offs_sb[:])
-        v = [[v_first[:, HALF * h:HALF * (h + 1)]] for h in range(2)]
-        v[0].append(gather_words("v0_1", tab_w[1], offs_sb[:, 0:32])[:])
-        w2_codes = tile("w2_codes", [P, 2, 2 * H], U8)
-        nc.vector.tensor_copy(out=w2_codes[:].bitcast(I32).rearrange("p a (t b e) -> p a t b e", t=4, e=2),
-                              in_=w2_raw[:].bitcast(I32).rearrange("p a (b t e) -> p a t b e", t=4, e=2))
+        w1_bf = [tile("w1_bf%d" % a, [P, 4 * H], BF16) for a in range(2)]
+        yi = [y_part("yi0", w4_codes, w4_scales, 0, low, [None])]
         w3_codes = tile("w3_codes", [P, H], U32)
-        nc.vector.tensor_copy(out=w3_codes[:].bitcast(I32).rearrange("p (t b q) -> p t b q", t=4, q=4),
+        nc.gpsimd.tensor_copy(out=w3_codes[:].bitcast(I32).rearrange("p (t b q) -> p t b q", t=4, q=4),
                               in_=w3_raw[:].bitcast(I32).rearrange("p (b t q) -> p t b q", t=4, q=4))
-        v[1].append(gather_words("v1_1", tab_w[1], offs_sb[:, 32:64], "w2_raw")[:])
-        w1_q = [quantize("w1_0", w1_bf[0][:], H, "w3_raw")]
-        w1_bf.append(tile("w1_bf1", [P, 4 * H], BF16))
-        for u in range(2):
-            for t in range(4):
-                nc.scalar.activation(
-                    out=w1_bf[1][:, H * t + 256 * u:H * t + 256 * (u + 1)].rearrange("p (b q j) -> p b j q", q=4, j=4),
-                    in_=w1_last[u][:].rearrange("p j (b t q) -> p t b j q", t=4, q=4)[:, t], func=COPY)
-        w1_q.append(quantize("w1_1", w1_bf[1][:], H))
+        for i in range(3):
+            round_weight(nc.scalar.copy, w1_bf[i // 2], w1_raw[i], 16 * (i % 2))
+        yr = [y_part("yr0", w3_codes, w3_scale, 0, high, (None, "w1_raw2"))]
+        w2_codes = tile("w2_codes", [P, 2, 2 * H], U8)
+        nc.gpsimd.tensor_copy(out=w2_codes[:].bitcast(I32).rearrange("p a (t b e) -> p a t b e", t=4, e=2),
+                              in_=w2_raw[:].bitcast(I32).rearrange("p a (b t e) -> p a t b e", t=4, e=2))
+        v_first = gather_words("v_first", tab_w[0], offs_sb[:])
+        v = [[v_first[:, HALF * h:HALF * (h + 1)],
+              gather_words("v%d_1" % h, tab_w[1], offs_sb[:, 32 * h:32 * (h + 1)])[:]] for h in range(2)]
 
-        def x_times_y(prod, lhs, y, h, slots):
+        def x_times_y(prod, lhs, y, h, banks, slots=range(4)):
             for t in slots:
-                bank = psum.tile([P, HALF], F32, name="x_ps", tag="x", bufs=8 - YB)
-                for a in (1, 0):
+                bank = banks[t]
+                for a in range(2):
                     codes, scales = lhs(a, t)
                     nc.tensor.matmul_mx(out=bank[:], lhsT=codes, lhsT_scale=scales, rhs=v[h][a].bitcast(FP8X4),
                                         rhs_scale=v_scale[a][:, HALF * h:HALF * (h + 1)],
-                                        start=(a == 1), stop=(a == 0))
-                nc.vector.tensor_tensor(out=prod[:, t, :], in0=y[:, t, :], in1=bank[:], op=MULT)
+                                        start=(a == 0), stop=(a == 1))
+                nc.vector.tensor_tensor(out=prod[t], in0=y[t], in1=bank[:], op=MULT)
 
         def w2_lhs(a, t):
             return (w2_codes[:, a, 2 * P * t:2 * P * (t + 1)].bitcast(FP4X4),
@@ -191,79 +182,84 @@ def tile_list_raman_phase_traces_kernel(tc, tab_words, tab_scales, tab2_words, t
         def w1_lhs(a, t):
             return (w1_q[a][0][:, P * t:P * (t + 1)].bitcast(FP8X4), w1_q[a][1][:, P * t:P * (t + 1)])
 
-        def add_round(engine, hb, h, j0, width):
-            engine.tensor_tensor(out=hb.rearrange("p (c i t) -> p c t i", i=2, t=4),
-                                 in0=prod_r[h][:, :, j0:j0 + width].rearrange("p t (c i) -> p c t i", i=2),
-                                 in1=prod_i[h][:, :, j0:j0 + width].rearrange("p t (c i) -> p c t i", i=2),
-                                 op=ADD)
-
-        prod_i = [tile("prod_i0", [P, 4, HALF], F32), tile("prod_i1", [P, 4, HALF], F32, "w1_bf1")]
-        prod_r = [tile("prod_r%d" % h, [P, 4, HALF], F32) for h in range(2)]
-        x_times_y(prod_i[0], w2_lhs, yi[0], 0, range(4))
-        yr = [y_part("yr0", w3_codes, w3_scale, 0, "w1_last1")]
-        x_times_y(prod_i[1], w2_lhs, yi[1], 1, range(FILL))
-        yr.append(y_part("yr1", w3_codes, w3_scale, 1))
-        x_times_y(prod_r[0], w1_lhs, yr[0], 0, range(4))
-        h_rows = tile("h_rows", [P, 4, HALF], BF16)
+        late_i = tile("late_i", [P, 4, HALF], F32)
+        late_r = tile("late_r", [P, 4, HALF], F32)
+        prod_i = [[], [late_i[:, t, :] for t in range(4)]]
+        prod_r = [[tile("early_r%d" % t, [P, HALF], F32)[:] for t in range(4)], [late_r[:, t, :] for t in range(4)]]
+        prod_i[0].extend(tile("early_i%d" % t, [P, HALF], F32)[:] for t in range(3))
+        x_times_y(prod_i[0], w2_lhs, yi[0], 0, low, range(3))
+        w1_q = [quantize("w1_0", w1_bf[0][:], H)]
+        round_weight(nc.vector.tensor_copy, w1_bf[1], w1_raw[3], 16)
+        w1_q.append(quantize("w1_1", w1_bf[1][:], H))
+        prod_i[0].append(tile("early_i3", [P, HALF], F32, "w1_bf1")[:])
+        x_times_y(prod_i[0], w2_lhs, yi[0], 0, low, [3])
+        x_times_y(prod_r[0], w1_lhs, yr[0], 0, high)
+        yi.append(y_part("yi1", w4_codes, w4_scales, 1, low, ["w1_raw3"]))
+        pairs = tile("pairs", [P, 2, HALF, 2], BF16)
         for t in range(4):
-            nc.gpsimd.tensor_tensor(out=h_rows[:, t, :], in0=prod_r[0][:, t, :], in1=prod_i[0][:, t, :], op=ADD)
+            nc.gpsimd.tensor_tensor(out=pairs[:, t // 2, :, t % 2], in0=prod_r[0][t], in1=prod_i[0][t],
+                                    op=ADD)
+        x_times_y(prod_i[1], w2_lhs, yi[1], 1, high)
         w5_bf = tile("w5_bf", [P, 4 * N], BF16)
         nc.scalar.copy(out=w5_bf[:].rearrange("p (c i t) -> p c t i", i=4, t=4),
                        in_=w5_raw[:].rearrange("p t (c i) -> p c t i", i=4))
-        h_first = tile("h_first", [P, 4 * HALF], BF16, "w5_raw")
-        h_bf = []
-        for c in range(4):
-            h_bf.append(h_first[:, 4 * TAIL * c:4 * TAIL * (c + 1)])
-            nc.scalar.copy(out=h_bf[c].rearrange("p (c i t) -> p c t i", i=4, t=4),
-                           in_=h_rows[:, :, TAIL * c:TAIL * (c + 1)].rearrange("p t (c i) -> p c t i", i=4))
-        x_times_y(prod_i[1], w2_lhs, yi[1], 1, range(FILL, 4))
-        x_times_y(prod_r[1], w1_lhs, yr[1], 1, range(4))
+        yr.append(y_part("yr1", w3_codes, w3_scale, 1, low, ("w5_raw", None)))
+        h_woven = tile("h_woven", [P, 4 * HALF], BF16, "w5_raw")
+        h_first = [h_woven[:, 2 * HALF * c:2 * HALF * (c + 1)] for c in range(2)]
+        pair_words = pairs[:].rearrange("p u j e -> p u (j e)").bitcast(U32).rearrange("p u j -> p j u")
+        for c in range(2):
+            nc.scalar.copy(out=h_first[c].bitcast(U32).rearrange("p (j u) -> p j u", u=2),
+                           in_=pair_words[:, 256 * c:256 * (c + 1), :])
+        x_times_y(prod_r[1], w1_lhs, yr[1], 1, high)
 
         out_rows = out.rearrange("(i p) j -> p i j", p=P)
-        w5_codes = tile("w5_codes", [P, N], U32, "yi1")
+        w5_codes = tile("w5_codes", [P, N], U32, "yr1_1")
         w5_scales = tile("w5_scales", [P, N], U8)
         nc.vector.quantize_mx(out=w5_codes[:, 0:256].bitcast(FP8X4), scales=w5_scales[:, 0:256], in_=w5_bf[:, 0:1024])
         nc.vector.quantize_mx(out=w5_codes[:, 256:N].bitcast(FP8X4), scales=w5_scales[:, 256:N], in_=w5_bf[:, 1024:4 * N])
 
-        chunks = S // TAIL
-        pairs = []
+        def mix(dst, i, codes, scales):
+            nc.tensor.matmul_mx(out=dst, lhsT=w5_codes[:, P * i:P * (i + 1)].bitcast(FP8X4),
+                                lhsT_scale=w5_scales[:, P * i:P * (i + 1)], rhs=codes[:].bitcast(FP8X4),
+                                rhs_scale=scales[:], start=True, stop=True)
 
-        def finish(c):
-            codes, scales = quantize("h%d" % c, h_bf[c], TAIL)
-            bank = psum.tile([P, HALF], F32, name="o_ps", tag="y", bufs=YB)
-            for i in range(3):
-                nc.tensor.matmul_mx(out=bank[:, TAIL * i:TAIL * (i + 1)],
-                                    lhsT=w5_codes[:, P * i:P * (i + 1)].bitcast(FP8X4),
-                                    lhsT_scale=w5_scales[:, P * i:P * (i + 1)], rhs=codes[:].bitcast(FP8X4),
-                                    rhs_scale=scales[:], start=True, stop=True)
-            sums = bank[:, 0:3 * TAIL].rearrange("p (i j) -> p i j", i=3)
-            if c < 6:
-                if c % 2 == 0:
-                    pairs.append(tile("res%d" % c, [P, 3, 2 * TAIL], F32))
-                nc.scalar.copy(out=pairs[c // 2][:, :, TAIL * (c % 2):TAIL * (c % 2 + 1)], in_=sums)
-                if c % 2 == 1:
-                    nc.sync.dma_start(out=out_rows[:, :, TAIL * (c - 1):TAIL * (c + 1)], in_=pairs[c // 2][:])
-            else:
-                res = tile("res%d" % c, [P, 3, TAIL], F32)
-                if c == chunks - 1:
-                    nc.vector.tensor_copy(out=res[:], in_=sums)
-                else:
-                    nc.scalar.copy(out=res[:], in_=sums)
-                nc.sync.dma_start(out=out_rows[:, :, TAIL * c:TAIL * (c + 1)], in_=res[:])
+        for c in range(2):
+            codes, scales = quantize("h_first%d" % c, h_first[c], 256)
+            res = tile("res_first%d" % c, [P, 3, 256], F32)
+            mix(low[2 * c][:, 0:256], 0, codes, scales)
+            mix(low[2 * c][:, 256:512], 1, codes, scales)
+            mix(low[2 * c + 1][:, 0:256], 2, codes, scales)
+            nc.scalar.copy(out=res[:, 0:2, :], in_=low[2 * c][:].rearrange("p (i j) -> p i j", i=2))
+            nc.scalar.copy(out=res[:, 2, :], in_=low[2 * c + 1][:, 0:256])
+            nc.sync.dma_start(out=out_rows[:, :, 256 * c:256 * (c + 1)], in_=res[:])
+
+        h_late = []
 
         def add_late(c):
-            h_bf.append(tile("h_bf%d" % c, [P, 4 * TAIL], BF16)[:])
-            add_round(nc.vector, h_bf[c], 1, TAIL * (c - 4), TAIL)
+            hb = tile("h_late%d" % c, [P, 4 * TAIL], BF16)
+            h_late.append(hb)
+            nc.vector.tensor_tensor(
+                out=hb[:].rearrange("p (c i t) -> p c t i", i=2, t=4),
+                in0=late_r[:, :, TAIL * c:TAIL * (c + 1)].rearrange("p t (c i) -> p c t i", i=2),
+                in1=late_i[:, :, TAIL * c:TAIL * (c + 1)].rearrange("p t (c i) -> p c t i", i=2), op=ADD)
 
-        finish(0)
-        finish(1)
-        add_late(4)
-        finish(2)
-        add_late(5)
-        finish(3)
-        finish(4)
-        add_late(6)
-        finish(5)
-        add_late(7)
-        finish(6)
-        finish(7)
+        def finish(c):
+            codes, scales = quantize("h%d" % c, h_late[c][:], TAIL)
+            bank = high[c]
+            for i in range(3):
+                mix(bank[:, TAIL * i:TAIL * (i + 1)], i, codes, scales)
+            res = tile("res%d" % c, [P, 3, TAIL], F32)
+            nc.scalar.copy(out=res[:], in_=bank[:, 0:3 * TAIL].rearrange("p (i j) -> p i j", i=3))
+            nc.sync.dma_start(out=out_rows[:, :, HALF + TAIL * c:HALF + TAIL * (c + 1)], in_=res[:])
+
+        add_late(0)
+        for c in range(1, 4):
+            add_late(c)
+            finish(c - 1)
+        codes, scales = quantize("h3", h_late[3][:], TAIL)
+        for i, (bank, copy) in enumerate(((high[3], nc.scalar.copy), (low[3], nc.vector.tensor_copy),
+                                          (low[0], nc.scalar.copy))):
+            mix(bank[:, 0:TAIL], i, codes, scales)
+            res = tile("res_last%d" % i, [P, TAIL], F32)
+            copy(out=res[:], in_=bank[:, 0:TAIL])
+            nc.sync.dma_start(out=out_rows[:, i, S - TAIL:S], in_=res[:])

@@ -43,8 +43,8 @@ def tile_list_raman_phase_traces_kernel(tc, tab_words, tab_scales, tab2_words, t
         plane = [tile("plane0", [P, S + 2 * H], U8), tile("plane1", [P, S + 2 * H], U8)]
         win_rows = tile("win_rows", [P, P], F32)
         ident = tile("ident", [P, P], F32)
-        nc.gpsimd.memset(tab2_bytes[:].bitcast(I32), 0)
-        for zeroed in (tab_bytes, w_bytes, win_rows, ident, plane[1]):
+        nc.gpsimd.memset(tab_bytes[:].bitcast(I32), 0)
+        for zeroed in (tab2_bytes, w_bytes, win_rows, ident, plane[1]):
             nc.vector.memset(zeroed[:].bitcast(I32), 0)
         make_identity(nc, ident[:], nomemset=True)
 
@@ -70,9 +70,8 @@ def tile_list_raman_phase_traces_kernel(tc, tab_words, tab_scales, tab2_words, t
             nc.sync.dma_start(out=dst.bitcast(I32)[0:P:4, :], in_=rows.bitcast(I32).rearrange("a z c -> z a c"))
 
         nc.sync.dma_start(offs_sb[:], offs)
-        w3_raw = load_words("w3_raw", w3_words[0], H)
-        load_scale_rows(tab_bytes[:], tab_scales)
         nc.sync.dma_start(offs2_sb[:], offs2)
+        load_scale_rows(tab_bytes[:], tab_scales)
         load_tab2_scales(0)
         w4_raw = load_rows("w4_raw", w4)
         for d in range(1, 4):
@@ -86,9 +85,14 @@ def tile_list_raman_phase_traces_kernel(tc, tab_words, tab_scales, tab2_words, t
         w2_raw = tile("w2_raw", [P, 2, 2 * H], U8)
         nc.sync.dma_start(out=w2_raw[:].bitcast(I32), in_=w2_words.rearrange("a p c -> p a c").bitcast(I32))
 
-        low = [psum.tile([P, HALF], F32, name="low%d" % t) for t in range(4)]
-        high = [psum.tile([P, HALF], F32, name="high%d" % t) for t in range(4)]
-        win_ps = high[3]
+        banks = [psum.tile([P, HALF], F32, name="bank%d" % b) for b in range(8)]
+        taken = []
+
+        def next_bank():
+            taken.append(banks[len(taken) % 8])
+            return taken[-1]
+
+        win_ps = banks[0]
         nc.tensor.transpose(win_ps[:, 0:P], win_rows[:], ident[:])
 
         def round_weight(copy, dst, raw, b0):
@@ -124,6 +128,7 @@ def tile_list_raman_phase_traces_kernel(tc, tab_words, tab_scales, tab2_words, t
         for r in range(1, 4):
             nc.sync.dma_start(out=plane[0][:, 0:S + H].bitcast(I32)[r:P:32, :],
                               in_=plane[0][:, 0:S + H].bitcast(I32)[8 * r:P:32, :])
+        w3_raw = load_words("w3_raw", w3_words[0], H)
         w1_raw = [load_w1(i) for i in range(4)]
         w5_raw = tile("w5_raw", [P, 4, N], F32)
         w5_by_slot = w5.rearrange("(b t q) n -> t b q n", t=4, q=4)
@@ -138,42 +143,21 @@ def tile_list_raman_phase_traces_kernel(tc, tab_words, tab_scales, tab2_words, t
         w4_codes, w4_scales = quantize("w4", w4_bf[:], H)
         v2 = [gather_words("v2_%d" % h, tab2_w, offs2_sb[:, 32 * h:32 * (h + 1)]) for h in range(2)]
 
-        def y_part(name, codes, scales, h, banks, after):
-            rows = 4 // len(after)
-            parts = [tile("%s_%d" % (name, u), [P, rows, HALF], F32, tag) for u, tag in enumerate(after)]
-            y = [parts[t // rows][:, t % rows, :] for t in range(4)]
-            for t in range(4):
-                bank = banks[t]
-                nc.tensor.matmul_mx(out=bank[:], lhsT=codes[:, P * t:P * (t + 1)].bitcast(FP8X4),
-                                    lhsT_scale=scales[:, P * t:P * (t + 1)], rhs=v2[h][:].bitcast(FP8X4),
-                                    rhs_scale=v2_scale[:, HALF * h:HALF * (h + 1)], start=True, stop=True)
-                nc.scalar.activation(out=y[t], in_=bank[:], func=COPY, scale=win_col[:, t:t + 1])
-            return y
+        def y_slot(y, codes, scales, h, t):
+            bank = next_bank()
+            nc.tensor.matmul_mx(out=bank[:], lhsT=codes[:, P * t:P * (t + 1)].bitcast(FP8X4),
+                                lhsT_scale=scales[:, P * t:P * (t + 1)], rhs=v2[h][:].bitcast(FP8X4),
+                                rhs_scale=v2_scale[:, HALF * h:HALF * (h + 1)], start=True, stop=True)
+            nc.scalar.activation(out=y, in_=bank[:], func=COPY, scale=win_col[:, t:t + 1])
 
-        w1_bf = [tile("w1_bf%d" % a, [P, 4 * H], BF16) for a in range(2)]
-        yi = [y_part("yi0", w4_codes, w4_scales, 0, low, [None])]
-        w3_codes = tile("w3_codes", [P, H], U32)
-        nc.gpsimd.tensor_copy(out=w3_codes[:].bitcast(I32).rearrange("p (t b q) -> p t b q", t=4, q=4),
-                              in_=w3_raw[:].bitcast(I32).rearrange("p (b t q) -> p t b q", t=4, q=4))
-        for i in range(3):
-            round_weight(nc.scalar.copy, w1_bf[i // 2], w1_raw[i], 16 * (i % 2))
-        yr = [y_part("yr0", w3_codes, w3_scale, 0, high, (None, "w1_raw2"))]
-        w2_codes = tile("w2_codes", [P, 2, 2 * H], U8)
-        nc.gpsimd.tensor_copy(out=w2_codes[:].bitcast(I32).rearrange("p a (t b e) -> p a t b e", t=4, e=2),
-                              in_=w2_raw[:].bitcast(I32).rearrange("p a (b t e) -> p a t b e", t=4, e=2))
-        v_first = gather_words("v_first", tab_w[0], offs_sb[:])
-        v = [[v_first[:, HALF * h:HALF * (h + 1)],
-              gather_words("v%d_1" % h, tab_w[1], offs_sb[:, 32 * h:32 * (h + 1)])[:]] for h in range(2)]
-
-        def x_times_y(prod, lhs, y, h, banks, slots=range(4)):
-            for t in slots:
-                bank = banks[t]
-                for a in range(2):
-                    codes, scales = lhs(a, t)
-                    nc.tensor.matmul_mx(out=bank[:], lhsT=codes, lhsT_scale=scales, rhs=v[h][a].bitcast(FP8X4),
-                                        rhs_scale=v_scale[a][:, HALF * h:HALF * (h + 1)],
-                                        start=(a == 0), stop=(a == 1))
-                nc.vector.tensor_tensor(out=prod[t], in0=y[t], in1=bank[:], op=MULT)
+        def x_times_y(prod, lhs, y, h, t):
+            bank = next_bank()
+            for a in range(2):
+                codes, scales = lhs(a, t)
+                nc.tensor.matmul_mx(out=bank[:], lhsT=codes, lhsT_scale=scales, rhs=v[h][a].bitcast(FP8X4),
+                                    rhs_scale=v_scale[a][:, HALF * h:HALF * (h + 1)],
+                                    start=(a == 0), stop=(a == 1))
+            nc.vector.tensor_tensor(out=prod, in0=y, in1=bank[:], op=MULT)
 
         def w2_lhs(a, t):
             return (w2_codes[:, a, 2 * P * t:2 * P * (t + 1)].bitcast(FP4X4),
@@ -182,35 +166,61 @@ def tile_list_raman_phase_traces_kernel(tc, tab_words, tab_scales, tab2_words, t
         def w1_lhs(a, t):
             return (w1_q[a][0][:, P * t:P * (t + 1)].bitcast(FP8X4), w1_q[a][1][:, P * t:P * (t + 1)])
 
+        yi = [tile("yi%d" % h, [P, 4, HALF], F32) for h in range(2)]
+        for n in range(7):
+            y_slot(yi[n // 4][:, n % 4, :], w4_codes, w4_scales, n // 4, n % 4)
+        v_first = gather_words("v_first", tab_w[0], offs_sb[:])
+        v = [[v_first[:, HALF * h:HALF * (h + 1)],
+              gather_words("v%d_1" % h, tab_w[1], offs_sb[:, 32 * h:32 * (h + 1)])[:]] for h in range(2)]
+        w2_codes = tile("w2_codes", [P, 2, 2 * H], U8)
+        nc.gpsimd.tensor_copy(out=w2_codes[:].bitcast(I32).rearrange("p a (t b e) -> p a t b e", t=4, e=2),
+                              in_=w2_raw[:].bitcast(I32).rearrange("p a (b t e) -> p a t b e", t=4, e=2))
+        w3_codes = tile("w3_codes", [P, H], U32, "tab_w1")
+        nc.gpsimd.tensor_copy(out=w3_codes[:].bitcast(I32).rearrange("p (t b q) -> p t b q", t=4, q=4),
+                              in_=w3_raw[:].bitcast(I32).rearrange("p (b t q) -> p t b q", t=4, q=4))
+
+        early_i = [tile("early_i%d" % t, [P, HALF], F32) for t in range(3)]
+        early_r = [tile("early_r%d" % t, [P, HALF], F32) for t in range(4)]
+        for t in range(3):
+            x_times_y(early_i[t][:], w2_lhs, yi[0][:, t, :], 0, t)
+        w1_bf = [tile("w1_bf%d" % a, [P, 4 * H], BF16) for a in range(2)]
+        for i in range(3):
+            round_weight(nc.scalar.copy, w1_bf[i // 2], w1_raw[i], 16 * (i % 2))
         late_i = tile("late_i", [P, 4, HALF], F32)
         late_r = tile("late_r", [P, 4, HALF], F32)
-        prod_i = [[], [late_i[:, t, :] for t in range(4)]]
-        prod_r = [[tile("early_r%d" % t, [P, HALF], F32)[:] for t in range(4)], [late_r[:, t, :] for t in range(4)]]
-        prod_i[0].extend(tile("early_i%d" % t, [P, HALF], F32)[:] for t in range(3))
-        x_times_y(prod_i[0], w2_lhs, yi[0], 0, low, range(3))
+        x_times_y(late_i[:, 0, :], w2_lhs, yi[1][:, 0, :], 1, 0)
         w1_q = [quantize("w1_0", w1_bf[0][:], H)]
         round_weight(nc.vector.tensor_copy, w1_bf[1], w1_raw[3], 16)
         w1_q.append(quantize("w1_1", w1_bf[1][:], H))
-        prod_i[0].append(tile("early_i3", [P, HALF], F32, "w1_bf1")[:])
-        x_times_y(prod_i[0], w2_lhs, yi[0], 0, low, [3])
-        x_times_y(prod_r[0], w1_lhs, yr[0], 0, high)
-        yi.append(y_part("yi1", w4_codes, w4_scales, 1, low, ["w1_raw3"]))
+        early_i.append(tile("early_i3", [P, HALF], F32, "w1_raw3"))
+        x_times_y(early_i[3][:], w2_lhs, yi[0][:, 3, :], 0, 3)
+        yr = [tile("yr0", [P, 4, HALF], F32, "w1_raw2")]
+        for t in range(4):
+            y_slot(yr[0][:, t, :], w3_codes, w3_scale, 0, t)
         pairs = tile("pairs", [P, 2, HALF, 2], BF16)
         for t in range(4):
-            nc.gpsimd.tensor_tensor(out=pairs[:, t // 2, :, t % 2], in0=prod_r[0][t], in1=prod_i[0][t],
-                                    op=ADD)
-        x_times_y(prod_i[1], w2_lhs, yi[1], 1, high)
+            x_times_y(early_r[t][:], w1_lhs, yr[0][:, t, :], 0, t)
+            nc.gpsimd.tensor_tensor(out=pairs[:, t // 2, :, t % 2], in0=early_r[t][:], in1=early_i[t][:], op=ADD)
+        y_slot(yi[1][:, 3, :], w4_codes, w4_scales, 1, 3)
+        yr_late = [tile("yr1_%d" % t, [P, HALF], F32) for t in range(3)]
+        for t in range(3):
+            y_slot(yr_late[t][:], w3_codes, w3_scale, 1, t)
         w5_bf = tile("w5_bf", [P, 4 * N], BF16)
         nc.scalar.copy(out=w5_bf[:].rearrange("p (c i t) -> p c t i", i=4, t=4),
                        in_=w5_raw[:].rearrange("p t (c i) -> p c t i", i=4))
-        yr.append(y_part("yr1", w3_codes, w3_scale, 1, low, ("w5_raw", None)))
-        h_woven = tile("h_woven", [P, 4 * HALF], BF16, "w5_raw")
-        h_first = [h_woven[:, 2 * HALF * c:2 * HALF * (c + 1)] for c in range(2)]
+        yr_late.append(tile("yr1_3", [P, HALF], F32, "w5_raw"))
+        y_slot(yr_late[3][:], w3_codes, w3_scale, 1, 3)
+        for t in range(1, 4):
+            x_times_y(late_i[:, t, :], w2_lhs, yi[1][:, t, :], 1, t)
+        for t in range(4):
+            x_times_y(late_r[:, t, :], w1_lhs, yr_late[t][:], 1, t)
+
+        h_woven = tile("h_woven", [P, 4 * HALF], BF16, "yr1_2")
+        h_bf = [h_woven[:, 4 * TAIL * c:4 * TAIL * (c + 1)] for c in range(4)]
         pair_words = pairs[:].rearrange("p u j e -> p u (j e)").bitcast(U32).rearrange("p u j -> p j u")
-        for c in range(2):
-            nc.scalar.copy(out=h_first[c].bitcast(U32).rearrange("p (j u) -> p j u", u=2),
-                           in_=pair_words[:, 256 * c:256 * (c + 1), :])
-        x_times_y(prod_r[1], w1_lhs, yr[1], 1, high)
+        for c in range(4):
+            nc.scalar.copy(out=h_bf[c].bitcast(U32).rearrange("p (j u) -> p j u", u=2),
+                           in_=pair_words[:, TAIL * c:TAIL * (c + 1), :])
 
         out_rows = out.rearrange("(i p) j -> p i j", p=P)
         w5_codes = tile("w5_codes", [P, N], U32, "yr1_1")
@@ -223,43 +233,38 @@ def tile_list_raman_phase_traces_kernel(tc, tab_words, tab_scales, tab2_words, t
                                 lhsT_scale=w5_scales[:, P * i:P * (i + 1)], rhs=codes[:].bitcast(FP8X4),
                                 rhs_scale=scales[:], start=True, stop=True)
 
-        for c in range(2):
-            codes, scales = quantize("h_first%d" % c, h_first[c], 256)
-            res = tile("res_first%d" % c, [P, 3, 256], F32)
-            mix(low[2 * c][:, 0:256], 0, codes, scales)
-            mix(low[2 * c][:, 256:512], 1, codes, scales)
-            mix(low[2 * c + 1][:, 0:256], 2, codes, scales)
-            nc.scalar.copy(out=res[:, 0:2, :], in_=low[2 * c][:].rearrange("p (i j) -> p i j", i=2))
-            nc.scalar.copy(out=res[:, 2, :], in_=low[2 * c + 1][:, 0:256])
-            nc.sync.dma_start(out=out_rows[:, :, 256 * c:256 * (c + 1)], in_=res[:])
-
-        h_late = []
-
         def add_late(c):
             hb = tile("h_late%d" % c, [P, 4 * TAIL], BF16)
-            h_late.append(hb)
-            nc.vector.tensor_tensor(
-                out=hb[:].rearrange("p (c i t) -> p c t i", i=2, t=4),
-                in0=late_r[:, :, TAIL * c:TAIL * (c + 1)].rearrange("p t (c i) -> p c t i", i=2),
-                in1=late_i[:, :, TAIL * c:TAIL * (c + 1)].rearrange("p t (c i) -> p c t i", i=2), op=ADD)
+            h_bf.append(hb[:])
+            cols = slice(TAIL * c - HALF, TAIL * (c + 1) - HALF)
+            nc.vector.tensor_tensor(out=hb[:].rearrange("p (c i t) -> p c t i", i=2, t=4),
+                                    in0=late_r[:, :, cols].rearrange("p t (c i) -> p c t i", i=2),
+                                    in1=late_i[:, :, cols].rearrange("p t (c i) -> p c t i", i=2), op=ADD)
 
         def finish(c):
-            codes, scales = quantize("h%d" % c, h_late[c][:], TAIL)
-            bank = high[c]
+            codes, scales = quantize("h%d" % c, h_bf[c], TAIL)
+            bank = next_bank()
             for i in range(3):
                 mix(bank[:, TAIL * i:TAIL * (i + 1)], i, codes, scales)
             res = tile("res%d" % c, [P, 3, TAIL], F32)
             nc.scalar.copy(out=res[:], in_=bank[:, 0:3 * TAIL].rearrange("p (i j) -> p i j", i=3))
-            nc.sync.dma_start(out=out_rows[:, :, HALF + TAIL * c:HALF + TAIL * (c + 1)], in_=res[:])
+            nc.sync.dma_start(out=out_rows[:, :, TAIL * c:TAIL * (c + 1)], in_=res[:])
 
-        add_late(0)
-        for c in range(1, 4):
-            add_late(c)
-            finish(c - 1)
-        codes, scales = quantize("h3", h_late[3][:], TAIL)
-        for i, (bank, copy) in enumerate(((high[3], nc.scalar.copy), (low[3], nc.vector.tensor_copy),
-                                          (low[0], nc.scalar.copy))):
+        finish(0)
+        finish(1)
+        add_late(4)
+        finish(2)
+        add_late(5)
+        finish(3)
+        finish(4)
+        add_late(6)
+        finish(5)
+        add_late(7)
+        finish(6)
+        codes, scales = quantize("h7", h_bf[7], TAIL)
+        for i, copy in enumerate((nc.vector.tensor_copy, nc.vector.tensor_copy, nc.scalar.copy)):
+            bank = next_bank()
             mix(bank[:, 0:TAIL], i, codes, scales)
-            res = tile("res_last%d" % i, [P, TAIL], F32)
-            copy(out=res[:], in_=bank[:, 0:TAIL])
-            nc.sync.dma_start(out=out_rows[:, i, S - TAIL:S], in_=res[:])
+            last = tile("last%d" % i, [P, TAIL], F32)
+            copy(out=last[:], in_=bank[:, 0:TAIL])
+            nc.sync.dma_start(out=out_rows[:, i, S - TAIL:S], in_=last[:])

@@ -21,6 +21,7 @@ COPY = mybir.ActivationFunctionType.Copy
 P = 128
 HALF = 512
 TAIL = 128
+WOVEN = 3
 
 
 def tile_list_raman_phase_traces_kernel(tc, tab_words, tab_scales, tab2_words, tab2_scales, offs, offs2,
@@ -40,11 +41,11 @@ def tile_list_raman_phase_traces_kernel(tc, tab_words, tab_scales, tab2_words, t
         tab_bytes = tile("tab_bytes", [P, T], U8)
         tab2_bytes = tile("tab2_bytes", [P, T], U8)
         w_bytes = tile("w_bytes", [P, 2 * H], U8)
-        plane = [tile("plane0", [P, S + 2 * H], U8), tile("plane1", [P, S + 2 * H], U8)]
+        plane = [tile("plane0", [P, 2 * H + S], U8), tile("plane1", [P, H + S], U8)]
         win_rows = tile("win_rows", [P, P], F32)
         ident = tile("ident", [P, P], F32)
         nc.gpsimd.memset(tab_bytes[:].bitcast(I32), 0)
-        for zeroed in (tab2_bytes, w_bytes, win_rows, ident, plane[1]):
+        for zeroed in (tab2_bytes, win_rows, w_bytes, ident, plane[1]):
             nc.vector.memset(zeroed[:].bitcast(I32), 0)
         make_identity(nc, ident[:], nomemset=True)
 
@@ -58,47 +59,38 @@ def tile_list_raman_phase_traces_kernel(tc, tab_words, tab_scales, tab2_words, t
             nc.sync.dma_start(out=t[:], in_=rows.rearrange("(p j) c -> p j c", j=4))
             return t
 
-        def load_w1(i):
-            a, u = divmod(i, 2)
-            return load_rows("w1_raw%d" % i, w1[512 * a:512 * (a + 1), 256 * u:256 * (u + 1)])
-
-        def load_tab2_scales(d):
-            nc.sync.dma_start(out=tab2_bytes[:].bitcast(I32)[32 * d:32 * d + 4, :],
-                              in_=tab2_scales[0, 4 * d:4 * d + 4, :].bitcast(I32))
-
         def load_scale_rows(dst, rows):
             nc.sync.dma_start(out=dst.bitcast(I32)[0:P:4, :], in_=rows.bitcast(I32).rearrange("a z c -> z a c"))
 
         nc.sync.dma_start(offs_sb[:], offs)
         nc.sync.dma_start(offs2_sb[:], offs2)
         load_scale_rows(tab_bytes[:], tab_scales)
-        load_tab2_scales(0)
         w4_raw = load_rows("w4_raw", w4)
-        for d in range(1, 4):
-            load_tab2_scales(d)
-        load_scale_rows(w_bytes[:, 0:H], w2_scales)
-        nc.sync.dma_start(out=w_bytes[:, H:2 * H].bitcast(I32)[4:P:8, :], in_=w3_scales[0].bitcast(I32))
+        for r in range(4):
+            nc.sync.dma_start(out=tab2_bytes[:].bitcast(I32)[r:P:32, :], in_=tab2_scales[0, r:16:4, :].bitcast(I32))
         nc.sync.dma_start(out=win_rows[0:4, :].rearrange("t (b q) -> t b q", q=4),
                           in_=win.rearrange("(b t q) -> t b q", t=4, q=4))
+        load_scale_rows(w_bytes[:, H:2 * H], w2_scales)
         tab2_w = load_words("tab2_w", tab2_words[0], T)
+        nc.sync.dma_start(out=w_bytes[:, 0:H].bitcast(I32)[0:P:8, :], in_=w3_scales[0].bitcast(I32))
         tab_w = [load_words("tab_w0", tab_words[0], T)]
         w2_raw = tile("w2_raw", [P, 2, 2 * H], U8)
         nc.sync.dma_start(out=w2_raw[:].bitcast(I32), in_=w2_words.rearrange("a p c -> p a c").bitcast(I32))
+        w3_raw = load_words("w3_raw", w3_words[0], H)
 
         banks = [psum.tile([P, HALF], F32, name="bank%d" % b) for b in range(8)]
         taken = []
 
         def next_bank():
-            taken.append(banks[len(taken) % 8])
+            taken.append(banks[(3, 0, 1, 6, 2, 7, 4, 5)[len(taken) % 8]])
             return taken[-1]
 
         win_ps = banks[0]
         nc.tensor.transpose(win_ps[:, 0:P], win_rows[:], ident[:])
 
-        def round_weight(copy, dst, raw, b0):
-            blocks = raw.shape[2] // 16
-            copy(out=dst[:].rearrange("p (t b q j) -> p t b j q", t=4, q=4, j=4)[:, :, b0:b0 + blocks],
-                 in_=raw[:].rearrange("p j (b t q) -> p t b j q", t=4, q=4))
+        def round_weight(copy, dst, raw, slots):
+            copy(out=dst.rearrange("p (t b q j) -> p t b j q", b=32, q=4, j=4),
+                 in_=raw[:].rearrange("p j (b t q) -> p t b j q", t=4, q=4)[:, slots])
 
         def quantize(name, src, width, after=None):
             codes = tile(name + "_codes", [P, width], U32, after)
@@ -112,51 +104,49 @@ def tile_list_raman_phase_traces_kernel(tc, tab_words, tab_scales, tab2_words, t
             return t
 
         w4_bf = tile("w4_bf", [P, 4 * H], BF16)
-        round_weight(nc.scalar.copy, w4_bf, w4_raw, 0)
+        round_weight(nc.scalar.copy, w4_bf[:], w4_raw, slice(0, 4))
 
         picked = tile("picked", [P, S], U8)
         nc.vector.tensor_copy(picked[:], tab_bytes[:].indirect(offs_sb[:]))
-        nc.vector.tensor_copy(out=plane[0][:, 0:S].bitcast(I32), in_=picked[:].bitcast(I32))
-        nc.gpsimd.tensor_copy(out=plane[0][:, S:S + 2 * H].bitcast(I32).rearrange("p (s t b) -> p s t b", s=2, t=4),
-                              in_=w_bytes[:].bitcast(I32).rearrange("p (s b t) -> p s t b", s=2, t=4))
+        nc.vector.tensor_copy(out=plane[0][:, 2 * H:].bitcast(I32), in_=picked[:].bitcast(I32))
         v2_scale = tile("v2_scale", [P, S], U8)
         nc.vector.tensor_copy(v2_scale[:], tab2_bytes[:].indirect(offs2_sb[:]))
+        nc.gpsimd.tensor_copy(out=plane[0][:, 0:2 * H].bitcast(I32).rearrange("p (s t b) -> p s t b", s=2, t=4),
+                              in_=w_bytes[:].bitcast(I32).rearrange("p (s b t) -> p s t b", s=2, t=4))
+        for r in range(1, 4):
+            nc.sync.dma_start(out=plane[0][:].bitcast(I32)[r:P:32, :], in_=plane[0][:].bitcast(I32)[8 * r:P:32, :])
+        tab_w.append(load_words("tab_w1", tab_words[1], T))
         for r in range(4):
             nc.sync.dma_start(out=plane[1][:].bitcast(I32)[r:P:32, :],
-                              in_=plane[0][:].bitcast(I32)[8 * r + 4:P:32, :])
-        tab_w.append(load_words("tab_w1", tab_words[1], T))
-        for r in range(1, 4):
-            nc.sync.dma_start(out=plane[0][:, 0:S + H].bitcast(I32)[r:P:32, :],
-                              in_=plane[0][:, 0:S + H].bitcast(I32)[8 * r:P:32, :])
-        w3_raw = load_words("w3_raw", w3_words[0], H)
-        w1_raw = [load_w1(i) for i in range(4)]
+                              in_=plane[0][:, H:].bitcast(I32)[8 * r + 4:P:32, :])
+        w1_raw = [load_rows("w1_raw%d" % a, w1[512 * a:512 * (a + 1), :]) for a in range(2)]
         w5_raw = tile("w5_raw", [P, 4, N], F32)
         w5_by_slot = w5.rearrange("(b t q) n -> t b q n", t=4, q=4)
         for t in range(4):
             nc.sync.dma_start(out=w5_raw[:, t, :], in_=w5_by_slot[t])
-        v_scale = [plane[a][:, 0:S] for a in range(2)]
-        w2_scale = [plane[a][:, S:S + H] for a in range(2)]
-        w3_scale = plane[1][:, S + H:S + 2 * H]
+        w3_scale = plane[0][:, 0:H]
+        w2_scale = [plane[0][:, H:2 * H], plane[1][:, 0:H]]
+        v_scale = [plane[0][:, 2 * H:], plane[1][:, H:]]
 
         win_col = tile("win_col", [P, 4], F32)
         nc.scalar.copy(out=win_col[:], in_=win_ps[:, 0:4])
-        w4_codes, w4_scales = quantize("w4", w4_bf[:], H)
+        w4_codes, w4_scales = quantize("w4", w4_bf[:], H, "tab2_bytes")
         v2 = [gather_words("v2_%d" % h, tab2_w, offs2_sb[:, 32 * h:32 * (h + 1)]) for h in range(2)]
 
-        def y_slot(y, codes, scales, h, t):
-            bank = next_bank()
+        def y_slot(y, codes, scales, h, t, b):
+            bank = banks[b]
             nc.tensor.matmul_mx(out=bank[:], lhsT=codes[:, P * t:P * (t + 1)].bitcast(FP8X4),
                                 lhsT_scale=scales[:, P * t:P * (t + 1)], rhs=v2[h][:].bitcast(FP8X4),
                                 rhs_scale=v2_scale[:, HALF * h:HALF * (h + 1)], start=True, stop=True)
             nc.scalar.activation(out=y, in_=bank[:], func=COPY, scale=win_col[:, t:t + 1])
 
-        def x_times_y(prod, lhs, y, h, t):
-            bank = next_bank()
-            for a in range(2):
+        def x_times_y(prod, lhs, y, h, t, b):
+            bank = banks[b]
+            for a in (1, 0):
                 codes, scales = lhs(a, t)
                 nc.tensor.matmul_mx(out=bank[:], lhsT=codes, lhsT_scale=scales, rhs=v[h][a].bitcast(FP8X4),
                                     rhs_scale=v_scale[a][:, HALF * h:HALF * (h + 1)],
-                                    start=(a == 0), stop=(a == 1))
+                                    start=(a == 1), stop=(a == 0))
             nc.vector.tensor_tensor(out=prod, in0=y, in1=bank[:], op=MULT)
 
         def w2_lhs(a, t):
@@ -164,66 +154,71 @@ def tile_list_raman_phase_traces_kernel(tc, tab_words, tab_scales, tab2_words, t
                     w2_scale[a][:, P * t:P * (t + 1)])
 
         def w1_lhs(a, t):
-            return (w1_q[a][0][:, P * t:P * (t + 1)].bitcast(FP8X4), w1_q[a][1][:, P * t:P * (t + 1)])
+            codes, scales = w1_q[t // 2]
+            cols = slice(P * (2 * a + t % 2), P * (2 * a + t % 2 + 1))
+            return codes[:, cols].bitcast(FP8X4), scales[:, cols]
 
         yi = [tile("yi%d" % h, [P, 4, HALF], F32) for h in range(2)]
-        for n in range(7):
-            y_slot(yi[n // 4][:, n % 4, :], w4_codes, w4_scales, n // 4, n % 4)
+        for n in range(8):
+            y_slot(yi[n // 4][:, n % 4, :], w4_codes, w4_scales, n // 4, n % 4, n)
         v_first = gather_words("v_first", tab_w[0], offs_sb[:])
+        w2_codes = tile("w2_codes", [P, 2, 2 * H], U8)
+        nc.vector.tensor_copy(out=w2_codes[:].bitcast(I32).rearrange("p a (t b e) -> p a t b e", t=4, e=2),
+                              in_=w2_raw[:].bitcast(I32).rearrange("p a (b t e) -> p a t b e", t=4, e=2))
+        w3_codes = tile("w3_codes", [P, H], U32)
+        nc.vector.tensor_copy(out=w3_codes[:].bitcast(I32).rearrange("p (t b q) -> p t b q", t=4, q=4),
+                              in_=w3_raw[:].bitcast(I32).rearrange("p (b t q) -> p t b q", t=4, q=4))
+        yr_early = [tile("yr0_0", [P, 2, HALF], F32)]
+        for t in range(2):
+            y_slot(yr_early[0][:, t, :], w3_codes, w3_scale, 0, t, t)
         v = [[v_first[:, HALF * h:HALF * (h + 1)],
               gather_words("v%d_1" % h, tab_w[1], offs_sb[:, 32 * h:32 * (h + 1)])[:]] for h in range(2)]
-        w2_codes = tile("w2_codes", [P, 2, 2 * H], U8)
-        nc.gpsimd.tensor_copy(out=w2_codes[:].bitcast(I32).rearrange("p a (t b e) -> p a t b e", t=4, e=2),
-                              in_=w2_raw[:].bitcast(I32).rearrange("p a (b t e) -> p a t b e", t=4, e=2))
-        w3_codes = tile("w3_codes", [P, H], U32, "tab_w1")
-        nc.gpsimd.tensor_copy(out=w3_codes[:].bitcast(I32).rearrange("p (t b q) -> p t b q", t=4, q=4),
-                              in_=w3_raw[:].bitcast(I32).rearrange("p (b t q) -> p t b q", t=4, q=4))
 
-        early_i = [tile("early_i%d" % t, [P, HALF], F32) for t in range(3)]
-        early_r = [tile("early_r%d" % t, [P, HALF], F32) for t in range(4)]
-        for t in range(3):
-            x_times_y(early_i[t][:], w2_lhs, yi[0][:, t, :], 0, t)
-        w1_bf = [tile("w1_bf%d" % a, [P, 4 * H], BF16) for a in range(2)]
-        for i in range(3):
-            round_weight(nc.scalar.copy, w1_bf[i // 2], w1_raw[i], 16 * (i % 2))
-        late_i = tile("late_i", [P, 4, HALF], F32)
+        early_i = tile("early_i", [P, 4, HALF], F32)
+        early_r = tile("early_r", [P, 4, HALF], F32)
+        for t in range(4):
+            x_times_y(early_i[:, t, :], w2_lhs, yi[0][:, t, :], 0, t, 2 + t)
+        w1_bf = [tile("w1_bf%d" % u, [P, 2, 2 * H], BF16) for u in range(2)]
+        for u in range(2):
+            round_weight(nc.scalar.copy, w1_bf[u][:, 0, :], w1_raw[0], slice(2 * u, 2 * u + 2))
+        round_weight(nc.vector.tensor_copy, w1_bf[0][:, 1, :], w1_raw[1], slice(0, 2))
+        round_weight(nc.scalar.copy, w1_bf[1][:, 1, :], w1_raw[1], slice(2, 4))
+        w1_q = [quantize("w1_0", w1_bf[0][:].rearrange("p a c -> p (a c)"), H)]
+        late_i = tile("late_i", [P, 4, HALF], F32, "w1_bf0")
         late_r = tile("late_r", [P, 4, HALF], F32)
-        x_times_y(late_i[:, 0, :], w2_lhs, yi[1][:, 0, :], 1, 0)
-        w1_q = [quantize("w1_0", w1_bf[0][:], H)]
-        round_weight(nc.vector.tensor_copy, w1_bf[1], w1_raw[3], 16)
-        w1_q.append(quantize("w1_1", w1_bf[1][:], H))
-        early_i.append(tile("early_i3", [P, HALF], F32, "w1_raw3"))
-        x_times_y(early_i[3][:], w2_lhs, yi[0][:, 3, :], 0, 3)
-        yr = [tile("yr0", [P, 4, HALF], F32, "w1_raw2")]
+        x_times_y(late_i[:, 0, :], w2_lhs, yi[1][:, 0, :], 1, 0, 6)
+        w1_q.append(quantize("w1_1", w1_bf[1][:].rearrange("p a c -> p (a c)"), H))
+        yr_early.append(tile("yr0_1", [P, 2, HALF], F32, "w1_raw1"))
+        for t in range(2, 4):
+            y_slot(yr_early[1][:, t - 2, :], w3_codes, w3_scale, 0, t, t)
+        pairs = tile("pairs", [P, 2, WOVEN * TAIL, 2], BF16)
         for t in range(4):
-            y_slot(yr[0][:, t, :], w3_codes, w3_scale, 0, t)
-        pairs = tile("pairs", [P, 2, HALF, 2], BF16)
-        for t in range(4):
-            x_times_y(early_r[t][:], w1_lhs, yr[0][:, t, :], 0, t)
-            nc.gpsimd.tensor_tensor(out=pairs[:, t // 2, :, t % 2], in0=early_r[t][:], in1=early_i[t][:], op=ADD)
-        y_slot(yi[1][:, 3, :], w4_codes, w4_scales, 1, 3)
-        yr_late = [tile("yr1_%d" % t, [P, HALF], F32) for t in range(3)]
-        for t in range(3):
-            y_slot(yr_late[t][:], w3_codes, w3_scale, 1, t)
+            x_times_y(early_r[:, t, :], w1_lhs, yr_early[t // 2][:, t % 2, :], 0, t, (0, 1, 6, 2)[t])
+            nc.gpsimd.tensor_tensor(out=pairs[:, t // 2, :, t % 2], in0=early_r[:, t, 0:WOVEN * TAIL],
+                                    in1=early_i[:, t, 0:WOVEN * TAIL], op=ADD)
+        for t in range(1, 4):
+            x_times_y(late_i[:, t, :], w2_lhs, yi[1][:, t, :], 1, t, (6, 7, 4, 5)[t])
         w5_bf = tile("w5_bf", [P, 4 * N], BF16)
         nc.scalar.copy(out=w5_bf[:].rearrange("p (c i t) -> p c t i", i=4, t=4),
                        in_=w5_raw[:].rearrange("p t (c i) -> p c t i", i=4))
-        yr_late.append(tile("yr1_3", [P, HALF], F32, "w5_raw"))
-        y_slot(yr_late[3][:], w3_codes, w3_scale, 1, 3)
-        for t in range(1, 4):
-            x_times_y(late_i[:, t, :], w2_lhs, yi[1][:, t, :], 1, t)
+        yr_late = [tile("yr1_%d" % t, [P, HALF], F32, "w5_raw" if t == 0 else None) for t in range(4)]
         for t in range(4):
-            x_times_y(late_r[:, t, :], w1_lhs, yr_late[t][:], 1, t)
+            y_slot(yr_late[t][:], w3_codes, w3_scale, 1, t, (3, 0, 1, 6)[t])
+        def late_product(t):
+            x_times_y(late_r[:, t, :], w1_lhs, yr_late[t][:], 1, t, (2, 7, 4, 5)[t])
 
-        h_woven = tile("h_woven", [P, 4 * HALF], BF16, "yr1_2")
-        h_bf = [h_woven[:, 4 * TAIL * c:4 * TAIL * (c + 1)] for c in range(4)]
+        for t in range(2):
+            late_product(t)
+
+        h_woven = tile("h_woven", [P, 4 * WOVEN * TAIL], BF16, "w3_codes")
+        h_bf = [h_woven[:, 4 * TAIL * c:4 * TAIL * (c + 1)] for c in range(WOVEN)]
         pair_words = pairs[:].rearrange("p u j e -> p u (j e)").bitcast(U32).rearrange("p u j -> p j u")
-        for c in range(4):
+        for c in range(WOVEN):
             nc.scalar.copy(out=h_bf[c].bitcast(U32).rearrange("p (j u) -> p j u", u=2),
                            in_=pair_words[:, TAIL * c:TAIL * (c + 1), :])
 
         out_rows = out.rearrange("(i p) j -> p i j", p=P)
-        w5_codes = tile("w5_codes", [P, N], U32, "yr1_1")
+        w5_codes = tile("w5_codes", [P, N], U32, "w5_raw")
         w5_scales = tile("w5_scales", [P, N], U8)
         nc.vector.quantize_mx(out=w5_codes[:, 0:256].bitcast(FP8X4), scales=w5_scales[:, 0:256], in_=w5_bf[:, 0:1024])
         nc.vector.quantize_mx(out=w5_codes[:, 256:N].bitcast(FP8X4), scales=w5_scales[:, 256:N], in_=w5_bf[:, 1024:4 * N])
@@ -234,33 +229,40 @@ def tile_list_raman_phase_traces_kernel(tc, tab_words, tab_scales, tab2_words, t
                                 rhs_scale=scales[:], start=True, stop=True)
 
         def add_late(c):
-            hb = tile("h_late%d" % c, [P, 4 * TAIL], BF16)
+            hb = tile("h_late%d" % c, [P, 4 * TAIL], BF16, "yr1_2" if c == WOVEN else None)
             h_bf.append(hb[:])
-            cols = slice(TAIL * c - HALF, TAIL * (c + 1) - HALF)
+            real, imag = (early_r, early_i) if c < 4 else (late_r, late_i)
+            cols = slice(TAIL * (c % 4), TAIL * (c % 4 + 1))
             nc.vector.tensor_tensor(out=hb[:].rearrange("p (c i t) -> p c t i", i=2, t=4),
-                                    in0=late_r[:, :, cols].rearrange("p t (c i) -> p c t i", i=2),
-                                    in1=late_i[:, :, cols].rearrange("p t (c i) -> p c t i", i=2), op=ADD)
+                                    in0=real[:, :, cols].rearrange("p t (c i) -> p c t i", i=2),
+                                    in1=imag[:, :, cols].rearrange("p t (c i) -> p c t i", i=2), op=ADD)
+
+        stores = [[0], [1, 2], [3], [4], [5], [6]]
+        res = {}
+        for group in stores:
+            held = tile("res%d" % group[0], [P, 3, TAIL * len(group)], F32)
+            for c in group:
+                res[c] = (held, group)
 
         def finish(c):
             codes, scales = quantize("h%d" % c, h_bf[c], TAIL)
             bank = next_bank()
             for i in range(3):
                 mix(bank[:, TAIL * i:TAIL * (i + 1)], i, codes, scales)
-            res = tile("res%d" % c, [P, 3, TAIL], F32)
-            nc.scalar.copy(out=res[:], in_=bank[:, 0:3 * TAIL].rearrange("p (i j) -> p i j", i=3))
-            nc.sync.dma_start(out=out_rows[:, :, TAIL * c:TAIL * (c + 1)], in_=res[:])
+            held, group = res[c]
+            nc.scalar.copy(out=held[:, :, TAIL * (c - group[0]):TAIL * (c - group[0] + 1)],
+                           in_=bank[:, 0:3 * TAIL].rearrange("p (i j) -> p i j", i=3))
+            if c == group[-1]:
+                nc.sync.dma_start(out=out_rows[:, :, TAIL * group[0]:TAIL * (c + 1)], in_=held[:])
 
-        finish(0)
-        finish(1)
-        add_late(4)
-        finish(2)
-        add_late(5)
-        finish(3)
-        finish(4)
-        add_late(6)
-        finish(5)
-        add_late(7)
-        finish(6)
+        late_product(2)
+        for c in range(WOVEN):
+            finish(c)
+        late_product(3)
+        add_late(WOVEN)
+        for c in range(WOVEN + 1, 8):
+            add_late(c)
+            finish(c - 1)
         codes, scales = quantize("h7", h_bf[7], TAIL)
         for i, copy in enumerate((nc.vector.tensor_copy, nc.vector.tensor_copy, nc.scalar.copy)):
             bank = next_bank()

@@ -82,7 +82,7 @@ def tile_list_raman_phase_traces_kernel(tc, tab_words, tab_scales, tab2_words, t
         taken = []
 
         def next_bank():
-            taken.append(banks[(3, 0, 1, 6, 2, 7, 4, 5)[len(taken) % 8]])
+            taken.append(banks[(6, 0, 1, 2, 3, 7, 4, 5)[len(taken) % 8]])
             return taken[-1]
 
         win_ps = banks[0]
@@ -158,9 +158,9 @@ def tile_list_raman_phase_traces_kernel(tc, tab_words, tab_scales, tab2_words, t
             cols = slice(P * (2 * a + t % 2), P * (2 * a + t % 2 + 1))
             return codes[:, cols].bitcast(FP8X4), scales[:, cols]
 
-        yi = [tile("yi%d" % h, [P, 4, HALF], F32) for h in range(2)]
+        yi = [tile("yi%d" % n, [P, HALF], F32) for n in range(8)]
         for n in range(8):
-            y_slot(yi[n // 4][:, n % 4, :], w4_codes, w4_scales, n // 4, n % 4, n)
+            y_slot(yi[n][:], w4_codes, w4_scales, n // 4, n % 4, n)
         v_first = gather_words("v_first", tab_w[0], offs_sb[:])
         w2_codes = tile("w2_codes", [P, 2, 2 * H], U8)
         nc.vector.tensor_copy(out=w2_codes[:].bitcast(I32).rearrange("p a (t b e) -> p a t b e", t=4, e=2),
@@ -177,35 +177,42 @@ def tile_list_raman_phase_traces_kernel(tc, tab_words, tab_scales, tab2_words, t
         early_i = tile("early_i", [P, 4, HALF], F32)
         early_r = tile("early_r", [P, 4, HALF], F32)
         for t in range(4):
-            x_times_y(early_i[:, t, :], w2_lhs, yi[0][:, t, :], 0, t, 2 + t)
+            x_times_y(early_i[:, t, :], w2_lhs, yi[t][:], 0, t, 2 + t)
         w1_bf = [tile("w1_bf%d" % u, [P, 2, 2 * H], BF16) for u in range(2)]
         for u in range(2):
             round_weight(nc.scalar.copy, w1_bf[u][:, 0, :], w1_raw[0], slice(2 * u, 2 * u + 2))
-        round_weight(nc.vector.tensor_copy, w1_bf[0][:, 1, :], w1_raw[1], slice(0, 2))
-        round_weight(nc.scalar.copy, w1_bf[1][:, 1, :], w1_raw[1], slice(2, 4))
-        w1_q = [quantize("w1_0", w1_bf[0][:].rearrange("p a c -> p (a c)"), H)]
+        for u in range(2):
+            round_weight(nc.vector.tensor_copy, w1_bf[u][:, 1, :], w1_raw[1], slice(2 * u, 2 * u + 2))
+        w1_q = [quantize("w1_%d" % u, w1_bf[u][:].rearrange("p a c -> p (a c)"), H) for u in range(2)]
         late_i = tile("late_i", [P, 4, HALF], F32, "w1_bf0")
         late_r = tile("late_r", [P, 4, HALF], F32)
-        x_times_y(late_i[:, 0, :], w2_lhs, yi[1][:, 0, :], 1, 0, 6)
-        w1_q.append(quantize("w1_1", w1_bf[1][:].rearrange("p a c -> p (a c)"), H))
-        yr_early.append(tile("yr0_1", [P, 2, HALF], F32, "w1_raw1"))
-        for t in range(2, 4):
-            y_slot(yr_early[1][:, t - 2, :], w3_codes, w3_scale, 0, t, t)
         pairs = tile("pairs", [P, 2, WOVEN * TAIL, 2], BF16)
-        for t in range(4):
-            x_times_y(early_r[:, t, :], w1_lhs, yr_early[t // 2][:, t % 2, :], 0, t, (0, 1, 6, 2)[t])
+
+        def late_imag(t):
+            x_times_y(late_i[:, t, :], w2_lhs, yi[4 + t][:], 1, t, (6, 7, 4, 5)[t])
+
+        def early_real(t):
+            x_times_y(early_r[:, t, :], w1_lhs, yr_early[t // 2][:, t % 2, :], 0, t, (0, 1, 2, 3)[t])
             nc.gpsimd.tensor_tensor(out=pairs[:, t // 2, :, t % 2], in0=early_r[:, t, 0:WOVEN * TAIL],
                                     in1=early_i[:, t, 0:WOVEN * TAIL], op=ADD)
+
+        yr_early.append(tile("yr0_1", [P, 2, HALF], F32, "w1_raw0"))
+        for t in range(2, 4):
+            y_slot(yr_early[1][:, t - 2, :], w3_codes, w3_scale, 0, t, t)
+        late_imag(0)
+        for t in range(4):
+            early_real(t)
         for t in range(1, 4):
-            x_times_y(late_i[:, t, :], w2_lhs, yi[1][:, t, :], 1, t, (6, 7, 4, 5)[t])
+            late_imag(t)
         w5_bf = tile("w5_bf", [P, 4 * N], BF16)
         nc.scalar.copy(out=w5_bf[:].rearrange("p (c i t) -> p c t i", i=4, t=4),
                        in_=w5_raw[:].rearrange("p t (c i) -> p c t i", i=4))
         yr_late = [tile("yr1_%d" % t, [P, HALF], F32, "w5_raw" if t == 0 else None) for t in range(4)]
         for t in range(4):
-            y_slot(yr_late[t][:], w3_codes, w3_scale, 1, t, (3, 0, 1, 6)[t])
+            y_slot(yr_late[t][:], w3_codes, w3_scale, 1, t, (6, 0, 1, 2)[t])
+
         def late_product(t):
-            x_times_y(late_r[:, t, :], w1_lhs, yr_late[t][:], 1, t, (2, 7, 4, 5)[t])
+            x_times_y(late_r[:, t, :], w1_lhs, yr_late[t][:], 1, t, (3, 7, 4, 5)[t])
 
         for t in range(2):
             late_product(t)

@@ -21,7 +21,6 @@ COPY = mybir.ActivationFunctionType.Copy
 P = 128
 HALF = 512
 TAIL = 128
-WOVEN = 3
 
 
 def tile_list_raman_phase_traces_kernel(tc, tab_words, tab_scales, tab2_words, tab2_scales, offs, offs2,
@@ -82,7 +81,7 @@ def tile_list_raman_phase_traces_kernel(tc, tab_words, tab_scales, tab2_words, t
         taken = []
 
         def next_bank():
-            taken.append(banks[(6, 0, 1, 2, 3, 7, 4, 5)[len(taken) % 8]])
+            taken.append(banks[(1, 2, 3, 6, 7, 4, 5, 0)[len(taken) % 8]])
             return taken[-1]
 
         win_ps = banks[0]
@@ -168,16 +167,16 @@ def tile_list_raman_phase_traces_kernel(tc, tab_words, tab_scales, tab2_words, t
         w3_codes = tile("w3_codes", [P, H], U32)
         nc.vector.tensor_copy(out=w3_codes[:].bitcast(I32).rearrange("p (t b q) -> p t b q", t=4, q=4),
                               in_=w3_raw[:].bitcast(I32).rearrange("p (b t q) -> p t b q", t=4, q=4))
-        yr_early = [tile("yr0_0", [P, 2, HALF], F32)]
-        for t in range(2):
-            y_slot(yr_early[0][:, t, :], w3_codes, w3_scale, 0, t, t)
+        yr_early = tile("yr0", [P, 4, HALF], F32)
+        for t in range(4):
+            y_slot(yr_early[:, t, :], w3_codes, w3_scale, 0, t, t)
         v = [[v_first[:, HALF * h:HALF * (h + 1)],
               gather_words("v%d_1" % h, tab_w[1], offs_sb[:, 32 * h:32 * (h + 1)])[:]] for h in range(2)]
 
         early_i = tile("early_i", [P, 4, HALF], F32)
         early_r = tile("early_r", [P, 4, HALF], F32)
         for t in range(4):
-            x_times_y(early_i[:, t, :], w2_lhs, yi[t][:], 0, t, 2 + t)
+            x_times_y(early_i[:, t, :], w2_lhs, yi[t][:], 0, t, 4 + t)
         w1_bf = [tile("w1_bf%d" % u, [P, 2, 2 * H], BF16) for u in range(2)]
         for u in range(2):
             round_weight(nc.scalar.copy, w1_bf[u][:, 0, :], w1_raw[0], slice(2 * u, 2 * u + 2))
@@ -186,94 +185,82 @@ def tile_list_raman_phase_traces_kernel(tc, tab_words, tab_scales, tab2_words, t
         w1_q = [quantize("w1_%d" % u, w1_bf[u][:].rearrange("p a c -> p (a c)"), H) for u in range(2)]
         late_i = tile("late_i", [P, 4, HALF], F32, "w1_bf0")
         late_r = tile("late_r", [P, 4, HALF], F32)
-        pairs = tile("pairs", [P, 2, WOVEN * TAIL, 2], BF16)
-
-        def late_imag(t):
-            x_times_y(late_i[:, t, :], w2_lhs, yi[4 + t][:], 1, t, (6, 7, 4, 5)[t])
-
-        def early_real(t):
-            x_times_y(early_r[:, t, :], w1_lhs, yr_early[t // 2][:, t % 2, :], 0, t, (0, 1, 2, 3)[t])
-            nc.gpsimd.tensor_tensor(out=pairs[:, t // 2, :, t % 2], in0=early_r[:, t, 0:WOVEN * TAIL],
-                                    in1=early_i[:, t, 0:WOVEN * TAIL], op=ADD)
-
-        yr_early.append(tile("yr0_1", [P, 2, HALF], F32, "w1_raw0"))
-        for t in range(2, 4):
-            y_slot(yr_early[1][:, t - 2, :], w3_codes, w3_scale, 0, t, t)
-        late_imag(0)
-        for t in range(4):
-            early_real(t)
-        for t in range(1, 4):
-            late_imag(t)
-        w5_bf = tile("w5_bf", [P, 4 * N], BF16)
-        nc.scalar.copy(out=w5_bf[:].rearrange("p (c i t) -> p c t i", i=4, t=4),
-                       in_=w5_raw[:].rearrange("p t (c i) -> p c t i", i=4))
-        yr_late = [tile("yr1_%d" % t, [P, HALF], F32, "w5_raw" if t == 0 else None) for t in range(4)]
-        for t in range(4):
-            y_slot(yr_late[t][:], w3_codes, w3_scale, 1, t, (6, 0, 1, 2)[t])
-
-        def late_product(t):
-            x_times_y(late_r[:, t, :], w1_lhs, yr_late[t][:], 1, t, (3, 7, 4, 5)[t])
-
+        yr_late = [tile("yr1_early", [P, 2, HALF], F32, "w1_raw0")]
         for t in range(2):
-            late_product(t)
+            y_slot(yr_late[0][:, t, :], w3_codes, w3_scale, 1, t, 4 + t)
+        pairs = tile("pairs", [P, 2, HALF, 2], BF16)
+        x_times_y(late_i[:, 0, :], w2_lhs, yi[4][:], 1, 0, 0)
+        for t in range(4):
+            x_times_y(early_r[:, t, :], w1_lhs, yr_early[:, t, :], 0, t, (6, 7, 4, 5)[t])
+            nc.gpsimd.tensor_tensor(out=pairs[:, t // 2, :, t % 2], in0=early_r[:, t, :], in1=early_i[:, t, :], op=ADD)
+        for t in range(1, 4):
+            x_times_y(late_i[:, t, :], w2_lhs, yi[4 + t][:], 1, t, t)
+        w5_and_h = tile("w5_and_h", [P, 4 * (N + TAIL)], BF16)
+        nc.scalar.copy(out=w5_and_h[:, 0:4 * N].rearrange("p (c i t) -> p c t i", i=4, t=4),
+                       in_=w5_raw[:].rearrange("p t (c i) -> p c t i", i=4))
+        yr_late.append(tile("yr1_late", [P, 2, HALF], F32, "w5_raw"))
+        for t in range(2, 4):
+            y_slot(yr_late[1][:, t - 2, :], w3_codes, w3_scale, 1, t, 4 + t)
+        for t in range(4):
+            x_times_y(late_r[:, t, :], w1_lhs, yr_late[t // 2][:, t % 2, :], 1, t, (0, 4, 5, 0)[t])
 
-        h_woven = tile("h_woven", [P, 4 * WOVEN * TAIL], BF16, "w3_codes")
-        h_bf = [h_woven[:, 4 * TAIL * c:4 * TAIL * (c + 1)] for c in range(WOVEN)]
         pair_words = pairs[:].rearrange("p u j e -> p u (j e)").bitcast(U32).rearrange("p u j -> p j u")
-        for c in range(WOVEN):
-            nc.scalar.copy(out=h_bf[c].bitcast(U32).rearrange("p (j u) -> p j u", u=2),
-                           in_=pair_words[:, TAIL * c:TAIL * (c + 1), :])
+
+        def weave(dst, first, width):
+            nc.scalar.copy(out=dst.bitcast(U32).rearrange("p (j u) -> p j u", u=2),
+                           in_=pair_words[:, first:first + width, :])
+
+        def add_late(first, width):
+            hb = tile("h_late%d" % first, [P, 4 * width], BF16)
+            cols = slice(first - HALF, first - HALF + width)
+            nc.vector.tensor_tensor(out=hb[:].rearrange("p (c i t) -> p c t i", i=2, t=4),
+                                    in0=late_r[:, :, cols].rearrange("p t (c i) -> p c t i", i=2),
+                                    in1=late_i[:, :, cols].rearrange("p t (c i) -> p c t i", i=2), op=ADD)
+            return hb
 
         out_rows = out.rearrange("(i p) j -> p i j", p=P)
-        w5_codes = tile("w5_codes", [P, N], U32, "w5_raw")
-        w5_scales = tile("w5_scales", [P, N], U8)
-        nc.vector.quantize_mx(out=w5_codes[:, 0:256].bitcast(FP8X4), scales=w5_scales[:, 0:256], in_=w5_bf[:, 0:1024])
-        nc.vector.quantize_mx(out=w5_codes[:, 256:N].bitcast(FP8X4), scales=w5_scales[:, 256:N], in_=w5_bf[:, 1024:4 * N])
 
         def mix(dst, i, codes, scales):
             nc.tensor.matmul_mx(out=dst, lhsT=w5_codes[:, P * i:P * (i + 1)].bitcast(FP8X4),
-                                lhsT_scale=w5_scales[:, P * i:P * (i + 1)], rhs=codes[:].bitcast(FP8X4),
-                                rhs_scale=scales[:], start=True, stop=True)
+                                lhsT_scale=w5_scales[:, P * i:P * (i + 1)], rhs=codes.bitcast(FP8X4),
+                                rhs_scale=scales, start=True, stop=True)
 
-        def add_late(c):
-            hb = tile("h_late%d" % c, [P, 4 * TAIL], BF16, "yr1_2" if c == WOVEN else None)
-            h_bf.append(hb[:])
-            real, imag = (early_r, early_i) if c < 4 else (late_r, late_i)
-            cols = slice(TAIL * (c % 4), TAIL * (c % 4 + 1))
-            nc.vector.tensor_tensor(out=hb[:].rearrange("p (c i t) -> p c t i", i=2, t=4),
-                                    in0=real[:, :, cols].rearrange("p t (c i) -> p c t i", i=2),
-                                    in1=imag[:, :, cols].rearrange("p t (c i) -> p c t i", i=2), op=ADD)
+        def finish(codes, scales, first, width):
+            res = tile("res%d" % first, [P, 3, width], F32)
+            per_bank = HALF // width
+            for i0 in range(0, 3, per_bank):
+                rows = min(per_bank, 3 - i0)
+                bank = next_bank()
+                for i in range(rows):
+                    mix(bank[:, width * i:width * (i + 1)], i0 + i, codes, scales)
+                nc.scalar.copy(out=res[:, i0:i0 + rows, :],
+                               in_=bank[:, 0:rows * width].rearrange("p (i j) -> p i j", i=rows))
+            nc.sync.dma_start(out=out_rows[:, :, first:first + width], in_=res[:])
 
-        stores = [[0], [1, 2], [3], [4], [5], [6]]
-        res = {}
-        for group in stores:
-            held = tile("res%d" % group[0], [P, 3, TAIL * len(group)], F32)
-            for c in group:
-                res[c] = (held, group)
-
-        def finish(c):
-            codes, scales = quantize("h%d" % c, h_bf[c], TAIL)
-            bank = next_bank()
+        weave(w5_and_h[:, 4 * N:], 0, TAIL)
+        h_woven = tile("h_woven", [P, 4 * (HALF - TAIL)], BF16, "w3_codes")
+        weave(h_woven[:, 0:4 * TAIL], TAIL, TAIL)
+        weave(h_woven[:, 4 * TAIL:], 2 * TAIL, 2 * TAIL)
+        w5_codes, w5_scales = quantize("w5_and_h", w5_and_h[:], N + TAIL, "w1_raw0")
+        finish(w5_codes[:, N:], w5_scales[:, N:], 0, TAIL)
+        codes, scales = quantize("h1", h_woven[:, 0:4 * TAIL], TAIL)
+        finish(codes[:], scales[:], TAIL, TAIL)
+        codes, scales = quantize("h2", h_woven[:, 4 * TAIL:], 2 * TAIL)
+        finish(codes[:], scales[:], 2 * TAIL, 2 * TAIL)
+        late = [add_late(HALF, TAIL)]
+        quantised = []
+        for c in range(1, 4):
+            late.append(add_late(HALF + TAIL * c, TAIL))
+            quantised.append(quantize("h_late%d" % c, late[c - 1][:], TAIL))
+            if c < 3:
+                finish(quantised[-1][0][:], quantised[-1][1][:], HALF + TAIL * (c - 1), TAIL)
+        quantised.append(quantize("h_last", late[3][:], TAIL))
+        last_banks = [next_bank() for i in range(3)]
+        for c in range(2):
+            codes, scales = quantised[2 + c]
             for i in range(3):
-                mix(bank[:, TAIL * i:TAIL * (i + 1)], i, codes, scales)
-            held, group = res[c]
-            nc.scalar.copy(out=held[:, :, TAIL * (c - group[0]):TAIL * (c - group[0] + 1)],
-                           in_=bank[:, 0:3 * TAIL].rearrange("p (i j) -> p i j", i=3))
-            if c == group[-1]:
-                nc.sync.dma_start(out=out_rows[:, :, TAIL * group[0]:TAIL * (c + 1)], in_=held[:])
-
-        late_product(2)
-        for c in range(WOVEN):
-            finish(c)
-        late_product(3)
-        add_late(WOVEN)
-        for c in range(WOVEN + 1, 8):
-            add_late(c)
-            finish(c - 1)
-        codes, scales = quantize("h7", h_bf[7], TAIL)
-        for i, copy in enumerate((nc.vector.tensor_copy, nc.vector.tensor_copy, nc.scalar.copy)):
-            bank = next_bank()
-            mix(bank[:, 0:TAIL], i, codes, scales)
-            last = tile("last%d" % i, [P, TAIL], F32)
-            copy(out=last[:], in_=bank[:, 0:TAIL])
-            nc.sync.dma_start(out=out_rows[:, i, S - TAIL:S], in_=last[:])
+                mix(last_banks[i][:, TAIL * c:TAIL * (c + 1)], i, codes[:], scales[:])
+        for i, copy in enumerate((nc.vector.tensor_copy, nc.scalar.copy, nc.vector.tensor_copy)):
+            last = tile("last%d" % i, [P, 2 * TAIL], F32)
+            copy(out=last[:], in_=last_banks[i][:, 0:2 * TAIL])
+            nc.sync.dma_start(out=out_rows[:, i, S - 2 * TAIL:S], in_=last[:])

@@ -21,6 +21,7 @@ COPY = mybir.ActivationFunctionType.Copy
 P = 128
 HALF = 512
 TAIL = 128
+WOVEN = 384
 
 
 def tile_list_raman_phase_traces_kernel(tc, tab_words, tab_scales, tab2_words, tab2_scales, offs, offs2,
@@ -40,7 +41,7 @@ def tile_list_raman_phase_traces_kernel(tc, tab_words, tab_scales, tab2_words, t
         tab_bytes = tile("tab_bytes", [P, T], U8)
         tab2_bytes = tile("tab2_bytes", [P, T], U8)
         w_bytes = tile("w_bytes", [P, 2 * H], U8)
-        plane = [tile("plane0", [P, 2 * H + S], U8), tile("plane1", [P, H + S], U8)]
+        plane = [tile("plane%d" % a, [P, 2 * H + S], U8) for a in range(2)]
         win_rows = tile("win_rows", [P, P], F32)
         ident = tile("ident", [P, P], F32)
         nc.gpsimd.memset(tab_bytes[:].bitcast(I32), 0)
@@ -71,17 +72,14 @@ def tile_list_raman_phase_traces_kernel(tc, tab_words, tab_scales, tab2_words, t
                           in_=win.rearrange("(b t q) -> t b q", t=4, q=4))
         load_scale_rows(w_bytes[:, H:2 * H], w2_scales)
         tab2_w = load_words("tab2_w", tab2_words[0], T)
-        nc.sync.dma_start(out=w_bytes[:, 0:H].bitcast(I32)[0:P:8, :], in_=w3_scales[0].bitcast(I32))
+        nc.sync.dma_start(out=w_bytes[:, 0:H].bitcast(I32)[4:P:8, :], in_=w3_scales[0].bitcast(I32))
         tab_w = [load_words("tab_w0", tab_words[0], T)]
-        w2_raw = tile("w2_raw", [P, 2, 2 * H], U8)
-        nc.sync.dma_start(out=w2_raw[:].bitcast(I32), in_=w2_words.rearrange("a p c -> p a c").bitcast(I32))
-        w3_raw = load_words("w3_raw", w3_words[0], H)
 
         banks = [psum.tile([P, HALF], F32, name="bank%d" % b) for b in range(8)]
         taken = []
 
         def next_bank():
-            taken.append(banks[(1, 2, 3, 6, 7, 4, 5, 0)[len(taken) % 8]])
+            taken.append(banks[(0, 3, 5, 4, 7, 2, 6, 1)[len(taken) % 8]])
             return taken[-1]
 
         win_ps = banks[0]
@@ -110,22 +108,27 @@ def tile_list_raman_phase_traces_kernel(tc, tab_words, tab_scales, tab2_words, t
         nc.vector.tensor_copy(out=plane[0][:, 2 * H:].bitcast(I32), in_=picked[:].bitcast(I32))
         v2_scale = tile("v2_scale", [P, S], U8)
         nc.vector.tensor_copy(v2_scale[:], tab2_bytes[:].indirect(offs2_sb[:]))
-        nc.gpsimd.tensor_copy(out=plane[0][:, 0:2 * H].bitcast(I32).rearrange("p (s t b) -> p s t b", s=2, t=4),
-                              in_=w_bytes[:].bitcast(I32).rearrange("p (s b t) -> p s t b", s=2, t=4))
+        for cols in (slice(H, 2 * H), slice(0, H)):
+            nc.gpsimd.tensor_copy(out=plane[0][:, cols].bitcast(I32).rearrange("p (t b) -> p t b", t=4),
+                                  in_=w_bytes[:, cols].bitcast(I32).rearrange("p (b t) -> p t b", t=4))
         for r in range(1, 4):
-            nc.sync.dma_start(out=plane[0][:].bitcast(I32)[r:P:32, :], in_=plane[0][:].bitcast(I32)[8 * r:P:32, :])
+            nc.sync.dma_start(out=plane[0][:, H:].bitcast(I32)[r:P:32, :],
+                              in_=plane[0][:, H:].bitcast(I32)[8 * r:P:32, :])
         tab_w.append(load_words("tab_w1", tab_words[1], T))
+        w2_raw = tile("w2_raw", [P, 2, 2 * H], U8)
+        nc.sync.dma_start(out=w2_raw[:].bitcast(I32), in_=w2_words.rearrange("a p c -> p a c").bitcast(I32))
         for r in range(4):
             nc.sync.dma_start(out=plane[1][:].bitcast(I32)[r:P:32, :],
-                              in_=plane[0][:, H:].bitcast(I32)[8 * r + 4:P:32, :])
+                              in_=plane[0][:].bitcast(I32)[8 * r + 4:P:32, :])
+        w3_raw = load_words("w3_raw", w3_words[0], H)
         w1_raw = [load_rows("w1_raw%d" % a, w1[512 * a:512 * (a + 1), :]) for a in range(2)]
         w5_raw = tile("w5_raw", [P, 4, N], F32)
         w5_by_slot = w5.rearrange("(b t q) n -> t b q n", t=4, q=4)
         for t in range(4):
             nc.sync.dma_start(out=w5_raw[:, t, :], in_=w5_by_slot[t])
-        w3_scale = plane[0][:, 0:H]
-        w2_scale = [plane[0][:, H:2 * H], plane[1][:, 0:H]]
-        v_scale = [plane[0][:, 2 * H:], plane[1][:, H:]]
+        w3_scale = plane[1][:, 0:H]
+        w2_scale = [plane[a][:, H:2 * H] for a in range(2)]
+        v_scale = [plane[a][:, 2 * H:] for a in range(2)]
 
         win_col = tile("win_col", [P, 4], F32)
         nc.scalar.copy(out=win_col[:], in_=win_ps[:, 0:4])
@@ -161,48 +164,49 @@ def tile_list_raman_phase_traces_kernel(tc, tab_words, tab_scales, tab2_words, t
         for n in range(8):
             y_slot(yi[n][:], w4_codes, w4_scales, n // 4, n % 4, n)
         v_first = gather_words("v_first", tab_w[0], offs_sb[:])
+        v_second = [gather_words("v_second0", tab_w[1], offs_sb[:, 0:32])]
         w2_codes = tile("w2_codes", [P, 2, 2 * H], U8)
         nc.vector.tensor_copy(out=w2_codes[:].bitcast(I32).rearrange("p a (t b e) -> p a t b e", t=4, e=2),
                               in_=w2_raw[:].bitcast(I32).rearrange("p a (b t e) -> p a t b e", t=4, e=2))
-        w3_codes = tile("w3_codes", [P, H], U32)
-        nc.vector.tensor_copy(out=w3_codes[:].bitcast(I32).rearrange("p (t b q) -> p t b q", t=4, q=4),
+        v_second.append(gather_words("v_second1", tab_w[1], offs_sb[:, 32:64], "w2_raw"))
+        v = [[v_first[:, HALF * h:HALF * (h + 1)], v_second[h][:]] for h in range(2)]
+
+        w3_codes = tile("w3_codes", [P, H], U32, "tab_w1")
+        nc.gpsimd.tensor_copy(out=w3_codes[:].bitcast(I32).rearrange("p (t b q) -> p t b q", t=4, q=4),
                               in_=w3_raw[:].bitcast(I32).rearrange("p (b t q) -> p t b q", t=4, q=4))
-        yr_early = tile("yr0", [P, 4, HALF], F32)
-        for t in range(4):
-            y_slot(yr_early[:, t, :], w3_codes, w3_scale, 0, t, t)
-        v = [[v_first[:, HALF * h:HALF * (h + 1)],
-              gather_words("v%d_1" % h, tab_w[1], offs_sb[:, 32 * h:32 * (h + 1)])[:]] for h in range(2)]
 
         early_i = tile("early_i", [P, 4, HALF], F32)
         early_r = tile("early_r", [P, 4, HALF], F32)
-        for t in range(4):
-            x_times_y(early_i[:, t, :], w2_lhs, yi[t][:], 0, t, 4 + t)
-        w1_bf = [tile("w1_bf%d" % u, [P, 2, 2 * H], BF16) for u in range(2)]
-        for u in range(2):
-            round_weight(nc.scalar.copy, w1_bf[u][:, 0, :], w1_raw[0], slice(2 * u, 2 * u + 2))
-        for u in range(2):
-            round_weight(nc.vector.tensor_copy, w1_bf[u][:, 1, :], w1_raw[1], slice(2 * u, 2 * u + 2))
-        w1_q = [quantize("w1_%d" % u, w1_bf[u][:].rearrange("p a c -> p (a c)"), H) for u in range(2)]
-        late_i = tile("late_i", [P, 4, HALF], F32, "w1_bf0")
+        late_i_row = tile("late_i", [P, 4 * HALF], F32)
+        late_i = late_i_row[:].rearrange("p (t j) -> p t j", t=4)
         late_r = tile("late_r", [P, 4, HALF], F32)
-        yr_late = [tile("yr1_early", [P, 2, HALF], F32, "w1_raw0")]
-        for t in range(2):
-            y_slot(yr_late[0][:, t, :], w3_codes, w3_scale, 1, t, 4 + t)
-        pairs = tile("pairs", [P, 2, HALF, 2], BF16)
-        x_times_y(late_i[:, 0, :], w2_lhs, yi[4][:], 1, 0, 0)
         for t in range(4):
-            x_times_y(early_r[:, t, :], w1_lhs, yr_early[:, t, :], 0, t, (6, 7, 4, 5)[t])
-            nc.gpsimd.tensor_tensor(out=pairs[:, t // 2, :, t % 2], in0=early_r[:, t, :], in1=early_i[:, t, :], op=ADD)
-        for t in range(1, 4):
-            x_times_y(late_i[:, t, :], w2_lhs, yi[4 + t][:], 1, t, t)
+            x_times_y(early_i[:, t, :], w2_lhs, yi[t][:], 0, t, t)
+        x_times_y(late_i[:, 0, :], w2_lhs, yi[4][:], 1, 0, 4)
+        w1_bf = [late_i_row[:, HALF:3 * HALF].bitcast(BF16), tile("w1_bf1", [P, 4 * H], BF16)[:]]
+        for a, copy in enumerate((nc.scalar.copy, nc.vector.tensor_copy)):
+            for u in range(2):
+                round_weight(copy, w1_bf[u][:, 2 * H * a:2 * H * (a + 1)], w1_raw[a], slice(2 * u, 2 * u + 2))
+        w1_q = [quantize("w1_%d" % u, w1_bf[u], H) for u in range(2)]
+        yr_early = tile("yr0", [P, 4, HALF], F32, "w1_raw0")
+        for t in range(4):
+            y_slot(yr_early[:, t, :], w3_codes, w3_scale, 0, t, t)
+        pairs = tile("pairs", [P, 2, WOVEN, 2], BF16)
+        x_times_y(late_i[:, 1, :], w2_lhs, yi[5][:], 1, 1, 5)
+        for t in range(4):
+            x_times_y(early_r[:, t, :], w1_lhs, yr_early[:, t, :], 0, t, (4, 7, 1, 2)[t])
+            nc.gpsimd.tensor_tensor(out=pairs[:, t // 2, :, t % 2], in0=early_r[:, t, 0:WOVEN],
+                                    in1=early_i[:, t, 0:WOVEN], op=ADD)
+        for t in range(2, 4):
+            x_times_y(late_i[:, t, :], w2_lhs, yi[4 + t][:], 1, t, (6, 0)[t - 2])
         w5_and_h = tile("w5_and_h", [P, 4 * (N + TAIL)], BF16)
         nc.scalar.copy(out=w5_and_h[:, 0:4 * N].rearrange("p (c i t) -> p c t i", i=4, t=4),
                        in_=w5_raw[:].rearrange("p t (c i) -> p c t i", i=4))
-        yr_late.append(tile("yr1_late", [P, 2, HALF], F32, "w5_raw"))
-        for t in range(2, 4):
-            y_slot(yr_late[1][:, t - 2, :], w3_codes, w3_scale, 1, t, 4 + t)
+        yr_late = [tile("yr1_%d" % t, [P, HALF], F32, "w5_raw" if t == 0 else None) for t in range(4)]
         for t in range(4):
-            x_times_y(late_r[:, t, :], w1_lhs, yr_late[t // 2][:, t % 2, :], 1, t, (0, 4, 5, 0)[t])
+            y_slot(yr_late[t][:], w3_codes, w3_scale, 1, t, (3, 5, 4, 7)[t])
+        for t in range(4):
+            x_times_y(late_r[:, t, :], w1_lhs, yr_late[t][:], 1, t, (1, 2, 6, 1)[t])
 
         pair_words = pairs[:].rearrange("p u j e -> p u (j e)").bitcast(U32).rearrange("p u j -> p j u")
 
@@ -210,12 +214,13 @@ def tile_list_raman_phase_traces_kernel(tc, tab_words, tab_scales, tab2_words, t
             nc.scalar.copy(out=dst.bitcast(U32).rearrange("p (j u) -> p j u", u=2),
                            in_=pair_words[:, first:first + width, :])
 
-        def add_late(first, width):
-            hb = tile("h_late%d" % first, [P, 4 * width], BF16)
-            cols = slice(first - HALF, first - HALF + width)
+        def add_late(first, width, after=None):
+            hb = tile("h_late%d" % first, [P, 4 * width], BF16, after)
+            real, imag = (early_r, early_i) if first < HALF else (late_r, late_i)
+            cols = slice(first % HALF, first % HALF + width)
             nc.vector.tensor_tensor(out=hb[:].rearrange("p (c i t) -> p c t i", i=2, t=4),
-                                    in0=late_r[:, :, cols].rearrange("p t (c i) -> p c t i", i=2),
-                                    in1=late_i[:, :, cols].rearrange("p t (c i) -> p c t i", i=2), op=ADD)
+                                    in0=real[:, :, cols].rearrange("p t (c i) -> p c t i", i=2),
+                                    in1=imag[:, :, cols].rearrange("p t (c i) -> p c t i", i=2), op=ADD)
             return hb
 
         out_rows = out.rearrange("(i p) j -> p i j", p=P)
@@ -238,26 +243,23 @@ def tile_list_raman_phase_traces_kernel(tc, tab_words, tab_scales, tab2_words, t
             nc.sync.dma_start(out=out_rows[:, :, first:first + width], in_=res[:])
 
         weave(w5_and_h[:, 4 * N:], 0, TAIL)
-        h_woven = tile("h_woven", [P, 4 * (HALF - TAIL)], BF16, "w3_codes")
-        weave(h_woven[:, 0:4 * TAIL], TAIL, TAIL)
-        weave(h_woven[:, 4 * TAIL:], 2 * TAIL, 2 * TAIL)
-        w5_codes, w5_scales = quantize("w5_and_h", w5_and_h[:], N + TAIL, "w1_raw0")
+        h_woven = tile("h_woven", [P, 4 * (WOVEN - TAIL)], BF16, "tab_w1")
+        weave(h_woven[:], TAIL, WOVEN - TAIL)
+        w5_codes, w5_scales = quantize("w5_and_h", w5_and_h[:], N + TAIL, "yr1_2")
         finish(w5_codes[:, N:], w5_scales[:, N:], 0, TAIL)
-        codes, scales = quantize("h1", h_woven[:, 0:4 * TAIL], TAIL)
-        finish(codes[:], scales[:], TAIL, TAIL)
-        codes, scales = quantize("h2", h_woven[:, 4 * TAIL:], 2 * TAIL)
-        finish(codes[:], scales[:], 2 * TAIL, 2 * TAIL)
-        late = [add_late(HALF, TAIL)]
+        codes, scales = quantize("h_woven", h_woven[:], WOVEN - TAIL)
+        finish(codes[:], scales[:], TAIL, WOVEN - TAIL)
+        late = [add_late(WOVEN, TAIL, "yr1_3")]
         quantised = []
-        for c in range(1, 4):
-            late.append(add_late(HALF + TAIL * c, TAIL))
-            quantised.append(quantize("h_late%d" % c, late[c - 1][:], TAIL))
-            if c < 3:
-                finish(quantised[-1][0][:], quantised[-1][1][:], HALF + TAIL * (c - 1), TAIL)
-        quantised.append(quantize("h_last", late[3][:], TAIL))
+        for first in range(HALF, S, TAIL):
+            late.append(add_late(first, TAIL))
+            quantised.append(quantize("h%d" % first, late[-2][:], TAIL))
+            if first < S - TAIL:
+                finish(quantised[-1][0][:], quantised[-1][1][:], first - TAIL, TAIL)
+        quantised.append(quantize("h_last", late[-1][:], TAIL))
         last_banks = [next_bank() for i in range(3)]
         for c in range(2):
-            codes, scales = quantised[2 + c]
+            codes, scales = quantised[c - 2]
             for i in range(3):
                 mix(last_banks[i][:, TAIL * c:TAIL * (c + 1)], i, codes[:], scales[:])
         for i, copy in enumerate((nc.vector.tensor_copy, nc.scalar.copy, nc.vector.tensor_copy)):

@@ -30,6 +30,7 @@ def tile_list_raman_phase_traces_kernel(tc, tab_words, tab_scales, tab2_words, t
     with ExitStack() as ctx:
         lists = ctx.enter_context(tc.tile_pool(name="lists", bufs=1))
         sb = ctx.enter_context(tc.tile_pool(name="sb", bufs=1))
+        shared = ctx.enter_context(tc.tile_pool(name="shared", bufs=1))
         psum = ctx.enter_context(tc.psum_pool(name="psum", bufs=1))
 
         def tile(name, shape, dtype, after=None):
@@ -41,11 +42,12 @@ def tile_list_raman_phase_traces_kernel(tc, tab_words, tab_scales, tab2_words, t
         tab_bytes = tile("tab_bytes", [P, T], U8)
         tab2_bytes = tile("tab2_bytes", [P, T], U8)
         w_bytes = tile("w_bytes", [P, 2 * H], U8)
-        plane = [tile("plane%d" % a, [P, 2 * H + S], U8) for a in range(2)]
-        win_rows = tile("win_rows", [P, P], F32)
+        plane = [tile("plane0", [P, 2 * H + S], U8), tile("plane1", [P, H + S], U8)]
+        win_row = tile("win_row", [1, H], F32)
+        win_slots = tile("win_slots", [P, H], F32)
         ident = tile("ident", [P, P], F32)
         nc.gpsimd.memset(tab_bytes[:].bitcast(I32), 0)
-        for zeroed in (tab2_bytes, win_rows, w_bytes, ident, plane[1]):
+        for zeroed in (tab2_bytes, w_bytes, ident, win_slots, plane[1]):
             nc.vector.memset(zeroed[:].bitcast(I32), 0)
         make_identity(nc, ident[:], nomemset=True)
 
@@ -54,8 +56,7 @@ def tile_list_raman_phase_traces_kernel(tc, tab_words, tab_scales, tab2_words, t
             nc.sync.dma_start(out=t[:].bitcast(I32), in_=words.rearrange("p t i -> p (t i)").bitcast(I32))
             return t
 
-        def load_rows(name, rows):
-            t = tile(name, [P, 4, rows.shape[1]], F32)
+        def load_rows(t, rows):
             nc.sync.dma_start(out=t[:], in_=rows.rearrange("(p j) c -> p j c", j=4))
             return t
 
@@ -65,29 +66,36 @@ def tile_list_raman_phase_traces_kernel(tc, tab_words, tab_scales, tab2_words, t
         nc.sync.dma_start(offs_sb[:], offs)
         nc.sync.dma_start(offs2_sb[:], offs2)
         load_scale_rows(tab_bytes[:], tab_scales)
-        w4_raw = load_rows("w4_raw", w4)
         for r in range(4):
             nc.sync.dma_start(out=tab2_bytes[:].bitcast(I32)[r:P:32, :], in_=tab2_scales[0, r:16:4, :].bitcast(I32))
-        nc.sync.dma_start(out=win_rows[0:4, :].rearrange("t (b q) -> t b q", q=4),
-                          in_=win.rearrange("(b t q) -> t b q", t=4, q=4))
-        load_scale_rows(w_bytes[:, H:2 * H], w2_scales)
         tab2_w = load_words("tab2_w", tab2_words[0], T)
-        nc.sync.dma_start(out=w_bytes[:, 0:H].bitcast(I32)[4:P:8, :], in_=w3_scales[0].bitcast(I32))
-        tab_w = [load_words("tab_w0", tab_words[0], T)]
+        nc.sync.dma_start(out=w_bytes[:, 0:H].bitcast(I32)[0:P:8, :], in_=w3_scales[0].bitcast(I32))
+        load_scale_rows(w_bytes[:, H:2 * H], w2_scales)
+        nc.sync.dma_start(out=win_row[:], in_=win.rearrange("(o r) -> o r", o=1))
+        w3_raw = load_words("w3_raw", w3_words[0], H)
+        w4_raw = load_rows(tile("w4_raw", [P, 4, H], F32), w4)
 
         banks = [psum.tile([P, HALF], F32, name="bank%d" % b) for b in range(8)]
         taken = []
 
         def next_bank():
-            taken.append(banks[(0, 3, 5, 4, 7, 2, 6, 1)[len(taken) % 8]])
+            taken.append(banks[(4, 5, 6, 7, 0, 1, 2, 3)[len(taken) % 8]])
             return taken[-1]
 
         win_ps = banks[0]
-        nc.tensor.transpose(win_ps[:, 0:P], win_rows[:], ident[:])
+        nc.gpsimd.tensor_copy(out=win_slots[0:1, :].rearrange("o (t b q) -> o t b q", t=4, q=4),
+                              in_=win_row[:].rearrange("o (b t q) -> o t b q", t=4, q=4))
+        for t in range(4):
+            nc.tensor.transpose(win_ps[:, P * t:P * (t + 1)], win_slots[:, P * t:P * (t + 1)], ident[:])
 
-        def round_weight(copy, dst, raw, slots):
-            copy(out=dst.rearrange("p (t b q j) -> p t b j q", b=32, q=4, j=4),
-                 in_=raw[:].rearrange("p j (b t q) -> p t b j q", t=4, q=4)[:, slots])
+        def round_slots(dst, raw, slots):
+            nc.scalar.copy(out=dst.rearrange("p (t b q j) -> p t b j q", b=32, q=4, j=4),
+                           in_=raw[:].rearrange("p j (b t q) -> p t b j q", t=4, q=4)[:, slots])
+
+        def round_slot_gpsimd(dst, raw, t):
+            nc.gpsimd.tensor_scalar(out=dst.rearrange("p (b q j) -> p b q j", q=4, j=4),
+                                    in0=raw[:].rearrange("p j (b t q) -> p t b q j", t=4, q=4)[:, t],
+                                    scalar1=1.0, scalar2=0.0, op0=MULT, op1=ADD)
 
         def quantize(name, src, width, after=None):
             codes = tile(name + "_codes", [P, width], U32, after)
@@ -101,7 +109,6 @@ def tile_list_raman_phase_traces_kernel(tc, tab_words, tab_scales, tab2_words, t
             return t
 
         w4_bf = tile("w4_bf", [P, 4 * H], BF16)
-        round_weight(nc.scalar.copy, w4_bf[:], w4_raw, slice(0, 4))
 
         picked = tile("picked", [P, S], U8)
         nc.vector.tensor_copy(picked[:], tab_bytes[:].indirect(offs_sb[:]))
@@ -112,101 +119,129 @@ def tile_list_raman_phase_traces_kernel(tc, tab_words, tab_scales, tab2_words, t
             nc.gpsimd.tensor_copy(out=plane[0][:, cols].bitcast(I32).rearrange("p (t b) -> p t b", t=4),
                                   in_=w_bytes[:, cols].bitcast(I32).rearrange("p (b t) -> p t b", t=4))
         for r in range(1, 4):
-            nc.sync.dma_start(out=plane[0][:, H:].bitcast(I32)[r:P:32, :],
-                              in_=plane[0][:, H:].bitcast(I32)[8 * r:P:32, :])
-        tab_w.append(load_words("tab_w1", tab_words[1], T))
-        w2_raw = tile("w2_raw", [P, 2, 2 * H], U8)
-        nc.sync.dma_start(out=w2_raw[:].bitcast(I32), in_=w2_words.rearrange("a p c -> p a c").bitcast(I32))
+            nc.sync.dma_start(out=plane[0][:].bitcast(I32)[r:P:32, :], in_=plane[0][:].bitcast(I32)[8 * r:P:32, :])
+        tab_w = [load_words("tab_w%d" % a, tab_words[a], T) for a in range(2)]
         for r in range(4):
             nc.sync.dma_start(out=plane[1][:].bitcast(I32)[r:P:32, :],
-                              in_=plane[0][:].bitcast(I32)[8 * r + 4:P:32, :])
-        w3_raw = load_words("w3_raw", w3_words[0], H)
-        w1_raw = [load_rows("w1_raw%d" % a, w1[512 * a:512 * (a + 1), :]) for a in range(2)]
+                              in_=plane[0][:, H:].bitcast(I32)[8 * r + 4:P:32, :])
+        w2_raw = tile("w2_raw", [P, 2, 2 * H], U8)
+        nc.sync.dma_start(out=w2_raw[:].bitcast(I32), in_=w2_words.rearrange("a p c -> p a c").bitcast(I32))
+        w1_raw = [load_rows(tile("w1_raw0", [P, 4, H], F32), w1[0:512, :]),
+                  load_rows(shared.tile([P, 4, H], F32, name="w1_raw1", offset=0, align_bytes=64), w1[512:1024, :])]
         w5_raw = tile("w5_raw", [P, 4, N], F32)
         w5_by_slot = w5.rearrange("(b t q) n -> t b q n", t=4, q=4)
         for t in range(4):
             nc.sync.dma_start(out=w5_raw[:, t, :], in_=w5_by_slot[t])
-        w3_scale = plane[1][:, 0:H]
-        w2_scale = [plane[a][:, H:2 * H] for a in range(2)]
-        v_scale = [plane[a][:, 2 * H:] for a in range(2)]
+        w3_scale = plane[0][:, 0:H]
+        w2_scale = [plane[0][:, H:2 * H], plane[1][:, 0:H]]
+        v_scale = [plane[0][:, 2 * H:], plane[1][:, H:]]
 
         win_col = tile("win_col", [P, 4], F32)
-        nc.scalar.copy(out=win_col[:], in_=win_ps[:, 0:4])
-        w4_codes, w4_scales = quantize("w4", w4_bf[:], H, "tab2_bytes")
-        v2 = [gather_words("v2_%d" % h, tab2_w, offs2_sb[:, 32 * h:32 * (h + 1)]) for h in range(2)]
+        nc.scalar.copy(out=win_col[:], in_=win_ps[:, 0:H:P])
+        round_slots(w4_bf[:, 0:2 * H], w4_raw, slice(0, 2))
+        w3_codes = tile("w3_codes", [P, H], U32)
+        nc.gpsimd.tensor_copy(out=w3_codes[:].bitcast(I32).rearrange("p (t b q) -> p t b q", t=4, q=4),
+                              in_=w3_raw[:].bitcast(I32).rearrange("p (b t q) -> p t b q", t=4, q=4))
+        for t in (2, 3):
+            round_slot_gpsimd(w4_bf[:, H * t:H * (t + 1)], w4_raw, t)
+        v2 = [gather_words("v2_0", tab2_w, offs2_sb[:, 0:32], "tab2_bytes"),
+              gather_words("v2_1", tab2_w, offs2_sb[:, 32:64])]
+        w4_codes, w4_scales = quantize("w4", w4_bf[:], H)
 
-        def y_slot(y, codes, scales, h, t, b):
-            bank = banks[b]
-            nc.tensor.matmul_mx(out=bank[:], lhsT=codes[:, P * t:P * (t + 1)].bitcast(FP8X4),
+        def y_pass(codes, scales, h, t, b):
+            nc.tensor.matmul_mx(out=banks[b][:], lhsT=codes[:, P * t:P * (t + 1)].bitcast(FP8X4),
                                 lhsT_scale=scales[:, P * t:P * (t + 1)], rhs=v2[h][:].bitcast(FP8X4),
                                 rhs_scale=v2_scale[:, HALF * h:HALF * (h + 1)], start=True, stop=True)
-            nc.scalar.activation(out=y, in_=bank[:], func=COPY, scale=win_col[:, t:t + 1])
+
+        def y_out(y, t, b):
+            nc.scalar.activation(out=y, in_=banks[b][:], func=COPY, scale=win_col[:, t:t + 1])
+
+        def y_slot(y, codes, scales, h, t, b):
+            y_pass(codes, scales, h, t, b)
+            y_out(y, t, b)
+
+        def on_w1_raw1(name, quarter, shape, dtype):
+            return shared.tile(shape, dtype, name=name, offset=4 * HALF * quarter, align_bytes=64)
+
+        def x_pass(lhs, a, h, t, b):
+            codes, scales = lhs(a, t)
+            nc.tensor.matmul_mx(out=banks[b][:], lhsT=codes, lhsT_scale=scales, rhs=v[h][a].bitcast(FP8X4),
+                                rhs_scale=v_scale[a][:, HALF * h:HALF * (h + 1)], start=(a == 0), stop=(a == 1))
+
+        def times_y(prod, y, b):
+            nc.vector.tensor_tensor(out=prod, in0=y, in1=banks[b][:], op=MULT)
 
         def x_times_y(prod, lhs, y, h, t, b):
-            bank = banks[b]
-            for a in (1, 0):
-                codes, scales = lhs(a, t)
-                nc.tensor.matmul_mx(out=bank[:], lhsT=codes, lhsT_scale=scales, rhs=v[h][a].bitcast(FP8X4),
-                                    rhs_scale=v_scale[a][:, HALF * h:HALF * (h + 1)],
-                                    start=(a == 1), stop=(a == 0))
-            nc.vector.tensor_tensor(out=prod, in0=y, in1=bank[:], op=MULT)
+            for a in range(2):
+                x_pass(lhs, a, h, t, b)
+            times_y(prod, y, b)
 
         def w2_lhs(a, t):
             return (w2_codes[:, a, 2 * P * t:2 * P * (t + 1)].bitcast(FP4X4),
                     w2_scale[a][:, P * t:P * (t + 1)])
 
         def w1_lhs(a, t):
-            codes, scales = w1_q[t // 2]
-            cols = slice(P * (2 * a + t % 2), P * (2 * a + t % 2 + 1))
+            codes, scales = w1_q[a * (1 + t // 2)]
+            cols = slice(P * (t % (4 - 2 * a)), P * (t % (4 - 2 * a) + 1))
             return codes[:, cols].bitcast(FP8X4), scales[:, cols]
 
-        yi = [tile("yi%d" % n, [P, HALF], F32) for n in range(8)]
+        late_i_row = tile("late_i", [P, 5 * HALF], F32)
+        late_i = late_i_row[:, HALF:].rearrange("p (t j) -> p t j", t=4)
+        yr_early = [late_i[:, 2 + t, :] if t < 2 else tile("yr0_%d" % t, [P, HALF], F32)[:] for t in range(4)]
+        for t in range(4):
+            y_slot(yr_early[t], w3_codes, w3_scale, 0, t, 4 + t)
+        yi = [tile("yi%d" % n, [P, HALF], F32) for n in range(6)]
         for n in range(8):
-            y_slot(yi[n][:], w4_codes, w4_scales, n // 4, n % 4, n)
-        v_first = gather_words("v_first", tab_w[0], offs_sb[:])
-        v_second = [gather_words("v_second0", tab_w[1], offs_sb[:, 0:32])]
+            y_pass(w4_codes, w4_scales, n // 4, n % 4, n)
+        for n in range(6):
+            y_out(yi[n][:], n % 4, n)
+        v_first = gather_words("v_first", tab_w[0], offs_sb[:], "w4_bf")
+        v_second = [gather_words("v_second%d" % h, tab_w[1], offs_sb[:, 32 * h:32 * (h + 1)]) for h in range(2)]
         w2_codes = tile("w2_codes", [P, 2, 2 * H], U8)
-        nc.vector.tensor_copy(out=w2_codes[:].bitcast(I32).rearrange("p a (t b e) -> p a t b e", t=4, e=2),
+        nc.gpsimd.tensor_copy(out=w2_codes[:].bitcast(I32).rearrange("p a (t b e) -> p a t b e", t=4, e=2),
                               in_=w2_raw[:].bitcast(I32).rearrange("p a (b t e) -> p a t b e", t=4, e=2))
-        v_second.append(gather_words("v_second1", tab_w[1], offs_sb[:, 32:64], "w2_raw"))
         v = [[v_first[:, HALF * h:HALF * (h + 1)], v_second[h][:]] for h in range(2)]
-
-        w3_codes = tile("w3_codes", [P, H], U32, "tab_w1")
-        nc.gpsimd.tensor_copy(out=w3_codes[:].bitcast(I32).rearrange("p (t b q) -> p t b q", t=4, q=4),
-                              in_=w3_raw[:].bitcast(I32).rearrange("p (b t q) -> p t b q", t=4, q=4))
 
         early_i = tile("early_i", [P, 4, HALF], F32)
         early_r = tile("early_r", [P, 4, HALF], F32)
-        late_i_row = tile("late_i", [P, 4 * HALF], F32)
-        late_i = late_i_row[:].rearrange("p (t j) -> p t j", t=4)
         late_r = tile("late_r", [P, 4, HALF], F32)
         for t in range(4):
             x_times_y(early_i[:, t, :], w2_lhs, yi[t][:], 0, t, t)
-        x_times_y(late_i[:, 0, :], w2_lhs, yi[4][:], 1, 0, 4)
-        w1_bf = [late_i_row[:, HALF:3 * HALF].bitcast(BF16), tile("w1_bf1", [P, 4 * H], BF16)[:]]
-        for a, copy in enumerate((nc.scalar.copy, nc.vector.tensor_copy)):
-            for u in range(2):
-                round_weight(copy, w1_bf[u][:, 2 * H * a:2 * H * (a + 1)], w1_raw[a], slice(2 * u, 2 * u + 2))
-        w1_q = [quantize("w1_%d" % u, w1_bf[u], H) for u in range(2)]
-        yr_early = tile("yr0", [P, 4, HALF], F32, "w1_raw0")
+        w1_bf = [late_i_row[:, 0:2 * HALF].bitcast(BF16), tile("w1_bf1", [P, 2 * H], BF16)[:],
+                 late_i_row[:, 0:HALF].bitcast(BF16)]
+        round_slots(w1_bf[0][:, 0:2 * H], w1_raw[0], slice(0, 2))
+        for t in (2, 3):
+            round_slot_gpsimd(w1_bf[0][:, H * t:H * (t + 1)], w1_raw[0], t)
+        w1_q = [quantize("w1_0", w1_bf[0], H)]
         for t in range(4):
-            y_slot(yr_early[:, t, :], w3_codes, w3_scale, 0, t, t)
+            x_pass(w1_lhs, 0, 0, t, t)
+        for t in range(2):
+            x_times_y(late_i[:, t, :], w2_lhs, yi[4 + t][:], 1, t, 4 + t)
+        round_slots(w1_bf[1], w1_raw[1], slice(0, 2))
+        round_slot_gpsimd(w1_bf[2][:, H:2 * H], w1_raw[1], 3)
+        round_slots(w1_bf[2][:, 0:H], w1_raw[1], slice(2, 3))
+        for u in range(2):
+            w1_q.append(quantize("w1_1%d" % u, w1_bf[1 + u], H // 2))
+        for n in range(6, 8):
+            yi.append(on_w1_raw1("yi%d" % n, n - 6, [P, HALF], F32))
+            y_out(yi[n][:], n % 4, n)
         pairs = tile("pairs", [P, 2, WOVEN, 2], BF16)
-        x_times_y(late_i[:, 1, :], w2_lhs, yi[5][:], 1, 1, 5)
         for t in range(4):
-            x_times_y(early_r[:, t, :], w1_lhs, yr_early[:, t, :], 0, t, (4, 7, 1, 2)[t])
+            x_pass(w1_lhs, 1, 0, t, t)
+            times_y(early_r[:, t, :], yr_early[t], t)
             nc.gpsimd.tensor_tensor(out=pairs[:, t // 2, :, t % 2], in0=early_r[:, t, 0:WOVEN],
                                     in1=early_i[:, t, 0:WOVEN], op=ADD)
         for t in range(2, 4):
-            x_times_y(late_i[:, t, :], w2_lhs, yi[4 + t][:], 1, t, (6, 0)[t - 2])
+            x_times_y(late_i[:, t, :], w2_lhs, yi[4 + t][:], 1, t, 4 + t)
+        yr_late = [on_w1_raw1("yr1_%d" % t, t + 2, [P, HALF], F32) if t < 2 else tile("yr1_%d" % t, [P, HALF], F32)
+                   for t in range(4)]
+        for t in range(4):
+            y_slot(yr_late[t][:], w3_codes, w3_scale, 1, t, 4 + t % 2)
         w5_and_h = tile("w5_and_h", [P, 4 * (N + TAIL)], BF16)
         nc.scalar.copy(out=w5_and_h[:, 0:4 * N].rearrange("p (c i t) -> p c t i", i=4, t=4),
                        in_=w5_raw[:].rearrange("p t (c i) -> p c t i", i=4))
-        yr_late = [tile("yr1_%d" % t, [P, HALF], F32, "w5_raw" if t == 0 else None) for t in range(4)]
         for t in range(4):
-            y_slot(yr_late[t][:], w3_codes, w3_scale, 1, t, (3, 5, 4, 7)[t])
-        for t in range(4):
-            x_times_y(late_r[:, t, :], w1_lhs, yr_late[t][:], 1, t, (1, 2, 6, 1)[t])
+            x_times_y(late_r[:, t, :], w1_lhs, yr_late[t][:], 1, t, t)
 
         pair_words = pairs[:].rearrange("p u j e -> p u (j e)").bitcast(U32).rearrange("p u j -> p j u")
 
@@ -214,8 +249,9 @@ def tile_list_raman_phase_traces_kernel(tc, tab_words, tab_scales, tab2_words, t
             nc.scalar.copy(out=dst.bitcast(U32).rearrange("p (j u) -> p j u", u=2),
                            in_=pair_words[:, first:first + width, :])
 
-        def add_late(first, width, after=None):
-            hb = tile("h_late%d" % first, [P, 4 * width], BF16, after)
+        def add_late(first, width, hb=None):
+            if hb is None:
+                hb = tile("h_late%d" % first, [P, 4 * width], BF16)
             real, imag = (early_r, early_i) if first < HALF else (late_r, late_i)
             cols = slice(first % HALF, first % HALF + width)
             nc.vector.tensor_tensor(out=hb[:].rearrange("p (c i t) -> p c t i", i=2, t=4),
@@ -243,26 +279,22 @@ def tile_list_raman_phase_traces_kernel(tc, tab_words, tab_scales, tab2_words, t
             nc.sync.dma_start(out=out_rows[:, :, first:first + width], in_=res[:])
 
         weave(w5_and_h[:, 4 * N:], 0, TAIL)
-        h_woven = tile("h_woven", [P, 4 * (WOVEN - TAIL)], BF16, "tab_w1")
+        h_woven = tile("h_woven", [P, 4 * (WOVEN - TAIL)], BF16, "w5_raw")
         weave(h_woven[:], TAIL, WOVEN - TAIL)
         w5_codes, w5_scales = quantize("w5_and_h", w5_and_h[:], N + TAIL, "yr1_2")
         finish(w5_codes[:, N:], w5_scales[:, N:], 0, TAIL)
         codes, scales = quantize("h_woven", h_woven[:], WOVEN - TAIL)
         finish(codes[:], scales[:], TAIL, WOVEN - TAIL)
-        late = [add_late(WOVEN, TAIL, "yr1_3")]
-        quantised = []
+        late = [add_late(WOVEN, TAIL, tile("h_first", [P, 4 * TAIL], BF16, "yr1_3"))]
         for first in range(HALF, S, TAIL):
             late.append(add_late(first, TAIL))
-            quantised.append(quantize("h%d" % first, late[-2][:], TAIL))
-            if first < S - TAIL:
-                finish(quantised[-1][0][:], quantised[-1][1][:], first - TAIL, TAIL)
-        quantised.append(quantize("h_last", late[-1][:], TAIL))
-        last_banks = [next_bank() for i in range(3)]
-        for c in range(2):
-            codes, scales = quantised[c - 2]
-            for i in range(3):
-                mix(last_banks[i][:, TAIL * c:TAIL * (c + 1)], i, codes[:], scales[:])
-        for i, copy in enumerate((nc.vector.tensor_copy, nc.scalar.copy, nc.vector.tensor_copy)):
-            last = tile("last%d" % i, [P, 2 * TAIL], F32)
-            copy(out=last[:], in_=last_banks[i][:, 0:2 * TAIL])
-            nc.sync.dma_start(out=out_rows[:, i, S - 2 * TAIL:S], in_=last[:])
+            codes, scales = quantize("h%d" % first, late[-2][:], TAIL)
+            finish(codes[:], scales[:], first - TAIL, TAIL)
+        codes, scales = quantize("h_last", late[-1][:], TAIL)
+        last = tile("last", [P, 3, TAIL], F32)
+        for rows, copy in ((slice(0, 2), nc.vector.tensor_copy), (slice(2, 3), nc.scalar.copy)):
+            bank = next_bank()[:].rearrange("p (i j) -> p i j", j=TAIL)
+            for i in range(rows.start, rows.stop):
+                mix(bank[:, i, :], i, codes[:], scales[:])
+            copy(out=last[:, rows, :], in_=bank[:, rows, :])
+        nc.sync.dma_start(out=out_rows[:, :, S - TAIL:S], in_=last[:])

@@ -64,8 +64,8 @@ def tile_list_raman_phase_traces_kernel(tc, tab_words, tab_scales, tab2_words, t
             nc.sync.dma_start(out=dst.bitcast(I32)[0:P:4, :], in_=rows.bitcast(I32).rearrange("a z c -> z a c"))
 
         nc.sync.dma_start(offs_sb[:], offs)
-        nc.sync.dma_start(offs2_sb[:], offs2)
         load_scale_rows(tab_bytes[:], tab_scales)
+        nc.sync.dma_start(offs2_sb[:], offs2)
         for r in range(4):
             nc.sync.dma_start(out=tab2_bytes[:].bitcast(I32)[r:P:32, :], in_=tab2_scales[0, r:16:4, :].bitcast(I32))
         tab2_w = load_words("tab2_w", tab2_words[0], T)
@@ -144,7 +144,7 @@ def tile_list_raman_phase_traces_kernel(tc, tab_words, tab_scales, tab2_words, t
                               in_=w3_raw[:].bitcast(I32).rearrange("p (b t q) -> p t b q", t=4, q=4))
         for t in (2, 3):
             round_slot_gpsimd(w4_bf[:, H * t:H * (t + 1)], w4_raw, t)
-        v2 = [gather_words("v2_0", tab2_w, offs2_sb[:, 0:32], "tab2_bytes"),
+        v2 = [gather_words("v2_0", tab2_w, offs2_sb[:, 0:32]),
               gather_words("v2_1", tab2_w, offs2_sb[:, 32:64])]
         w4_codes, w4_scales = quantize("w4", w4_bf[:], H)
 
@@ -195,7 +195,7 @@ def tile_list_raman_phase_traces_kernel(tc, tab_words, tab_scales, tab2_words, t
             y_pass(w4_codes, w4_scales, n // 4, n % 4, n)
         for n in range(6):
             y_out(yi[n][:], n % 4, n)
-        v_first = gather_words("v_first", tab_w[0], offs_sb[:], "w4_bf")
+        v_first = gather_words("v_first", tab_w[0], offs_sb[:])
         v_second = [gather_words("v_second%d" % h, tab_w[1], offs_sb[:, 32 * h:32 * (h + 1)]) for h in range(2)]
         w2_codes = tile("w2_codes", [P, 2, 2 * H], U8)
         nc.gpsimd.tensor_copy(out=w2_codes[:].bitcast(I32).rearrange("p a (t b e) -> p a t b e", t=4, e=2),
@@ -233,11 +233,12 @@ def tile_list_raman_phase_traces_kernel(tc, tab_words, tab_scales, tab2_words, t
                                     in1=early_i[:, t, 0:WOVEN], op=ADD)
         for t in range(2, 4):
             x_times_y(late_i[:, t, :], w2_lhs, yi[4 + t][:], 1, t, 4 + t)
-        yr_late = [on_w1_raw1("yr1_%d" % t, t + 2, [P, HALF], F32) if t < 2 else tile("yr1_%d" % t, [P, HALF], F32)
-                   for t in range(4)]
+        w5_and_h_row = tile("w5_and_h", [P, 2 * N + HALF], F32)
+        w5_and_h = w5_and_h_row[:, 0:2 * (N + TAIL)].bitcast(BF16)
+        yr_late = [on_w1_raw1("yr1_0", 2, [P, HALF], F32), w5_and_h_row[:, 2 * N:],
+                   tile("yr1_2", [P, HALF], F32), tile("yr1_3", [P, HALF], F32)]
         for t in range(4):
             y_slot(yr_late[t][:], w3_codes, w3_scale, 1, t, 4 + t % 2)
-        w5_and_h = tile("w5_and_h", [P, 4 * (N + TAIL)], BF16)
         nc.scalar.copy(out=w5_and_h[:, 0:4 * N].rearrange("p (c i t) -> p c t i", i=4, t=4),
                        in_=w5_raw[:].rearrange("p t (c i) -> p c t i", i=4))
         for t in range(4):
@@ -279,9 +280,9 @@ def tile_list_raman_phase_traces_kernel(tc, tab_words, tab_scales, tab2_words, t
             nc.sync.dma_start(out=out_rows[:, :, first:first + width], in_=res[:])
 
         weave(w5_and_h[:, 4 * N:], 0, TAIL)
-        h_woven = tile("h_woven", [P, 4 * (WOVEN - TAIL)], BF16, "w5_raw")
+        h_woven = tile("h_woven", [P, 4 * (WOVEN - TAIL)], BF16, "yr1_2")
         weave(h_woven[:], TAIL, WOVEN - TAIL)
-        w5_codes, w5_scales = quantize("w5_and_h", w5_and_h[:], N + TAIL, "yr1_2")
+        w5_codes, w5_scales = quantize("w5_and_h", w5_and_h, N + TAIL)
         finish(w5_codes[:, N:], w5_scales[:, N:], 0, TAIL)
         codes, scales = quantize("h_woven", h_woven[:], WOVEN - TAIL)
         finish(codes[:], scales[:], TAIL, WOVEN - TAIL)

@@ -47,7 +47,7 @@ def tile_list_raman_phase_traces_kernel(tc, tab_words, tab_scales, tab2_words, t
         win_slots = tile("win_slots", [P, H], F32)
         ident = tile("ident", [P, P], F32)
         nc.gpsimd.memset(tab_bytes[:].bitcast(I32), 0)
-        for zeroed in (tab2_bytes, w_bytes, ident, win_slots, plane[1]):
+        for zeroed in (w_bytes, tab2_bytes, ident, win_slots, plane[1]):
             nc.vector.memset(zeroed[:].bitcast(I32), 0)
         make_identity(nc, ident[:], nomemset=True)
 
@@ -66,11 +66,11 @@ def tile_list_raman_phase_traces_kernel(tc, tab_words, tab_scales, tab2_words, t
         nc.sync.dma_start(offs_sb[:], offs)
         load_scale_rows(tab_bytes[:], tab_scales)
         nc.sync.dma_start(offs2_sb[:], offs2)
-        for r in range(4):
-            nc.sync.dma_start(out=tab2_bytes[:].bitcast(I32)[r:P:32, :], in_=tab2_scales[0, r:16:4, :].bitcast(I32))
-        tab2_w = load_words("tab2_w", tab2_words[0], T)
         nc.sync.dma_start(out=w_bytes[:, 0:H].bitcast(I32)[0:P:8, :], in_=w3_scales[0].bitcast(I32))
         load_scale_rows(w_bytes[:, H:2 * H], w2_scales)
+        tab2_w = load_words("tab2_w", tab2_words[0], T)
+        for r in range(4):
+            nc.sync.dma_start(out=tab2_bytes[:].bitcast(I32)[r:P:32, :], in_=tab2_scales[0, r:16:4, :].bitcast(I32))
         nc.sync.dma_start(out=win_row[:], in_=win.rearrange("(o r) -> o r", o=1))
         w3_raw = load_words("w3_raw", w3_words[0], H)
         w4_raw = load_rows(tile("w4_raw", [P, 4, H], F32), w4)
@@ -113,8 +113,6 @@ def tile_list_raman_phase_traces_kernel(tc, tab_words, tab_scales, tab2_words, t
         picked = tile("picked", [P, S], U8)
         nc.vector.tensor_copy(picked[:], tab_bytes[:].indirect(offs_sb[:]))
         nc.vector.tensor_copy(out=plane[0][:, 2 * H:].bitcast(I32), in_=picked[:].bitcast(I32))
-        v2_scale = tile("v2_scale", [P, S], U8)
-        nc.vector.tensor_copy(v2_scale[:], tab2_bytes[:].indirect(offs2_sb[:]))
         for cols in (slice(H, 2 * H), slice(0, H)):
             nc.gpsimd.tensor_copy(out=plane[0][:, cols].bitcast(I32).rearrange("p (t b) -> p t b", t=4),
                                   in_=w_bytes[:, cols].bitcast(I32).rearrange("p (b t) -> p t b", t=4))
@@ -144,14 +142,17 @@ def tile_list_raman_phase_traces_kernel(tc, tab_words, tab_scales, tab2_words, t
                               in_=w3_raw[:].bitcast(I32).rearrange("p (b t q) -> p t b q", t=4, q=4))
         for t in (2, 3):
             round_slot_gpsimd(w4_bf[:, H * t:H * (t + 1)], w4_raw, t)
-        v2 = [gather_words("v2_0", tab2_w, offs2_sb[:, 0:32]),
-              gather_words("v2_1", tab2_w, offs2_sb[:, 32:64])]
+        v2_words = gather_words("v2_words", tab2_w, offs2_sb[:])
+        v2 = [v2_words[:, HALF * h:HALF * (h + 1)] for h in range(2)]
+        v2_scale = [tile("v2_scale%d" % h, [P, HALF], U8) for h in range(2)]
+        for h in range(2):
+            nc.vector.tensor_copy(v2_scale[h][:], tab2_bytes[:].indirect(offs2_sb[:, 32 * h:32 * (h + 1)]))
         w4_codes, w4_scales = quantize("w4", w4_bf[:], H)
 
         def y_pass(codes, scales, h, t, b):
             nc.tensor.matmul_mx(out=banks[b][:], lhsT=codes[:, P * t:P * (t + 1)].bitcast(FP8X4),
                                 lhsT_scale=scales[:, P * t:P * (t + 1)], rhs=v2[h][:].bitcast(FP8X4),
-                                rhs_scale=v2_scale[:, HALF * h:HALF * (h + 1)], start=True, stop=True)
+                                rhs_scale=v2_scale[h][:], start=True, stop=True)
 
         def y_out(y, t, b):
             nc.scalar.activation(out=y, in_=banks[b][:], func=COPY, scale=win_col[:, t:t + 1])
@@ -181,8 +182,8 @@ def tile_list_raman_phase_traces_kernel(tc, tab_words, tab_scales, tab2_words, t
                     w2_scale[a][:, P * t:P * (t + 1)])
 
         def w1_lhs(a, t):
-            codes, scales = w1_q[a * (1 + t // 2)]
-            cols = slice(P * (t % (4 - 2 * a)), P * (t % (4 - 2 * a) + 1))
+            codes, scales = w1_q[a][t // 2]
+            cols = slice(P * (t % 2), P * (t % 2 + 1))
             return codes[:, cols].bitcast(FP8X4), scales[:, cols]
 
         late_i_row = tile("late_i", [P, 5 * HALF], F32)
@@ -207,21 +208,20 @@ def tile_list_raman_phase_traces_kernel(tc, tab_words, tab_scales, tab2_words, t
         late_r = tile("late_r", [P, 4, HALF], F32)
         for t in range(4):
             x_times_y(early_i[:, t, :], w2_lhs, yi[t][:], 0, t, t)
-        w1_bf = [late_i_row[:, 0:2 * HALF].bitcast(BF16), tile("w1_bf1", [P, 2 * H], BF16)[:],
-                 late_i_row[:, 0:HALF].bitcast(BF16)]
-        round_slots(w1_bf[0][:, 0:2 * H], w1_raw[0], slice(0, 2))
+        halves = [late_i_row[:, HALF * (1 - u):HALF * (1 - u + 1)].bitcast(BF16) for u in range(2)]
+        round_slots(halves[0], w1_raw[0], slice(0, 2))
         for t in (2, 3):
-            round_slot_gpsimd(w1_bf[0][:, H * t:H * (t + 1)], w1_raw[0], t)
-        w1_q = [quantize("w1_0", w1_bf[0], H)]
+            round_slot_gpsimd(halves[1][:, H * (t - 2):H * (t - 1)], w1_raw[0], t)
+        w1_q = [{u: quantize("w1_0%d" % u, halves[u], H // 2) for u in (0, 1)}]
         for t in range(4):
             x_pass(w1_lhs, 0, 0, t, t)
         for t in range(2):
             x_times_y(late_i[:, t, :], w2_lhs, yi[4 + t][:], 1, t, 4 + t)
-        round_slots(w1_bf[1], w1_raw[1], slice(0, 2))
-        round_slot_gpsimd(w1_bf[2][:, H:2 * H], w1_raw[1], 3)
-        round_slots(w1_bf[2][:, 0:H], w1_raw[1], slice(2, 3))
-        for u in range(2):
-            w1_q.append(quantize("w1_1%d" % u, w1_bf[1 + u], H // 2))
+        halves = [tile("w1_bf1", [P, 2 * H], BF16)[:], late_i_row[:, 0:HALF].bitcast(BF16)]
+        round_slots(halves[0], w1_raw[1], slice(0, 2))
+        round_slot_gpsimd(halves[1][:, H:2 * H], w1_raw[1], 3)
+        round_slots(halves[1][:, 0:H], w1_raw[1], slice(2, 3))
+        w1_q.append({u: quantize("w1_1%d" % u, halves[u], H // 2) for u in range(2)})
         for n in range(6, 8):
             yi.append(on_w1_raw1("yi%d" % n, n - 6, [P, HALF], F32))
             y_out(yi[n][:], n % 4, n)
@@ -286,7 +286,7 @@ def tile_list_raman_phase_traces_kernel(tc, tab_words, tab_scales, tab2_words, t
         finish(w5_codes[:, N:], w5_scales[:, N:], 0, TAIL)
         codes, scales = quantize("h_woven", h_woven[:], WOVEN - TAIL)
         finish(codes[:], scales[:], TAIL, WOVEN - TAIL)
-        late = [add_late(WOVEN, TAIL, tile("h_first", [P, 4 * TAIL], BF16, "yr1_3"))]
+        late = [add_late(WOVEN, TAIL, tile("h_first", [P, 4 * TAIL], BF16, "pairs"))]
         for first in range(HALF, S, TAIL):
             late.append(add_late(first, TAIL))
             codes, scales = quantize("h%d" % first, late[-2][:], TAIL)

@@ -21,7 +21,7 @@ COPY = mybir.ActivationFunctionType.Copy
 P = 128
 HALF = 512
 TAIL = 128
-WOVEN = 384
+QUARTER = 256
 
 
 def tile_list_raman_phase_traces_kernel(tc, tab_words, tab_scales, tab2_words, tab2_scales, offs, offs2,
@@ -79,7 +79,7 @@ def tile_list_raman_phase_traces_kernel(tc, tab_words, tab_scales, tab2_words, t
         taken = []
 
         def next_bank():
-            taken.append(banks[(4, 5, 6, 7, 0, 1, 2, 3)[len(taken) % 8]])
+            taken.append(banks[(6, 7, 4, 5, 0, 1, 2, 3)[len(taken) % 8]])
             return taken[-1]
 
         win_ps = banks[0]
@@ -186,9 +186,13 @@ def tile_list_raman_phase_traces_kernel(tc, tab_words, tab_scales, tab2_words, t
             cols = slice(P * (t % 2), P * (t % 2 + 1))
             return codes[:, cols].bitcast(FP8X4), scales[:, cols]
 
-        late_i_row = tile("late_i", [P, 5 * HALF], F32)
-        late_i = late_i_row[:, HALF:].rearrange("p (t j) -> p t j", t=4)
-        yr_early = [late_i[:, 2 + t, :] if t < 2 else tile("yr0_%d" % t, [P, HALF], F32)[:] for t in range(4)]
+        wide_row = tile("late_i", [P, 2 * (N + QUARTER) + 6 * HALF], F32)
+        w5_and_h = wide_row[:, 0:2 * (N + QUARTER)].bitcast(BF16)
+        late_i_row = wide_row[:, 2 * (N + QUARTER) - HALF:]
+        late_i = late_i_row[:, HALF:5 * HALF].rearrange("p (t j) -> p t j", t=4)
+        yr_first = late_i_row[:, 3 * HALF:].rearrange("p (t j) -> p t j", t=4)
+        yr_early = [yr_first[:, t, :] for t in range(4)]
+        bank_slots = ((slice(0, 2), slice(2, 4)), (slice(0, 4, 2), slice(1, 4, 2)))
         for t in range(4):
             y_slot(yr_early[t], w3_codes, w3_scale, 0, t, 4 + t)
         yi = [tile("yi%d" % n, [P, HALF], F32) for n in range(6)]
@@ -204,60 +208,69 @@ def tile_list_raman_phase_traces_kernel(tc, tab_words, tab_scales, tab2_words, t
         v = [[v_first[:, HALF * h:HALF * (h + 1)], v_second[h][:]] for h in range(2)]
 
         early_i = tile("early_i", [P, 4, HALF], F32)
-        early_r = tile("early_r", [P, 4, HALF], F32)
+        early_r = [tile("early_r%d" % q, [P, 4, QUARTER], F32) for q in range(2)]
         late_r = tile("late_r", [P, 4, HALF], F32)
         for t in range(4):
             x_times_y(early_i[:, t, :], w2_lhs, yi[t][:], 0, t, t)
-        halves = [late_i_row[:, HALF * (1 - u):HALF * (1 - u + 1)].bitcast(BF16) for u in range(2)]
+        halves = [late_i_row[:, HALF:2 * HALF].bitcast(BF16), w5_and_h[:, 0:2 * H]]
         round_slots(halves[0], w1_raw[0], slice(0, 2))
         for t in (2, 3):
             round_slot_gpsimd(halves[1][:, H * (t - 2):H * (t - 1)], w1_raw[0], t)
         w1_q = [{u: quantize("w1_0%d" % u, halves[u], H // 2) for u in (0, 1)}]
-        for t in range(4):
-            x_pass(w1_lhs, 0, 0, t, t)
+
+        def xr_quarter(a, q, u):
+            for n, t in enumerate(range(4)[bank_slots[q][u]]):
+                codes, scales = w1_lhs(a, t)
+                cols = slice(QUARTER * q, QUARTER * (q + 1))
+                nc.tensor.matmul_mx(out=banks[2 * q + u][:, QUARTER * n:QUARTER * (n + 1)], lhsT=codes,
+                                    lhsT_scale=scales, rhs=v[0][a][:, cols].bitcast(FP8X4),
+                                    rhs_scale=v_scale[a][:, cols], start=(a == 0 and n == 0),
+                                    stop=(a == 1 and n == 1))
+
+        for q in range(2):
+            for u in range(2):
+                xr_quarter(0, q, u)
         for t in range(2):
             x_times_y(late_i[:, t, :], w2_lhs, yi[4 + t][:], 1, t, 4 + t)
-        halves = [tile("w1_bf1", [P, 2 * H], BF16)[:], late_i_row[:, 0:HALF].bitcast(BF16)]
+        halves = [tile("w1_bf1", [P, 2 * H], BF16)[:], w5_and_h[:, 0:2 * H]]
         round_slots(halves[0], w1_raw[1], slice(0, 2))
         round_slot_gpsimd(halves[1][:, H:2 * H], w1_raw[1], 3)
         round_slots(halves[1][:, 0:H], w1_raw[1], slice(2, 3))
         w1_q.append({u: quantize("w1_1%d" % u, halves[u], H // 2) for u in range(2)})
+        nc.gpsimd.tensor_scalar(out=w5_and_h[:, 0:8 * P].rearrange("p (n t) -> p n t", t=4),
+                                in0=w5_raw[:, :, 0:2 * P].rearrange("p t n -> p n t"),
+                                scalar1=1.0, scalar2=0.0, op0=MULT, op1=ADD)
         for n in range(6, 8):
             yi.append(on_w1_raw1("yi%d" % n, n - 6, [P, HALF], F32))
             y_out(yi[n][:], n % 4, n)
-        pairs = tile("pairs", [P, 2, WOVEN, 2], BF16)
-        for t in range(4):
-            x_pass(w1_lhs, 1, 0, t, t)
-            times_y(early_r[:, t, :], yr_early[t], t)
-            nc.gpsimd.tensor_tensor(out=pairs[:, t // 2, :, t % 2], in0=early_r[:, t, 0:WOVEN],
-                                    in1=early_i[:, t, 0:WOVEN], op=ADD)
+
+        def add_pairs(engine, dst, real, imag, run):
+            engine.tensor_tensor(out=dst.rearrange("p (c i t) -> p c t i", i=run, t=4),
+                                 in0=real.rearrange("p t (c i) -> p c t i", i=run),
+                                 in1=imag.rearrange("p t (c i) -> p c t i", i=run), op=ADD)
+
+        for q in range(2):
+            cols = slice(QUARTER * q, QUARTER * (q + 1))
+            for u in range(2):
+                xr_quarter(1, q, u)
+                nc.vector.tensor_tensor(out=early_r[q][:, bank_slots[q][u], :], in0=yr_first[:, bank_slots[q][u], cols],
+                                        in1=banks[2 * q + u][:].rearrange("p (t j) -> p t j", t=2), op=MULT)
+        add_pairs(nc.gpsimd, w5_and_h[:, 4 * N:], early_r[0][:], early_i[:, :, 0:QUARTER], 4)
         for t in range(2, 4):
             x_times_y(late_i[:, t, :], w2_lhs, yi[4 + t][:], 1, t, 4 + t)
-        w5_and_h_row = tile("w5_and_h", [P, 2 * N + HALF], F32)
-        w5_and_h = w5_and_h_row[:, 0:2 * (N + TAIL)].bitcast(BF16)
-        yr_late = [on_w1_raw1("yr1_0", 2, [P, HALF], F32), w5_and_h_row[:, 2 * N:],
+        yr_late = [on_w1_raw1("yr1_0", 2, [P, HALF], F32), tile("yr1_1", [P, HALF], F32),
                    tile("yr1_2", [P, HALF], F32), tile("yr1_3", [P, HALF], F32)]
         for t in range(4):
             y_slot(yr_late[t][:], w3_codes, w3_scale, 1, t, 4 + t % 2)
-        nc.scalar.copy(out=w5_and_h[:, 0:4 * N].rearrange("p (c i t) -> p c t i", i=4, t=4),
-                       in_=w5_raw[:].rearrange("p t (c i) -> p c t i", i=4))
-        for t in range(4):
-            x_times_y(late_r[:, t, :], w1_lhs, yr_late[t][:], 1, t, t)
 
-        pair_words = pairs[:].rearrange("p u j e -> p u (j e)").bitcast(U32).rearrange("p u j -> p j u")
-
-        def weave(dst, first, width):
-            nc.scalar.copy(out=dst.bitcast(U32).rearrange("p (j u) -> p j u", u=2),
-                           in_=pair_words[:, first:first + width, :])
-
-        def add_late(first, width, hb=None):
-            if hb is None:
-                hb = tile("h_late%d" % first, [P, 4 * width], BF16)
-            real, imag = (early_r, early_i) if first < HALF else (late_r, late_i)
-            cols = slice(first % HALF, first % HALF + width)
-            nc.vector.tensor_tensor(out=hb[:].rearrange("p (c i t) -> p c t i", i=2, t=4),
-                                    in0=real[:, :, cols].rearrange("p t (c i) -> p c t i", i=2),
-                                    in1=imag[:, :, cols].rearrange("p t (c i) -> p c t i", i=2), op=ADD)
+        def add_late(first, width):
+            hb = tile("h_late%d" % first, [P, 4 * width], BF16)
+            if first < HALF:
+                real, imag = early_r[1][:, :, first - QUARTER:], early_i[:, :, first:]
+            else:
+                cols = slice(first - HALF, first - HALF + width)
+                real, imag = late_r[:, :, cols], late_i[:, :, cols]
+            add_pairs(nc.vector, hb[:], real, imag, 2)
             return hb
 
         out_rows = out.rearrange("(i p) j -> p i j", p=P)
@@ -279,14 +292,23 @@ def tile_list_raman_phase_traces_kernel(tc, tab_words, tab_scales, tab2_words, t
                                in_=bank[:, 0:rows * width].rearrange("p (i j) -> p i j", i=rows))
             nc.sync.dma_start(out=out_rows[:, :, first:first + width], in_=res[:])
 
-        weave(w5_and_h[:, 4 * N:], 0, TAIL)
-        h_woven = tile("h_woven", [P, 4 * (WOVEN - TAIL)], BF16, "yr1_2")
-        weave(h_woven[:], TAIL, WOVEN - TAIL)
-        w5_codes, w5_scales = quantize("w5_and_h", w5_and_h, N + TAIL)
-        finish(w5_codes[:, N:], w5_scales[:, N:], 0, TAIL)
-        codes, scales = quantize("h_woven", h_woven[:], WOVEN - TAIL)
-        finish(codes[:], scales[:], TAIL, WOVEN - TAIL)
-        late = [add_late(WOVEN, TAIL, tile("h_first", [P, 4 * TAIL], BF16, "pairs"))]
+        nc.scalar.copy(out=w5_and_h[:, 8 * P:4 * N].rearrange("p (c i t) -> p c t i", i=4, t=4),
+                       in_=w5_raw[:, :, 2 * P:].rearrange("p t (c i) -> p c t i", i=4))
+        x_times_y(late_r[:, 0, :], w1_lhs, yr_late[0][:], 1, 0, 0)
+        w5_codes = tile("w5_codes", [P, N + QUARTER], U32, "w2_codes")
+        w5_scales = tile("w5_scales", [P, N + QUARTER], U8)
+        for first, width in ((0, N + TAIL), (N + TAIL, TAIL)):
+            nc.vector.quantize_mx(out=w5_codes[:, first:first + width].bitcast(FP8X4),
+                                  scales=w5_scales[:, first:first + width],
+                                  in_=w5_and_h[:, 4 * first:4 * (first + width)])
+        third = w5_and_h[:, 4 * (N + TAIL):]
+        add_pairs(nc.gpsimd, third, early_r[1][:, :, 0:TAIL], early_i[:, :, QUARTER:QUARTER + TAIL], 4)
+        finish(w5_codes[:, N:], w5_scales[:, N:], 0, QUARTER)
+        for t in range(1, 4):
+            x_times_y(late_r[:, t, :], w1_lhs, yr_late[t][:], 1, t, t)
+        codes, scales = quantize("h_third", third, TAIL, "v_second1")
+        finish(codes[:], scales[:], QUARTER, TAIL)
+        late = [add_late(HALF - TAIL, TAIL)]
         for first in range(HALF, S, TAIL):
             late.append(add_late(first, TAIL))
             codes, scales = quantize("h%d" % first, late[-2][:], TAIL)

@@ -48,7 +48,9 @@ def tile_list_raman_phase_traces_kernel(tc, tab_words, tab_scales, tab2_words, t
         ident = tile("ident", [P, P], F32)
         nc.gpsimd.memset(tab_bytes[:].bitcast(I32), 0)
         for zeroed in (w_bytes, tab2_bytes, ident, win_slots, plane[1]):
-            nc.vector.memset(zeroed[:].bitcast(I32), 0)
+            words = zeroed[:].bitcast(I32)
+            nc.vector.memset(words[:, 0:words.shape[1] - 1], 0)
+            nc.vector.memset(words[:, words.shape[1] - 1:], 0)
         make_identity(nc, ident[:], nomemset=True)
 
         def load_words(name, words, width):
@@ -79,7 +81,7 @@ def tile_list_raman_phase_traces_kernel(tc, tab_words, tab_scales, tab2_words, t
         taken = []
 
         def next_bank():
-            taken.append(banks[(6, 7, 4, 5, 0, 1, 2, 3)[len(taken) % 8]])
+            taken.append(banks[(6, 4, 5, 0, 1, 2, 3, 7)[len(taken) % 8]])
             return taken[-1]
 
         win_ps = banks[0]
@@ -265,12 +267,8 @@ def tile_list_raman_phase_traces_kernel(tc, tab_words, tab_scales, tab2_words, t
 
         def add_late(first, width):
             hb = tile("h_late%d" % first, [P, 4 * width], BF16)
-            if first < HALF:
-                real, imag = early_r[1][:, :, first - QUARTER:], early_i[:, :, first:]
-            else:
-                cols = slice(first - HALF, first - HALF + width)
-                real, imag = late_r[:, :, cols], late_i[:, :, cols]
-            add_pairs(nc.vector, hb[:], real, imag, 2)
+            cols = slice(first - HALF, first - HALF + width)
+            add_pairs(nc.vector, hb[:], late_r[:, :, cols], late_i[:, :, cols], 2)
             return hb
 
         out_rows = out.rearrange("(i p) j -> p i j", p=P)
@@ -306,11 +304,27 @@ def tile_list_raman_phase_traces_kernel(tc, tab_words, tab_scales, tab2_words, t
         finish(w5_codes[:, N:], w5_scales[:, N:], 0, QUARTER)
         for t in range(1, 4):
             x_times_y(late_r[:, t, :], w1_lhs, yr_late[t][:], 1, t, t)
+        turning = banks[7]
+        for t in range(4):
+            for n, src in enumerate((early_i[:, t, HALF - TAIL:], early_r[1][:, t, TAIL:])):
+                nc.tensor.matmul(out=turning[:, P * t:P * (t + 1)], lhsT=src, rhs=ident[:], is_transpose=True,
+                                 start=(n == 0), stop=(n == 1))
+        rounded = tile("rounded", [P, 4 * P], BF16)
+        nc.scalar.copy(out=rounded[:].rearrange("j (u p e) -> j u p e", u=2, e=2),
+                       in_=turning[:].rearrange("j (u e p) -> j u p e", u=2, e=2))
+        for u in range(2):
+            nc.tensor.transpose(turning[:, P * u:P * (u + 1)], rounded[:].bitcast(F32)[:, P * u:P * (u + 1)], ident[:])
         codes, scales = quantize("h_third", third, TAIL, "v_second1")
         finish(codes[:], scales[:], QUARTER, TAIL)
-        late = [add_late(HALF - TAIL, TAIL)]
-        for first in range(HALF, S, TAIL):
+        h_turned = tile("h_turned", [P, 4 * TAIL], BF16)
+        nc.scalar.copy(out=h_turned[:].bitcast(F32).rearrange("p (j u) -> p j u", u=2),
+                       in_=turning[:, 0:2 * P].rearrange("p (u j) -> p j u", u=2))
+        late = [add_late(HALF, TAIL)]
+        for first in range(HALF + TAIL, S, TAIL):
             late.append(add_late(first, TAIL))
+            if first == HALF + TAIL:
+                codes, scales = quantize("h_turned", h_turned[:], TAIL)
+                finish(codes[:], scales[:], HALF - TAIL, TAIL)
             codes, scales = quantize("h%d" % first, late[-2][:], TAIL)
             finish(codes[:], scales[:], first - TAIL, TAIL)
         codes, scales = quantize("h_last", late[-1][:], TAIL)

@@ -138,12 +138,11 @@ def tile_list_raman_phase_traces_kernel(tc, tab_words, tab_scales, tab2_words, t
 
         win_col = tile("win_col", [P, 4], F32)
         nc.scalar.copy(out=win_col[:], in_=win_ps[:, 0:H:P])
-        round_slots(w4_bf[:, 0:2 * H], w4_raw, slice(0, 2))
+        round_slots(w4_bf[:, 0:3 * H], w4_raw, slice(0, 3))
         w3_codes = tile("w3_codes", [P, H], U32)
         nc.gpsimd.tensor_copy(out=w3_codes[:].bitcast(I32).rearrange("p (t b q) -> p t b q", t=4, q=4),
                               in_=w3_raw[:].bitcast(I32).rearrange("p (b t q) -> p t b q", t=4, q=4))
-        for t in (2, 3):
-            round_slot_gpsimd(w4_bf[:, H * t:H * (t + 1)], w4_raw, t)
+        round_slot_gpsimd(w4_bf[:, 3 * H:], w4_raw, 3)
         v2_words = gather_words("v2_words", tab2_w, offs2_sb[:])
         v2 = [v2_words[:, HALF * h:HALF * (h + 1)] for h in range(2)]
         v2_scale = [tile("v2_scale%d" % h, [P, HALF], U8) for h in range(2)]
@@ -239,8 +238,8 @@ def tile_list_raman_phase_traces_kernel(tc, tab_words, tab_scales, tab2_words, t
         round_slot_gpsimd(halves[1][:, H:2 * H], w1_raw[1], 3)
         round_slots(halves[1][:, 0:H], w1_raw[1], slice(2, 3))
         w1_q.append({u: quantize("w1_1%d" % u, halves[u], H // 2) for u in range(2)})
-        nc.gpsimd.tensor_scalar(out=w5_and_h[:, 0:8 * P].rearrange("p (n t) -> p n t", t=4),
-                                in0=w5_raw[:, :, 0:2 * P].rearrange("p t n -> p n t"),
+        nc.gpsimd.tensor_scalar(out=w5_and_h[:, 0:4 * P].rearrange("p (n t) -> p n t", t=4),
+                                in0=w5_raw[:, :, 0:P].rearrange("p t n -> p n t"),
                                 scalar1=1.0, scalar2=0.0, op0=MULT, op1=ADD)
         for n in range(6, 8):
             yi.append(on_w1_raw1("yi%d" % n, n - 6, [P, HALF], F32))
@@ -290,8 +289,8 @@ def tile_list_raman_phase_traces_kernel(tc, tab_words, tab_scales, tab2_words, t
                                in_=bank[:, 0:rows * width].rearrange("p (i j) -> p i j", i=rows))
             nc.sync.dma_start(out=out_rows[:, :, first:first + width], in_=res[:])
 
-        nc.scalar.copy(out=w5_and_h[:, 8 * P:4 * N].rearrange("p (c i t) -> p c t i", i=4, t=4),
-                       in_=w5_raw[:, :, 2 * P:].rearrange("p t (c i) -> p c t i", i=4))
+        nc.scalar.copy(out=w5_and_h[:, 4 * P:4 * N].rearrange("p (c i t) -> p c t i", i=4, t=4),
+                       in_=w5_raw[:, :, P:].rearrange("p t (c i) -> p c t i", i=4))
         x_times_y(late_r[:, 0, :], w1_lhs, yr_late[0][:], 1, 0, 0)
         w5_codes = tile("w5_codes", [P, N + QUARTER], U32, "w2_codes")
         w5_scales = tile("w5_scales", [P, N + QUARTER], U8)

@@ -22,6 +22,7 @@ P = 128
 HALF = 512
 TAIL = 128
 QUARTER = 256
+V2_ROW = 12
 
 
 def tile_list_raman_phase_traces_kernel(tc, tab_words, tab_scales, tab2_words, tab2_scales, offs, offs2,
@@ -72,7 +73,7 @@ def tile_list_raman_phase_traces_kernel(tc, tab_words, tab_scales, tab2_words, t
         load_scale_rows(w_bytes[:, H:2 * H], w2_scales)
         tab2_w = load_words("tab2_w", tab2_words[0], T)
         for r in range(4):
-            nc.sync.dma_start(out=tab2_bytes[:].bitcast(I32)[r:P:32, :], in_=tab2_scales[0, r:16:4, :].bitcast(I32))
+            nc.sync.dma_start(out=tab2_bytes[:].bitcast(I32)[V2_ROW + r:P:32, :], in_=tab2_scales[0, r:16:4, :].bitcast(I32))
         nc.sync.dma_start(out=win_row[:], in_=win.rearrange("(o r) -> o r", o=1))
         w3_raw = load_words("w3_raw", w3_words[0], H)
         w4_raw = load_rows(tile("w4_raw", [P, 4, H], F32), w4)
@@ -153,7 +154,7 @@ def tile_list_raman_phase_traces_kernel(tc, tab_words, tab_scales, tab2_words, t
         def y_pass(codes, scales, h, t, b):
             nc.tensor.matmul_mx(out=banks[b][:], lhsT=codes[:, P * t:P * (t + 1)].bitcast(FP8X4),
                                 lhsT_scale=scales[:, P * t:P * (t + 1)], rhs=v2[h][:].bitcast(FP8X4),
-                                rhs_scale=v2_scale[h][:], start=True, stop=True)
+                                rhs_scale=v2_scale[h][V2_ROW:, :], start=True, stop=True)
 
         def y_out(y, t, b):
             nc.scalar.activation(out=y, in_=banks[b][:], func=COPY, scale=win_col[:, t:t + 1])

from contextlib import ExitStack

import concourse.mybir as mybir
from concourse.masks import make_identity

K, K2, H, N, T, S = 1024, 512, 512, 384, 2048, 1024
FLOPS = 2 * S * (2 * K * H + 2 * K2 * H + H * N)

F32 = mybir.dt.float32
BF16 = mybir.dt.bfloat16
I32 = mybir.dt.int32
U32 = mybir.dt.uint32
U16 = mybir.dt.uint16
U8 = mybir.dt.uint8
FP8X4 = mybir.dt.float8_e4m3fn_x4
FP4X4 = mybir.dt.float4_e2m1fn_x4
MULT = mybir.AluOpType.mult
ADD = mybir.AluOpType.add
COPY = mybir.ActivationFunctionType.Copy

P = 128
HALF = 512
TAIL = 128
QUARTER = 256
V2_ROW = 12


def tile_list_raman_phase_traces_kernel(tc, tab_words, tab_scales, tab2_words, tab2_scales, offs, offs2,
                                                     w1, w2_words, w2_scales, w3_words, w3_scales, w4, win, w5, out):
    nc = tc.nc
    with ExitStack() as ctx:
        lists = ctx.enter_context(tc.tile_pool(name="lists", bufs=1))
        sb = ctx.enter_context(tc.tile_pool(name="sb", bufs=1))
        shared = ctx.enter_context(tc.tile_pool(name="shared", bufs=1))
        psum = ctx.enter_context(tc.psum_pool(name="psum", bufs=1))

        def tile(name, shape, dtype, after=None):
            return sb.tile(shape, dtype, name=name, tag=after or name, align_bytes=64)

        offs_sb = lists.tile([P, S // 16], U16, name="offs_sb")
        offs2_sb = lists.tile([P, S // 16], U16, name="offs2_sb")

        tab_bytes = tile("tab_bytes", [P, T], U8)
        tab2_bytes = tile("tab2_bytes", [P, T], U8)
        w_bytes = tile("w_bytes", [P, 2 * H], U8)
        plane = [tile("plane0", [P, 2 * H + S], U8), tile("plane1", [P, H + S], U8)]
        win_row = tile("win_row", [1, H], F32)
        win_slots = tile("win_slots", [P, H], F32)
        ident = tile("ident", [P, P], F32)
        nc.gpsimd.memset(tab_bytes[:].bitcast(I32), 0)
        for zeroed in (w_bytes, tab2_bytes, ident, win_slots, plane[1]):
            words = zeroed[:].bitcast(I32)
            nc.vector.memset(words[:, 0:words.shape[1] - 1], 0)
            nc.vector.memset(words[:, words.shape[1] - 1:], 0)
        make_identity(nc, ident[:], nomemset=True)

        def load_words(name, words, width):
            t = tile(name, [P, width], U32)
            nc.sync.dma_start(out=t[:].bitcast(I32), in_=words.rearrange("p t i -> p (t i)").bitcast(I32))
            return t

        def load_rows(t, rows):
            nc.sync.dma_start(out=t[:], in_=rows.rearrange("(p j) c -> p j c", j=4))
            return t

        def load_scale_rows(dst, rows):
            nc.sync.dma_start(out=dst.bitcast(I32)[0:P:4, :], in_=rows.bitcast(I32).rearrange("a z c -> z a c"))

        nc.sync.dma_start(offs_sb[:], offs)
        load_scale_rows(tab_bytes[:], tab_scales)
        nc.sync.dma_start(offs2_sb[:], offs2)
        nc.sync.dma_start(out=w_bytes[:, 0:H].bitcast(I32)[0:P:8, :], in_=w3_scales[0].bitcast(I32))
        load_scale_rows(w_bytes[:, H:2 * H], w2_scales)
        tab2_w = load_words("tab2_w", tab2_words[0], T)
        for r in range(4):
            nc.sync.dma_start(out=tab2_bytes[:].bitcast(I32)[V2_ROW + r:P:32, :], in_=tab2_scales[0, r:16:4, :].bitcast(I32))
        nc.sync.dma_start(out=win_row[:], in_=win.rearrange("(o r) -> o r", o=1))
        w3_raw = load_words("w3_raw", w3_words[0], H)
        w4_raw = load_rows(tile("w4_raw", [P, 4, H], F32), w4)

        banks = [psum.tile([P, HALF], F32, name="bank%d" % b) for b in range(8)]
        taken = []

        def next_bank():
            taken.append(banks[(6, 4, 5, 0, 1, 2, 3, 7)[len(taken) % 8]])
            return taken[-1]

        win_ps = banks[0]
        nc.gpsimd.tensor_copy(out=win_slots[0:1, :].rearrange("o (t b q) -> o t b q", t=4, q=4),
                              in_=win_row[:].rearrange("o (b t q) -> o t b q", t=4, q=4))
        for t in range(4):
            nc.tensor.transpose(win_ps[:, P * t:P * (t + 1)], win_slots[:, P * t:P * (t + 1)], ident[:])

        def round_slots(dst, raw, slots):
            nc.scalar.copy(out=dst.rearrange("p (t b q j) -> p t b j q", b=32, q=4, j=4),
                           in_=raw[:].rearrange("p j (b t q) -> p t b j q", t=4, q=4)[:, slots])

        def round_slot_gpsimd(dst, raw, t):
            nc.gpsimd.tensor_scalar(out=dst.rearrange("p (b q j) -> p b q j", q=4, j=4),
                                    in0=raw[:].rearrange("p j (b t q) -> p t b q j", t=4, q=4)[:, t],
                                    scalar1=1.0, scalar2=0.0, op0=MULT, op1=ADD)

        def quantize(name, src, width, after=None):
            codes = tile(name + "_codes", [P, width], U32, after)
            scales = tile(name + "_scales", [P, width], U8)
            nc.vector.quantize_mx(out=codes[:].bitcast(FP8X4), scales=scales[:], in_=src)
            return codes, scales

        def gather_words(name, window, offsets, after=None):
            t = tile(name, [P, 16 * offsets.shape[1]], U32, after)
            nc.vector.tensor_copy(t[:], window[:].indirect(offsets))
            return t

        w4_bf = tile("w4_bf", [P, 4 * H], BF16)

        picked = tile("picked", [P, S], U8)
        nc.vector.tensor_copy(picked[:], tab_bytes[:].indirect(offs_sb[:]))
        nc.vector.tensor_copy(out=plane[0][:, 2 * H:].bitcast(I32), in_=picked[:].bitcast(I32))
        for cols in (slice(H, 2 * H), slice(0, H)):
            nc.gpsimd.tensor_copy(out=plane[0][:, cols].bitcast(I32).rearrange("p (t b) -> p t b", t=4),
                                  in_=w_bytes[:, cols].bitcast(I32).rearrange("p (b t) -> p t b", t=4))
        for r in range(1, 4):
            nc.sync.dma_start(out=plane[0][:].bitcast(I32)[r:P:32, :], in_=plane[0][:].bitcast(I32)[8 * r:P:32, :])
        tab_w = [load_words("tab_w%d" % a, tab_words[a], T) for a in range(2)]
        for r in range(4):
            nc.sync.dma_start(out=plane[1][:].bitcast(I32)[r:P:32, :],
                              in_=plane[0][:, H:].bitcast(I32)[8 * r + 4:P:32, :])
        w2_raw = tile("w2_raw", [P, 2, 2 * H], U8)
        nc.sync.dma_start(out=w2_raw[:].bitcast(I32), in_=w2_words.rearrange("a p c -> p a c").bitcast(I32))
        w1_raw = [load_rows(tile("w1_raw0", [P, 4, H], F32), w1[0:512, :]),
                  load_rows(shared.tile([P, 4, H], F32, name="w1_raw1", offset=0, align_bytes=64), w1[512:1024, :])]
        w5_raw = tile("w5_raw", [P, 4, N], F32)
        w5_by_slot = w5.rearrange("(b t q) n -> t b q n", t=4, q=4)
        for t in range(4):
            nc.sync.dma_start(out=w5_raw[:, t, :], in_=w5_by_slot[t])
        w3_scale = plane[0][:, 0:H]
        w2_scale = [plane[0][:, H:2 * H], plane[1][:, 0:H]]
        v_scale = [plane[0][:, 2 * H:], plane[1][:, H:]]

        win_col = tile("win_col", [P, 4], F32)
        nc.scalar.copy(out=win_col[:], in_=win_ps[:, 0:H:P])
        round_slots(w4_bf[:, 0:3 * H], w4_raw, slice(0, 3))
        w3_codes = tile("w3_codes", [P, H], U32)
        nc.gpsimd.tensor_copy(out=w3_codes[:].bitcast(I32).rearrange("p (t b q) -> p t b q", t=4, q=4),
                              in_=w3_raw[:].bitcast(I32).rearrange("p (b t q) -> p t b q", t=4, q=4))
        round_slot_gpsimd(w4_bf[:, 3 * H:], w4_raw, 3)
        v2_words = gather_words("v2_words", tab2_w, offs2_sb[:])
        v2 = [v2_words[:, HALF * h:HALF * (h + 1)] for h in range(2)]
        v2_scale = [tile("v2_scale%d" % h, [P, HALF], U8) for h in range(2)]
        for h in range(2):
            nc.vector.tensor_copy(v2_scale[h][:], tab2_bytes[:].indirect(offs2_sb[:, 32 * h:32 * (h + 1)]))
        w4_codes, w4_scales = quantize("w4", w4_bf[:], H)

        def y_pass(codes, scales, h, t, b):
            nc.tensor.matmul_mx(out=banks[b][:], lhsT=codes[:, P * t:P * (t + 1)].bitcast(FP8X4),
                                lhsT_scale=scales[:, P * t:P * (t + 1)], rhs=v2[h][:].bitcast(FP8X4),
                                rhs_scale=v2_scale[h][V2_ROW:, :], start=True, stop=True)

        def y_out(y, t, b):
            nc.scalar.activation(out=y, in_=banks[b][:], func=COPY, scale=win_col[:, t:t + 1])

        def y_slot(y, codes, scales, h, t, b):
            y_pass(codes, scales, h, t, b)
            y_out(y, t, b)

        def on_w1_raw1(name, quarter, shape, dtype):
            return shared.tile(shape, dtype, name=name, offset=4 * HALF * quarter, align_bytes=64)

        def x_pass(lhs, a, h, t, b):
            codes, scales = lhs(a, t)
            nc.tensor.matmul_mx(out=banks[b][:], lhsT=codes, lhsT_scale=scales, rhs=v[h][a].bitcast(FP8X4),
                                rhs_scale=v_scale[a][:, HALF * h:HALF * (h + 1)], start=(a == 0), stop=(a == 1))

        def times_y(prod, y, b):
            nc.vector.tensor_tensor(out=prod, in0=y, in1=banks[b][:], op=MULT)

        def x_times_y(prod, lhs, y, h, t, b):
            for a in range(2):
                x_pass(lhs, a, h, t, b)
            times_y(prod, y, b)

        def w2_lhs(a, t):
            return (w2_codes[:, a, 2 * P * t:2 * P * (t + 1)].bitcast(FP4X4),
                    w2_scale[a][:, P * t:P * (t + 1)])

        def w1_lhs(a, t):
            codes, scales = w1_q[a][t // 2]
            cols = slice(P * (t % 2), P * (t % 2 + 1))
            return codes[:, cols].bitcast(FP8X4), scales[:, cols]

        wide_row = tile("late_i", [P, 2 * (N + QUARTER) + 6 * HALF], F32)
        w5_and_h = wide_row[:, 0:2 * (N + QUARTER)].bitcast(BF16)
        late_i_row = wide_row[:, 2 * (N + QUARTER) - HALF:]
        late_i = late_i_row[:, HALF:5 * HALF].rearrange("p (t j) -> p t j", t=4)
        yr_first = late_i_row[:, 3 * HALF:].rearrange("p (t j) -> p t j", t=4)
        yr_early = [yr_first[:, t, :] for t in range(4)]
        bank_slots = ((slice(0, 2), slice(2, 4)), (slice(0, 4, 2), slice(1, 4, 2)))
        for t in range(4):
            y_slot(yr_early[t], w3_codes, w3_scale, 0, t, 4 + t)
        yi = [tile("yi%d" % n, [P, HALF], F32) for n in range(6)]
        for n in range(8):
            y_pass(w4_codes, w4_scales, n // 4, n % 4, n)
        for n in range(6):
            y_out(yi[n][:], n % 4, n)
        v_first = gather_words("v_first", tab_w[0], offs_sb[:])
        v_second = [gather_words("v_second%d" % h, tab_w[1], offs_sb[:, 32 * h:32 * (h + 1)]) for h in range(2)]
        w2_codes = tile("w2_codes", [P, 2, 2 * H], U8)
        nc.gpsimd.tensor_copy(out=w2_codes[:].bitcast(I32).rearrange("p a (t b e) -> p a t b e", t=4, e=2),
                              in_=w2_raw[:].bitcast(I32).rearrange("p a (b t e) -> p a t b e", t=4, e=2))
        v = [[v_first[:, HALF * h:HALF * (h + 1)], v_second[h][:]] for h in range(2)]

        early_i = tile("early_i", [P, 4, HALF], F32)
        early_r = [tile("early_r%d" % q, [P, 4, QUARTER], F32) for q in range(2)]
        late_r = tile("late_r", [P, 4, HALF], F32)
        for t in range(4):
            x_times_y(early_i[:, t, :], w2_lhs, yi[t][:], 0, t, t)
        halves = [late_i_row[:, HALF:2 * HALF].bitcast(BF16), w5_and_h[:, 0:2 * H]]
        round_slots(halves[0], w1_raw[0], slice(0, 2))
        for t in (2, 3):
            round_slot_gpsimd(halves[1][:, H * (t - 2):H * (t - 1)], w1_raw[0], t)
        w1_q = [{u: quantize("w1_0%d" % u, halves[u], H // 2) for u in (0, 1)}]

        def xr_quarter(a, q, u):
            for n, t in enumerate(range(4)[bank_slots[q][u]]):
                codes, scales = w1_lhs(a, t)
                cols = slice(QUARTER * q, QUARTER * (q + 1))
                nc.tensor.matmul_mx(out=banks[2 * q + u][:, QUARTER * n:QUARTER * (n + 1)], lhsT=codes,
                                    lhsT_scale=scales, rhs=v[0][a][:, cols].bitcast(FP8X4),
                                    rhs_scale=v_scale[a][:, cols], start=(a == 0 and n == 0),
                                    stop=(a == 1 and n == 1))

        for q in range(2):
            for u in range(2):
                xr_quarter(0, q, u)
        for t in range(2):
            x_times_y(late_i[:, t, :], w2_lhs, yi[4 + t][:], 1, t, 4 + t)
        halves = [tile("w1_bf1", [P, 2 * H], BF16)[:], w5_and_h[:, 0:2 * H]]
        round_slots(halves[0], w1_raw[1], slice(0, 2))
        round_slot_gpsimd(halves[1][:, H:2 * H], w1_raw[1], 3)
        round_slots(halves[1][:, 0:H], w1_raw[1], slice(2, 3))
        w1_q.append({u: quantize("w1_1%d" % u, halves[u], H // 2) for u in range(2)})
        nc.gpsimd.tensor_scalar(out=w5_and_h[:, 0:4 * P].rearrange("p (n t) -> p n t", t=4),
                                in0=w5_raw[:, :, 0:P].rearrange("p t n -> p n t"),
                                scalar1=1.0, scalar2=0.0, op0=MULT, op1=ADD)
        for n in range(6, 8):
            yi.append(on_w1_raw1("yi%d" % n, n - 6, [P, HALF], F32))
            y_out(yi[n][:], n % 4, n)

        def add_pairs(engine, dst, real, imag, run):
            engine.tensor_tensor(out=dst.rearrange("p (c i t) -> p c t i", i=run, t=4),
                                 in0=real.rearrange("p t (c i) -> p c t i", i=run),
                                 in1=imag.rearrange("p t (c i) -> p c t i", i=run), op=ADD)

        for q in range(2):
            cols = slice(QUARTER * q, QUARTER * (q + 1))
            for u in range(2):
                xr_quarter(1, q, u)
                nc.vector.tensor_tensor(out=early_r[q][:, bank_slots[q][u], :], in0=yr_first[:, bank_slots[q][u], cols],
                                        in1=banks[2 * q + u][:].rearrange("p (t j) -> p t j", t=2), op=MULT)
        add_pairs(nc.gpsimd, w5_and_h[:, 4 * N:], early_r[0][:], early_i[:, :, 0:QUARTER], 4)
        for t in range(2, 4):
            x_times_y(late_i[:, t, :], w2_lhs, yi[4 + t][:], 1, t, 4 + t)
        yr_late = [on_w1_raw1("yr1_0", 2, [P, HALF], F32), tile("yr1_1", [P, HALF], F32),
                   tile("yr1_2", [P, HALF], F32), tile("yr1_3", [P, HALF], F32)]
        for t in range(4):
            y_slot(yr_late[t][:], w3_codes, w3_scale, 1, t, 4 + t % 2)

        def add_late(first, width):
            hb = tile("h_late%d" % first, [P, 4 * width], BF16)
            cols = slice(first - HALF, first - HALF + width)
            add_pairs(nc.vector, hb[:], late_r[:, :, cols], late_i[:, :, cols], 2)
            return hb

        out_rows = out.rearrange("(i p) j -> p i j", p=P)

        def mix(dst, i, codes, scales):
            nc.tensor.matmul_mx(out=dst, lhsT=w5_codes[:, P * i:P * (i + 1)].bitcast(FP8X4),
                                lhsT_scale=w5_scales[:, P * i:P * (i + 1)], rhs=codes.bitcast(FP8X4),
                                rhs_scale=scales, start=True, stop=True)

        def finish(codes, scales, first, width):
            res = tile("res%d" % first, [P, 3, width], F32)
            per_bank = HALF // width
            for i0 in range(0, 3, per_bank):
                rows = min(per_bank, 3 - i0)
                bank = next_bank()
                for i in range(rows):
                    mix(bank[:, width * i:width * (i + 1)], i0 + i, codes, scales)
                nc.scalar.copy(out=res[:, i0:i0 + rows, :],
                               in_=bank[:, 0:rows * width].rearrange("p (i j) -> p i j", i=rows))
            nc.sync.dma_start(out=out_rows[:, :, first:first + width], in_=res[:])

        nc.scalar.copy(out=w5_and_h[:, 4 * P:4 * N].rearrange("p (c i t) -> p c t i", i=4, t=4),
                       in_=w5_raw[:, :, P:].rearrange("p t (c i) -> p c t i", i=4))
        x_times_y(late_r[:, 0, :], w1_lhs, yr_late[0][:], 1, 0, 0)
        w5_codes = tile("w5_codes", [P, N + QUARTER], U32, "w2_codes")
        w5_scales = tile("w5_scales", [P, N + QUARTER], U8)
        for first, width in ((0, N + TAIL), (N + TAIL, TAIL)):
            nc.vector.quantize_mx(out=w5_codes[:, first:first + width].bitcast(FP8X4),
                                  scales=w5_scales[:, first:first + width],
                                  in_=w5_and_h[:, 4 * first:4 * (first + width)])
        third = w5_and_h[:, 4 * (N + TAIL):]
        add_pairs(nc.gpsimd, third, early_r[1][:, :, 0:TAIL], early_i[:, :, QUARTER:QUARTER + TAIL], 4)
        finish(w5_codes[:, N:], w5_scales[:, N:], 0, QUARTER)
        for t in range(1, 4):
            x_times_y(late_r[:, t, :], w1_lhs, yr_late[t][:], 1, t, t)
        turning = banks[7]
        for t in range(4):
            for n, src in enumerate((early_i[:, t, HALF - TAIL:], early_r[1][:, t, TAIL:])):
                nc.tensor.matmul(out=turning[:, P * t:P * (t + 1)], lhsT=src, rhs=ident[:], is_transpose=True,
                                 start=(n == 0), stop=(n == 1))
        rounded = tile("rounded", [P, 4 * P], BF16)
        nc.scalar.copy(out=rounded[:].rearrange("j (u p e) -> j u p e", u=2, e=2),
                       in_=turning[:].rearrange("j (u e p) -> j u p e", u=2, e=2))
        for u in range(2):
            nc.tensor.transpose(turning[:, P * u:P * (u + 1)], rounded[:].bitcast(F32)[:, P * u:P * (u + 1)], ident[:])
        codes, scales = quantize("h_third", third, TAIL, "v_second1")
        finish(codes[:], scales[:], QUARTER, TAIL)
        h_turned = tile("h_turned", [P, 4 * TAIL], BF16)
        nc.scalar.copy(out=h_turned[:].bitcast(F32).rearrange("p (j u) -> p j u", u=2),
                       in_=turning[:, 0:2 * P].rearrange("p (u j) -> p j u", u=2))
        late = [add_late(HALF, TAIL)]
        for first in range(HALF + TAIL, S, TAIL):
            late.append(add_late(first, TAIL))
            if first == HALF + TAIL:
                codes, scales = quantize("h_turned", h_turned[:], TAIL)
                finish(codes[:], scales[:], HALF - TAIL, TAIL)
            codes, scales = quantize("h%d" % first, late[-2][:], TAIL)
            finish(codes[:], scales[:], first - TAIL, TAIL)
        codes, scales = quantize("h_last", late[-1][:], TAIL)
        last = tile("last", [P, 3, TAIL], F32)
        for rows, copy in ((slice(0, 2), nc.vector.tensor_copy), (slice(2, 3), nc.scalar.copy)):
            bank = next_bank()[:].rearrange("p (i j) -> p i j", j=TAIL)
            for i in range(rows.start, rows.stop):
                mix(bank[:, i, :], i, codes[:], scales[:])
            copy(out=last[:, rows, :], in_=bank[:, rows, :])
        nc.sync.dma_start(out=out_rows[:, :, S - TAIL:S], in_=last[:])
